import numpy as np, ml_dtypes
CORES = [23,119,17,113]
N = 4
BF = ml_dtypes.bfloat16
def gentries(a):
    return np.ascontiguousarray(a.reshape(8, 16, -1).transpose(0, 2, 1)).reshape(8, -1)
def gtable(e):
    e = np.asarray(e); return np.ascontiguousarray(e.reshape(8, -1, 16).transpose(0, 2, 1)).reshape(128, -1).astype(np.int32)
W, UN, P, SH, MS = 4096, 256, 16, 5, (1, 2, 3)
def parts(rng):
    e = (0.5 + 2.5 * rng.random((N, 8, 16, 1))).astype(np.float32)
    sh = np.minimum(np.floor(256 * rng.random((N, 8, 16, W), dtype=np.float32) ** e), 255)
    return sh, rng.integers(0, W, (N, 8, UN, P))
def pack(sh, un):
    return {"shelf": np.ascontiguousarray(sh.reshape(N, 128, W)).astype(np.float32).astype(BF), "units": np.stack([gtable(a.reshape(8, -1)) for a in un])}
def setup_inputs(rng):
    sh, un = parts(rng)
    return pack(sh, un)
def setup_inputs_ties(rng):
    sh, un = parts(rng)
    sh = (rng.random((N, 8, 16, W)) < 0.03) * rng.choice(np.array([1, 7, 255]), (1, 8, 1, 1))
    sh[:, rng.integers(0, 8)] = 9
    return pack(sh, un)
def setup_inputs_alike(rng):
    sh, un = parts(rng)
    un[:, 0] = un[0, 0].copy()
    un[:, 1] = rng.choice(np.array([0, 1, W - 1, W // 2]), (N, UN, P))
    un[:, 2] = un[:, 2, :1].copy()
    un[:, 3] = un[:, 3, :, :1].copy()
    un[:, 4] = 0
    un[:, 5, 1::2] = un[:, 5, ::2].copy()
    un[:, 6, :, P // 2:] = un[:1, 6, :1, P // 2:].copy()
    return pack(sh, un)
def setup_inputs_ends(rng):
    sh, un = parts(rng)
    sh[:, :7] = sh[:1, :7].copy(); x = rng.integers(1, W, (N, 7, UN)); un[:, :7] = 0
    for g, e in enumerate((0, P - 1, P // 2 - 1, P // 2, 1, P - 2, int(rng.integers(0, P)))): un[:, g, :, e] = x[:, g]
    return pack(sh, un)
def setup_inputs_rare(rng):
    sh, un = parts(rng)
    few = W // (8 * P) * np.array([1, 2, 3, 4, 2, 3])[:, None, None]
    hit = np.argsort(rng.random((N, 6, 1, W)), axis=-1) < few
    v = rng.integers(1, 256, (N, 6, 16, W)); v[:, 0] = 1; v[:, 1] = 255
    v = np.where(hit, v, 0); v[:, 4:] = 255 - v[:, 4:]
    sh[:, :6] = v
    sh[:, 6] = rng.choice(np.array([0, 1, 2, 253, 254, 255]), (N, 16, W))
    sh[:, 7] = np.clip(rng.integers(-64, 320, (N, 16, W)), 0, 255)
    sh = np.where((sh == 0) & (rng.random(sh.shape, dtype=np.float32) < 0.5), np.float32(-0.0), sh)
    return pack(sh, un)
def setup_inputs_spread(rng):
    sh, un = parts(rng)
    k = np.exp2(8 * rng.random((N, 8, 1, W))) * (rng.random((N, 8, 1, W)) > 0.0625)
    sh = np.minimum(np.floor(rng.random((N, 8, 16, W)) * k), 255)
    un = np.minimum((W * rng.random((N, 8, UN, P)) ** rng.choice(np.array([1, 2, 4, 8]), (N, 8, 1, 1))).astype(np.int64), W - 1)
    return pack(sh, un)
def check_inputs(d):
    bad = []; v = np.asarray(d["shelf"]).astype(np.float32)
    if not np.all((v >= 0) & (v <= 255) & (v == np.floor(v))): bad.append("values of shelf")
    if np.min(d["units"]) < 0 or np.max(d["units"]) > W - 1: bad.append("range of units")
    return bad
def reference(shelf, units):
    tab = np.ascontiguousarray(shelf.astype(np.float32).astype(np.int16).reshape(N, 8, 16, W).transpose(0, 1, 3, 2))
    un = np.stack([gentries(a) for a in units]).astype(np.int64).reshape(N, 8, UN, P)
    A = np.zeros((N, 8), np.int64); rank = np.arange(N); place = np.arange(P)
    n3, g3 = rank[:, None, None], np.arange(8)[None, :, None]
    def measure(x):
        z = (A[:, :, None, None] + np.add.accumulate(x, axis=3)) & 4095
        c = ((z * z >> SH) + x) & (W - 1)
        b = tab[n3[..., None], g3[..., None], c]
        return np.sum((np.max(b, axis=3) - np.min(b, axis=3)).astype(np.int64), axis=3)
    for m in MS:
        mate = rank ^ m; low = (rank < mate)[:, None, None]
        q = measure(un)
        order = np.argsort(np.where(low, -q, q), axis=2, kind="stable")
        own = un[n3, g3, order]; qo = q[n3, g3, order]; far = own[mate]; qf = qo[mate]
        s0 = np.where(low, qo > qf, qf > qo)
        first = np.zeros((N, 8, UN), np.int64); n = P
        while n > 1:
            n = n // 2
            swapped = (place >= first[..., None]) & (place < first[..., None] + n)
            a = measure(np.where(swapped, far, own)); b = a[mate]
            s = np.where(low, a > b, b > a)
            first = np.where(s != s0, first, first + n)
        takes = np.where(low, qo < qf, qo <= qf)
        new = np.where(takes[..., None] & (place == first[..., None]), far, own)
        un = np.zeros_like(un); un[n3, g3, order] = new
        A = np.sum(first, axis=2)
    return {"yu": np.stack([gtable(a.reshape(8, -1)) for a in un]).astype(np.float32), "yq": q.astype(np.float32)}

@@ -1,0 +1,501 @@
+from concourse.mybir import AluOpType as OP, ActivationFunctionType as AF
+
+BCH = [(0, 64), (64, 128), (128, 192), (192, 256)]
+TCH = [(0, 44), (44, 86), (86, 128)]
+SUBS = 2
+NS = 10
+ROUNDS = (1, 2, 3)
+P2 = 2.0 ** -12
+NE = 8
+
+SCRATCH = {}
+for _n, _w, _d in [
+        ("sh", 4096, "bfloat16"), ("sh1", 4096, "bfloat16"), ("sh2", 4096, "bfloat16"), ("sh3", 4096, "bfloat16"), ("uin", 256, "int32"),
+        ("ip", 1, "int32"), ("im", 128, "int32"), ("jj", 1024, "int32"), ("ii", 8, "int32"), ("fc", 24, "float32"), ("mg", 128, "int32"),
+        ("bf", 128, "float32"), ("gef", 128, "float32"), ("trif", 128, "float32"), ("idf", 128, "float32"), ("wa", 128, "float32"),
+        ("mh", 19 * 128, "float16"), ("mb", 13 * 128, "bfloat16"), ("da", 6 * 128, "float16"),
+        ("half", 8, "float16"), ("one", 128, "float16"), ("ones", 256, "bfloat16"), ("mhalf", 64, "bfloat16"), ("tie", 256, "bfloat16"),
+        ("dm", 64, "float32"), ("rm", 1024, "bfloat16"), ("bg", 1024, "bfloat16"), ("bs", 8, "float32"), ("bt", 8, "float32"),
+        ("ac", 16, "float32"), ("xc", 256, "float16"), ("tb", 256, "bfloat16"), ("sq", 256, "float32"), ("yb", 256, "int32"),
+        ("cb", 256, "int32"), ("c16", 256, "uint16"), ("gb", 4096, "bfloat16"), ("mx", 4096, "bfloat16"), ("mn", 4096, "bfloat16"),
+        ("ksb", 256, "float32"), ("kd", 256, "float32"), ("kc", 256, "float32"), ("vu", 256, "int32"), ("acc", 16, "float32"),
+        ("trash", 1024, "bfloat16"), ("cmp", 4096, "bfloat16"), ("cs", 4096, "bfloat16"), ("rl", 48, "uint16"),
+        ("vs", 3 * 272, "int32"), ("vf", 3 * 144, "int32"), ("nx", 3 * 272, "int32"), ("nf", 3 * 144, "int32"),
+        ("oi", 256, "int32"), ("oc", 256, "float16"), ("qo", 128, "int32"), ("qf", 128, "int32"), ("d", 128, "int32"),
+        ("s0", 128, "float32"), ("sg", 4 * 128, "float32"), ("tl", 256, "float32"), ("u", 128, "float32"), ("e", 128, "float32"),
+        ("rr", 128, "float16"), ("r5", 128, "float32"), ("r2", 256, "float32"), ("ns", 256, "int32"), ("cnt", 8, "float32"),
+        ("sgn", 128, "bfloat16"), ("yo", 256, "float32"), ("qi", 256, "int32"), ("qy", 256, "float32")]:
+    SCRATCH[_n] = ("sbuf", [128, _w], _d)
+for _b in range(8):
+    SCRATCH["p%d" % _b] = ("psum", [128, 512], "float32")
+SEMAPHORES = ["eP", "eV", "eS", "eG", "ldu", "lds0", "lds1", "lds2", "lds3", "lsem", "styu0", "styu1", "styq"]
+SEMAPHORES += ["v%d" % r for r in range(3)] + ["n%d" % r for r in range(3)] + ["s0_%d" % h for h in range(4)] + ["s1_0", "s2_0"]
+
+CY = 0.00083
+COST = {"V": 0.0302, "S": 0.0645, "P": 0.0405, "lat": 0.161, "self": 0.0428, "send": 0.8, "net": 2.6, "g": 1.8198, "long": 0.2036}
+WIN = 0.0124
+
+
+def build(rank):
+    ops, hist, bank, stg = [], {}, {}, [None]
+
+    def add(eng, fn, rd, wr, cost, sem=None, amt=1, dep=(), kind="c", lat=None, n=1):
+        i = len(ops)
+        deps = set(dep)
+        for acc, w in [(a, False) for a in rd] + [(a, True) for a in wr]:
+            nm, lo, hi = acc[0], acc[1], acc[2]
+            if nm[0] == "p" and nm[1:].isdigit():
+                st = bank.setdefault(nm, [None, [], []])
+                if st[0] != eng:
+                    st[2] = st[1]
+                    st[1] = []
+                    st[0] = eng
+                deps.update(st[2])
+                st[1].append(i)
+                continue
+            keep = []
+            for (a, b, j, jw) in hist.setdefault(nm, []):
+                over = a < hi and lo < b and j != i
+                if over and (w or jw):
+                    deps.add(j)
+                if not (over and w and lo <= a and b <= hi):
+                    keep.append((a, b, j, jw))
+            keep.append((lo, hi, i, w))
+            hist[nm] = keep
+        deps.discard(i)
+        ops.append({"e": eng, "fn": fn, "d": sorted(deps), "c": cost, "sem": sem, "amt": amt, "k": kind, "lat": lat,
+                    "o": [a[0] for a in wr], "s": stg[0], "n": n})
+        return i
+
+    def A(nm, lo=0, hi=None, st=1):
+        return (nm, lo, SCRATCH[nm][1][1] if hi is None else hi, st)
+
+    def ap(T, a):
+        return T[a[0]][:, a[1]:a[2]:a[3]] if a[3] != 1 else T[a[0]][:, a[1]:a[2]]
+
+    def size(a):
+        return (a[2] - a[1] + a[3] - 1) // a[3]
+
+    def vcost(n, f=1.0):
+        return COST["V"] + max(64, n * f) * CY
+
+    def arg(T, s):
+        return ap(T, s) if isinstance(s, tuple) else s
+
+    def cols(*xs):
+        return [s for s in xs if isinstance(s, tuple)]
+
+    def ts(out, i0, s1, s2, o1, o2=None):
+        def fn(g, T):
+            if o2 is None:
+                return g.vector.tensor_scalar(ap(T, out), ap(T, i0), arg(T, s1), None, o1)
+            return g.vector.tensor_scalar(ap(T, out), ap(T, i0), arg(T, s1), arg(T, s2), o1, o2)
+        return add("V", fn, [i0] + cols(s1, s2), [out], vcost(size(out)))
+
+    def tt(out, i0, i1, op):
+        f = 1 if (i0[0][0] == "p" or i1[0][0] == "p") else 2
+        return add("V", lambda g, T: g.vector.tensor_tensor(ap(T, out), ap(T, i0), ap(T, i1), op), [i0, i1], [out], vcost(size(out), f))
+
+    def cp(out, i0):
+        return add("V", lambda g, T: g.vector.tensor_copy(ap(T, out), ap(T, i0)), [i0], [out], vcost(size(out)))
+
+    def scan(out, d0, d1, o0, o1, f=0.5):
+        return add("V", lambda g, T: g.vector.tensor_tensor_scan(ap(T, out), ap(T, d0), ap(T, d1), 0.0, o0, o1), [d0, d1], [out], vcost(size(out), f))
+
+    def act(out, i0, func, bias=None, scale=None, acc=None):
+        def fn(g, T):
+            kw = {}
+            if bias is not None:
+                kw["bias"] = arg(T, bias)
+            if scale is not None:
+                kw["scale"] = arg(T, scale)
+            if acc is not None:
+                kw["accum_out"] = ap(T, acc)
+            return g.scalar.activation(ap(T, out), ap(T, i0), func, **kw)
+        return add("S", fn, [i0] + cols(bias, scale), [out] + ([acc] if acc else []), COST["S"] + size(out) * CY)
+
+    def mm(terms, first=True, last=True, dep=()):
+        def fn(g, T):
+            r = None
+            for k, (o, l, x) in enumerate(terms):
+                r = g.tensor.matmul(ap(T, o), ap(T, l), ap(T, x), first and k == 0, last and k == len(terms) - 1)
+            return r
+        c = sum(max(64, size(o)) * (4 if l[0] == "wa" else 1) for o, l, x in terms) * 0.0007
+        return add("P", fn, [x for tm in terms for x in tm[1:]], [terms[0][0]], COST["P"] + c, n=len(terms), dep=dep)
+
+    def gath(out, win, off, eng):
+        n = size(out)
+        if eng == "S":
+            return add("S", lambda g, T: g.scalar.activation(ap(T, out), ap(T, win).indirect(ap(T, off)), AF.Copy), [win, off], [out], 0.065 + n * CY * COST["g"])
+        return add("V", lambda g, T: g.vector.tensor_copy(ap(T, out), ap(T, win).indirect(ap(T, off))), [win, off], [out], 0.05 + n * CY * COST["g"])
+
+    def MH(k):
+        return A("mh", 128 * k, 128 * k + 128)
+
+    def MB(k):
+        return A("mb", 128 * k, 128 * k + 128)
+
+    def DA(k):
+        return A("da", 128 * k, 128 * k + 128)
+
+    def FC(k):
+        return A("fc", k, k + 1)
+
+    def iota(out, pat, base, cm, flag=False):
+        def fn(g, T):
+            if flag:
+                return g.iota(ap(T, out), pat, base, cm, allow_small_or_imprecise_dtypes=True)
+            return g.iota(ap(T, out), pat, base, cm)
+        return add("G", fn, [], [out], 0.13 + 2 * size(out) * CY)
+
+    def dma(dst, src, rd, wr, sem, lat):
+        return add("Y", lambda g, T: g.sync.dma_start(dst(T), src(T)), rd, wr, 0.1, sem=sem, amt=16, kind="dma", lat=lat)
+
+    def send(mate, dst, src, here, sem, net, dep=()):
+        i = add("G", (mate, dst, src, sem), [src], [], COST["send"], dep=dep, kind="send")
+        add("N", None, [], [here], 0.0, sem=sem, amt=NE, dep=(i,), kind="net", lat=net)
+        return i
+
+    def send_shelf(r, cuts, net, dep=()):
+        for h, (a, b) in enumerate(cuts):
+            far = A("sh%d" % (r + 1), a, b)
+            send(rank ^ ROUNDS[r], far, A("sh", a, b), far, "s%d_%d" % (r, a // 1024), net + 3 * h, dep)
+
+    dma(lambda T: T.uin[:], lambda T: T.units[:], [], [A("uin")], "ldu", 2.5)
+    for h in range(4):
+        a, b = 1024 * h, 1024 * h + 1024
+        dma(lambda T, a=a, b=b: T.sh[:, a:b], lambda T, a=a, b=b: T.shelf[:, a:b], [], [A("sh", a, b)], "lds%d" % h, 3.5 + 1.5 * h)
+    iota(A("ip"), [[1, 1]], 0, 1)
+    iota(A("im"), [[1, 128]], 0, 0)
+    iota(A("jj"), [[0, 64], [1, 16]], 0, 0)
+    iota(A("tie"), [[-1, 256]], 255, 0, True)
+    send_shelf(0, [(0, 1024), (1024, 2048), (2048, 3072)], 8.0)
+    cp(FC(0), A("ip"))
+    ts(A("ii", 0, 1), A("ip"), 4, None, OP.arith_shift_right)
+    cp(FC(1), A("ii", 0, 1))
+    ts(A("ii", 1, 2), A("ip"), 15, None, OP.bitwise_and)
+    cp(FC(2), A("ii", 1, 2))
+    ts(A("mg"), A("im"), 4, None, OP.arith_shift_right)
+    ts(A("bf"), A("mg"), FC(1), None, OP.is_equal)
+    ts(A("gef"), A("im"), FC(0), None, OP.is_ge)
+    tt(A("trif"), A("bf"), A("gef"), OP.mult)
+    ts(A("idf"), A("im"), FC(0), None, OP.is_equal)
+    ts(MH(0), A("trif"), 1.0, None, OP.mult)
+    ts(MH(1), A("idf"), 32.0, None, OP.mult)
+    ts(MH(2), A("idf"), 1.0, None, OP.mult)
+    ts(A("half"), A("im", 0, 8), 0.0, 0.5, OP.mult, OP.add)
+    ts(A("one"), A("im"), 0.0, 1.0, OP.mult, OP.add)
+    ts(DA(0), A("idf"), -2048.0, None, OP.mult)
+    for k, src, f in ((0, "idf", -4096.0), (1, "idf", -8388608.0 + 65536.0), (6, "bf", 1.0), (7, "bf", -1.0), (8, "bf", 256.0),
+                      (9, "bf", -256.0), (10, "bf", 4096.0), (11, "bf", -4096.0), (12, "idf", 1.0)):
+        act(MB(k), A(src), AF.Copy, scale=f)
+    add("V", lambda g, T: g.vector.memset(T.ones[:], 1.0), [], [A("ones")], vcost(128))
+    add("V", lambda g, T: g.vector.memset(T.mhalf[:], -0.5), [], [A("mhalf")], vcost(64))
+    ts(A("rm"), A("jj"), 0, None, OP.is_gt)
+    ts(A("bg"), A("jj"), 0, 256.0, OP.is_equal, OP.mult)
+    ts(A("dm"), A("jj", 0, 64), FC(2), None, OP.is_equal)
+    for t in range(4):
+        ts(A("ii", 2 + t, 3 + t), A("ip"), 8 >> t, None, OP.bitwise_and)
+        ts(FC(3 + t), A("ii", 2 + t, 3 + t), 0, None, OP.is_equal)
+        ts(FC(7 + t), FC(3 + t), -16384.0, 8192.0, OP.mult, OP.add)
+        ts(FC(11 + t), FC(3 + t), 65536.0, -8388608.0 + 65536.0, OP.mult, OP.add)
+        ts(FC(15 + t), FC(3 + t), -1.0, None, OP.mult)
+        ts(MH(3 + t), A("trif"), FC(3 + t), None, OP.mult)
+        ts(MH(7 + t), A("trif"), FC(15 + t), None, OP.mult)
+        ts(MH(11 + t), A("idf"), FC(3 + t), 32.0, OP.mult, OP.mult)
+        ts(MH(15 + t), A("idf"), FC(3 + t), -32.0, OP.mult, OP.mult)
+        act(MB(2 + t), A("idf"), AF.Copy, scale=FC(11 + t))
+    ts(A("wa"), A("bf"), FC(2), 0.5, OP.mult, OP.mult)
+    h1 = A("half", 0, 1)
+
+    def pcol(k):
+        return A("p7", 500 + k, 501 + k)
+    mm([(pcol(0), MH(0), h1)])
+    ts(A("bs", 0, 1), pcol(0), 4096.0, 788480.0, OP.mult, OP.add)
+    ts(A("bt", 0, 1), A("bs", 0, 1), P2, -4095.0 / 8192, OP.mult, OP.add)
+    for t in range(4):
+        mm([(pcol(1 + t), MH(0), h1), (pcol(1 + t), MH(3 + t), h1)])
+    ts(A("bs", 1, 5), A("p7", 501, 505), 4096.0, 788480.0, OP.mult, OP.add)
+    ts(A("bt", 1, 5), A("bs", 1, 5), P2, -4095.0 / 8192, OP.mult, OP.add)
+    ts(A("xc"), A("uin"), -2048.0, None, OP.add)
+    a0 = 264 if rank < (rank ^ ROUNDS[0]) else 7
+    ts(A("vs", a0, a0 + 1), A("ip"), 0.0, -2048.0, OP.mult, OP.add)
+
+    def columns(c, lo, hi, k, pre, late, xpt):
+        n = hi - lo
+        x, w, xp = A("p%d" % (2 * c), 0, n), A("p%d" % (2 * c + 1), 0, n), A("p%d" % (2 * c), 384, 384 + n)
+        tb = A("tb", lo, hi)
+        i = mm(pre(x), last=not late(x))
+        if late(x):
+            i = mm(late(x), first=False, dep=(i,))
+        i = mm(pre(w) + late(w), last=False, dep=(i,))
+        ts(tb, x, P2, A("bt", k, k + 1), OP.mult, OP.add)
+        mm([(w, MB(0), tb)], first=False, dep=(i,))
+        mm(xpt(xp))
+        act(A("sq", lo, hi), w, AF.Square, bias=A("bs", k, k + 1))
+        tt(A("yb", lo, hi), A("sq", lo, hi), xp, OP.add)
+        ts(A("cb", lo, hi), A("yb", lo, hi), 5, 4095, OP.arith_shift_right, OP.bitwise_and)
+        cp(A("c16", lo, hi), A("cb", lo, hi))
+
+    def gather_scan(parts):
+        for (a, b, win) in parts:
+            gath(A("gb", 16 * a, 16 * b), A(win), A("c16", a, b), "S")
+        for (a, b, win) in parts:
+            m = 16 * (b - a)
+            scan(A("mx", 16 * a, 16 * b), A("rm", 0, m), A("gb", 16 * a, 16 * b), OP.mult, OP.max)
+            scan(A("mn", 16 * a, 16 * b), A("bg", 0, m), A("gb", 16 * a, 16 * b), OP.max, OP.min)
+
+    def ends(nm, a, b):
+        return A(nm, 16 * a + 15, 16 * b, 16)
+
+    for r, m in enumerate(ROUNDS):
+        mate = rank ^ m
+        low = rank < mate
+        for c, (lo, hi) in enumerate(BCH):
+            n = hi - lo
+            stg[0] = 1000 * r + c
+            xs = A("xc", lo, hi)
+            columns(c, lo, hi, 0, lambda x: [(x, MH(0), xs), (x, DA(r), A("one", 0, n))], lambda x: [],
+                    lambda x: [(x, MH(1), xs), (x, MB(1), A("ones", 0, n))])
+            st = n // SUBS // 2 * 2
+            cut = [lo + s * st for s in range(SUBS)] + [hi]
+            gather_scan([(cut[s], cut[s + 1], "sh") for s in range(SUBS)])
+            mx, mn = ends("mx", lo, hi), ends("mn", lo, hi)
+            kp, vp = A("p%d" % (2 * c + 1), 128, 128 + n), A("p%d" % (2 * c + 1), 256, 256 + n)
+            mm([(kp, MB(8 if low else 9), mx), (kp, MB(9 if low else 8), mn), (kp, MB(12), A("tie", lo, hi))])
+            mm([(vp, MB(10), mx), (vp, MB(11), mn), (vp, MH(2), xs)])
+            tt(A("kd", lo, hi), kp, A("dm", 0, n), OP.mult)
+            cp(A("ksb", lo, hi), kp)
+            scan(A("kc", lo, hi), A("rm", 0, n), A("kd", lo, hi), OP.mult, OP.add, 1)
+            ts(A("vu", lo, hi), vp, 2048.0, None, OP.add)
+        stg[0] = 1000 * r + 20
+        for j in range(16):
+            kcol = A("kc", 16 * j + 15, 16 * j + 16)
+            if j < NS:
+                act(A("trash", 256 * (j % 4), 256 * (j % 4) + 256), A("ksb"), AF.Sign, bias=kcol, scale=-1.0, acc=A("acc", j, j + 1))
+            else:
+                ts(A("cmp", 256 * j, 256 * j + 256), A("ksb"), kcol, None, OP.is_gt)
+                scan(A("cs", 256 * j, 256 * j + 256), A("ones"), A("cmp", 256 * j, 256 * j + 256), OP.mult, OP.add)
+        ts(A("rl", 16 * r + NS, 16 * r + 16), A("cs", 256 * NS + 255, 4096, 256), 1.0, None, OP.mult)
+        ts(A("rl", 16 * r, 16 * r + NS), A("acc", 0, NS), -0.5, 127.5, OP.mult, OP.add)
+        rl = A("rl", 16 * r, 16 * r + 16)
+        v0 = 272 * r + 8
+        vw = A("vs", v0, v0 + 256)
+        add("V", lambda g, T, vw=vw, rl=rl: g.vector.tensor_copy(ap(T, vw).indirect(ap(T, rl)), T.vu[:]), [rl, A("vu")], [vw], 0.05 + 256 * CY * 3)
+        mine = v0 + (0 if low else 128)
+        f0 = 144 * r
+        x0 = f0 + (1 if low else 0)
+        far = A("vf", f0, f0 + 129)
+        iv = send(mate, far, A("vs", v0 + 128, v0 + 257) if low else A("vs", v0 - 1, v0 + 128), far, "v%d" % r, COST["net"])
+        mv, fv = A("vs", mine, mine + 128), A("vf", x0, x0 + 128)
+        stg[0] = 1000 * r + 21
+        if r == 0:
+            send_shelf(0, [(3072, 4096)], 6.0, (iv,))
+        if r < 2:
+            send_shelf(r + 1, [(0, 4096)], 16.0, (len(ops) - 2,))
+        for c, (a, b) in enumerate(TCH):
+            n = b - a
+            stg[0] = 1000 * r + 100 + c
+            L, H = A("oi", 2 * a, 2 * a + n), A("oi", 2 * a + n, 2 * b)
+            cL, cH = A("oc", 2 * a, 2 * a + n), A("oc", 2 * a + n, 2 * b)
+            ow, fr = (L, H) if low else (H, L)
+            cow, cfr = (cL, cH) if low else (cH, cL)
+            ts(ow, A("vs", mine + a, mine + b), 4095, None, OP.bitwise_and)
+            ts(cow, ow, -2048.0, None, OP.add)
+            ts(fr, A("vf", x0 + a, x0 + b), 4095, None, OP.bitwise_and)
+            ts(cfr, fr, -2048.0, None, OP.add)
+            d = A("d", a, b)
+            tt(d, H, L, OP.subtract)
+            ts(d, d, 4095, None, OP.bitwise_and)
+            ts(A("rr", a, b), d, -2048.0, None, OP.add)
+        stg[0] = 1000 * r + 100
+        ac = A("ac", 4 * r + 2, 4 * r + 3)
+        fa = f0 if low else f0 + 128
+        cp(ac, A("vf", fa, fa + 1))
+        ts(DA(3 + r), A("idf"), ac, None, OP.mult)
+        stg[0] = 1000 * r + 103
+        ts(A("qo"), mv, 12, None, OP.arith_shift_right)
+        ts(A("qf"), fv, 12, None, OP.arith_shift_right)
+        qL, qH = (A("qo"), A("qf")) if low else (A("qf"), A("qo"))
+        tt(A("s0"), qL, qH, OP.is_gt)
+        ts(A("s0"), A("s0"), 2.0, -1.0, OP.mult, OP.add)
+        for t in range(4):
+            stg[0] = 1000 * r + 103 + 4 * t
+            ts(A("sg", 128 * t, 128 * t + 128), A("s0"), FC(7 + t), None, OP.mult)
+        tt(A("tl", 0, 128), qL, qH, OP.is_lt)
+        ts(A("tl", 128, 256), A("tl", 0, 128), -1.0, None, OP.add)
+        if r == 2:
+            ts(A("qi"), A("vu"), 12, None, OP.arith_shift_right)
+            cp(A("qy"), A("qi"))
+            dma(lambda T: T.yq[:], lambda T: T.qy[0:128:16, :], [A("qy")], [], "styq", 2.0)
+        dL, dH = (DA(r), DA(3 + r)) if low else (DA(3 + r), DA(r))
+        wL, wH = ("sh", "sh%d" % (r + 1)) if low else ("sh%d" % (r + 1), "sh")
+        for t in range(4):
+            for c, (a, b) in enumerate(TCH):
+                n = b - a
+                lo, mid, hi = 2 * a, 2 * a + n, 2 * b
+                stg[0] = 1000 * r + 100 + 4 * t + c
+                R, oc, one = A("rr", a, b), A("oc", lo, hi), A("one", 0, n)
+
+                def lh(x):
+                    return (x[0], x[1], x[1] + n, 1), (x[0], x[1] + n, x[1] + 2 * n, 1)
+                columns(c, lo, hi, 1 + t,
+                        lambda x: [(x, MH(0), oc), (lh(x)[0], dL, one), (lh(x)[1], dH, one)],
+                        lambda x: [(lh(x)[0], MH(3 + t), R), (lh(x)[1], MH(7 + t), R)],
+                        lambda x: [(x, MH(1), oc), (x, MB(2 + t), A("ones", 0, 2 * n)), (lh(x)[0], MH(11 + t), R), (lh(x)[1], MH(15 + t), R)])
+                gather_scan([(lo, mid, wL), (mid, hi, wH)])
+                q = A("p%d" % (2 * c + 1), 128, 128 + n)
+                i = mm([(q, MB(12), A("mhalf", 0, n)), (q, MB(6), ends("mx", lo, mid)), (q, MB(7), ends("mn", lo, mid))], last=False)
+                mm([(q, MB(7), ends("mx", mid, hi)), (q, MB(6), ends("mn", mid, hi))], first=False, dep=(i,))
+                stg[0] += 4
+                u, e = A("u", a, b), A("e", a, b)
+                tt(u, q, A("sg", 128 * t + a, 128 * t + b), OP.mult)
+                tt(e, A("d" if t == 0 else "e", a, b), u, OP.min)
+                if t < 3:
+                    ts(R, e, 0.0, -2048.0, OP.max, OP.add)
+                    continue
+                if r < 2:
+                    act(A("sgn", a, b), e, AF.Sign, bias=0.5, acc=A("cnt", c, c + 1))
+                r5, rL, rH = A("r5", a, b), A("r2", lo, mid), A("r2", mid, hi)
+                ts(r5, e, 0.0, None, OP.max)
+                tt(rL, r5, A("tl", a, b), OP.mult)
+                tt(rH, r5, A("tl", 128 + a, 128 + b), OP.mult)
+                tt(A("ns", lo, hi), A("oi", lo, hi), A("r2", lo, hi), OP.add)
+                sL, sH = A("ns", lo, mid), A("ns", mid, hi)
+                so, sf = (sL, sH) if low else (sH, sL)
+                ts(A("nf", x0 + a, x0 + b), sf, 4095, None, OP.bitwise_and)
+                ts(A("nx", mine + a, mine + b), so, 4095, None, OP.bitwise_and)
+        stg[0] = 1000 * r + 200
+        nw = A("nx", v0, v0 + 256)
+        n0 = 144 * r
+        if r < 2:
+            pa = A("p0", 500, 501)
+            cn = [(pa, A("wa"), A("cnt", c, c + 1)) for c in range(len(TCH))]
+            mm(cn[-1:], first=False, dep=(mm(cn[:-1], last=False),))
+            fcol = n0 if low else n0 + 128
+            ts(A("nf", fcol, fcol + 1), pa, 7680.0, None, OP.add)
+            ts(A("ac", 4 * r, 4 * r + 1), pa, 5632.0, None, OP.add)
+            front, back = A("nx", v0 - 1, v0 + 128), A("nx", v0 + 128, v0 + 257)
+            send(mate, front if low else back, A("nf", n0, n0 + 129), back if low else front, "n%d" % r, COST["net"])
+            rcv = A("nx", v0 + 256, v0 + 257) if low else A("nx", v0 - 1, v0)
+            asum = A("ac", 4 * r + 1, 4 * r + 2)
+            tt(asum, A("ac", 4 * r, 4 * r + 1), rcv, OP.add)
+            ts(DA(r + 1), A("idf"), asum, None, OP.mult)
+            vn = 272 * (r + 1) + 8
+            acol = A("vs", vn + 256, vn + 257) if rank < (rank ^ ROUNDS[r + 1]) else A("vs", vn - 1, vn)
+            cp(acol, asum)
+            for c, (lo, hi) in enumerate(BCH):
+                stg[0] = 1000 * (r + 1) + c
+                xs, rc = A("xc", lo, hi), A("rl", 16 * r + lo // 16, 16 * r + hi // 16)
+                add("V", lambda g, T, xs=xs, rc=rc, nw=nw: g.vector.tensor_scalar(ap(T, xs), ap(T, nw).indirect(ap(T, rc)), -2048.0, None, OP.add),
+                    [rc, nw], [xs], 0.05 + (hi - lo) * CY * COST["g"])
+        else:
+            front, back = A("nx", v0, v0 + 128), A("nx", v0 + 128, v0 + 256)
+            send(mate, front if low else back, A("nf", x0, x0 + 128), back if low else front, "n%d" % r, COST["net"])
+            for h in range(2):
+                a, b = 128 * h, 128 * h + 128
+                gath(A("yo", a, b), nw, A("rl", 16 * r + 8 * h, 16 * r + 8 * h + 8), "V")
+                dma(lambda T, a=a, b=b: T.yu[:, a:b], lambda T, a=a, b=b: T.yo[:, a:b], [A("yo", a, b)], [], "styu%d" % h, 2.0)
+    return ops
+
+
+def schedule(ops):
+    n = len(ops)
+    succ = [[] for _ in ops]
+    for i, o in enumerate(ops):
+        for j in o["d"]:
+            succ[j].append(i)
+
+    def lat(j, i):
+        if ops[j]["lat"] is not None:
+            return ops[j]["lat"]
+        return COST["self"] if ops[j]["e"] == ops[i]["e"] else COST["lat"]
+    pr = [0.0] * n
+    sg = [9999 if o["s"] is None else o["s"] for o in ops]
+    for i in range(n - 1, -1, -1):
+        pr[i] = ops[i]["c"] + max([pr[s] + lat(i, s) for s in succ[i]] + [0.0])
+        if ops[i]["s"] is None:
+            sg[i] = min([sg[x] for x in succ[i]] + [9999])
+    cnt = [len(o["d"]) for o in ops]
+    ready, start = [0.0] * n, [0.0] * n
+    free, avail, order = {}, {}, []
+    for i in range(n):
+        if cnt[i] == 0:
+            avail.setdefault(ops[i]["e"], []).append(i)
+    while len(order) < n:
+        best = None
+        for e, lst in avail.items():
+            if not lst:
+                continue
+            f = free.get(e, 0.0)
+            s0 = max(f, min(ready[k] for k in lst))
+            if e == "N":
+                i = min(lst, key=lambda k: ready[k])
+                s = ready[i]
+            else:
+                i = min((k for k in lst if ready[k] <= s0 + WIN), key=lambda k: (ops[k]["c"] > COST["long"], sg[k], -pr[k]))
+                s = max(f, ready[i])
+            if best is None or s < best[0]:
+                best = (s, i, e)
+        s, i, e = best
+        avail[e].remove(i)
+        start[i] = s
+        end = s + ops[i]["c"]
+        if e != "N":
+            free[e] = end
+        order.append(i)
+        for k in succ[i]:
+            ready[k] = max(ready[k], end + lat(i, k))
+            cnt[k] -= 1
+            if cnt[k] == 0:
+                avail.setdefault(ops[k]["e"], []).append(k)
+    return order, start
+
+
+def rank_program(g, core, T, topo):
+    rank = T.rank_of(core)
+    if rank is None:
+        return
+    ops = build(rank)
+    order, start = schedule(ops)
+    queue = {"P": g.tensor, "V": g.vector, "S": g.scalar, "G": g, "Y": g.sync}
+    own = {"P": "eP", "V": "eV", "S": "eS", "G": "eG"}
+    known = {e: {} for e in queue}
+    after = {}
+    count, sent = {}, 0
+    for i in order:
+        o = ops[i]
+        e = o["e"]
+        if e == "N":
+            o["at"] = (o["sem"], o["amt"])
+            after[i] = {o["sem"]: o["amt"]}
+            continue
+        kn = known[e]
+        need = [ops[j]["at"] + (j,) for j in o["d"]
+                if (e, ops[j]["e"]) != ("P", "P") and kn.get(ops[j]["at"][0], 0) < ops[j]["at"][1]]
+        for (s, v, j) in need:
+            if not any(j2 != j and after[j2].get(s, 0) >= v and (s2 != s or v2 > v or j2 > j) for (s2, v2, j2) in need):
+                queue[e].wait_ge(T.sem[s], v)
+        for (s, v, j) in need:
+            for s2, v2 in after[j].items():
+                kn[s2] = max(kn.get(s2, 0), v2)
+        if o["k"] == "send":
+            mate, dst, src, sem = o["fn"]
+            to = T.cores[mate]
+            rid, pid, ring = topo.addr(to)
+            eng = topo.engines(core, to)[-NE:]
+            g.remote_dma(T[dst[0]][:, dst[1]:dst[2]], T[src[0]][:, src[1]:src[2]], T.sem[sem], T.sem.lsem, pid, rid, sum(1 << x for x in eng))
+            sent += len(eng)
+            after[i] = dict(kn)
+            o["at"] = ("lsem", 0)
+            continue
+        s = o["sem"] or own[e]
+        o["fn"](g, T).then_inc(T.sem[s], o["amt"])
+        count[s] = count.get(s, 0) + o["amt"]
+        o["at"] = (s, count[s])
+        after[i] = dict(kn)
+        after[i][s] = count[s]
+    for s, v in sorted(count.items()):
+        if known["G"].get(s, 0) < v:
+            g.wait_ge(T.sem[s], v)
+    g.wait_ge(T.sem.lsem, sent)

@@ -1,45 +1,54 @@
-from concourse.mybir import AluOpType as OP, ActivationFunctionType as AF
+from concourse.bass import DstId, RemoteDMATransfer
+from concourse.mybir import AluOpType as OP, ActivationFunctionType as AF, AxisListType as AX
 
-BCH = [(0, 64), (64, 128), (128, 192), (192, 256)]
-TCH = [(0, 44), (44, 86), (86, 128)]
-SUBS = 2
-NS = 10
+N = 4
 ROUNDS = (1, 2, 3)
+CH = [(0, 64), (64, 128)]
 P2 = 2.0 ** -12
-NE = 8
+PAR = {"subs": 2, "ns": 4, "off": 0.0, "tb": "V", "vu": "S", "sig": "S", "nw": "S", "qy": "S", "coff": 0.5, "mat": "S"}
+SL = 512
 
+MH_ = ["T", "I", "nI", "I32", "R0", "R1"] + [k + str(i) for k in ("TL", "IL") for i in (1, 2, 3)]
+MH_ += [k + str(r) for k in ("T1", "S1", "Pm") for r in range(3)] + ["W0", "W1"]
+MB_ = ["B", "KLE", "n4096", "cst", "Ko+", "Ko-", "K0+", "K0-", "K1+", "K1-", "D4", "D5", "V+", "V-", "tmp"]
+MB_ += ["Q%d%s" % (r, s) for r in range(3) for s in "+-"]
 SCRATCH = {}
 for _n, _w, _d in [
-        ("sh", 4096, "bfloat16"), ("sh1", 4096, "bfloat16"), ("sh2", 4096, "bfloat16"), ("sh3", 4096, "bfloat16"), ("uin", 256, "int32"),
-        ("ip", 1, "int32"), ("im", 128, "int32"), ("jj", 1024, "int32"), ("ii", 8, "int32"), ("fc", 24, "float32"), ("mg", 128, "int32"),
-        ("bf", 128, "float32"), ("gef", 128, "float32"), ("trif", 128, "float32"), ("idf", 128, "float32"), ("wa", 128, "float32"),
-        ("mh", 19 * 128, "float16"), ("mb", 13 * 128, "bfloat16"), ("da", 6 * 128, "float16"),
-        ("half", 8, "float16"), ("one", 128, "float16"), ("ones", 256, "bfloat16"), ("mhalf", 64, "bfloat16"), ("tie", 256, "bfloat16"),
-        ("dm", 64, "float32"), ("rm", 1024, "bfloat16"), ("bg", 1024, "bfloat16"), ("bs", 8, "float32"), ("bt", 8, "float32"),
-        ("ac", 16, "float32"), ("xc", 256, "float16"), ("tb", 256, "bfloat16"), ("sq", 256, "float32"), ("yb", 256, "int32"),
+        ("w0", 4096, "bfloat16"), ("w1", 4096, "bfloat16"), ("uin", 256, "int32"), ("ul", 4 * 256, "float16"),
+        ("ip", 1, "int32"), ("ii", 8, "int32"), ("fc", 96, "float32"),
+        ("iu", 256, "bfloat16"), ("uo", 128, "bfloat16"), ("mg", 128, "bfloat16"), ("ms", 128, "bfloat16"), ("m64", 128, "bfloat16"),
+        ("ids", 5 * 128, "bfloat16"), ("jj", SL, "bfloat16"), ("jn", SL, "bfloat16"), ("rm", 64, "bfloat16"), ("dm", 64, "bfloat16"),
+        ("mh", len(MH_) * 128, "float16"), ("mb", len(MB_) * 128, "bfloat16"), ("me", 256, "float32"), ("z", 512, "float16"),
+        ("ones", 256, "bfloat16"), ("mhalf", 64, "float16"), ("bias", 16, "float32"),
+        ("xc", 256, "float16"), ("tb", 256, "bfloat16"), ("sq", 256, "float32"), ("yb", 256, "int32"),
         ("cb", 256, "int32"), ("c16", 256, "uint16"), ("gb", 4096, "bfloat16"), ("mx", 4096, "bfloat16"), ("mn", 4096, "bfloat16"),
-        ("ksb", 256, "float32"), ("kd", 256, "float32"), ("kc", 256, "float32"), ("vu", 256, "int32"), ("acc", 16, "float32"),
+        ("kd", 256, "float32"), ("kc", 256, "float32"), ("vu", 256, "float32"), ("acc", 16, "float32"),
         ("trash", 1024, "bfloat16"), ("cmp", 4096, "bfloat16"), ("cs", 4096, "bfloat16"), ("rl", 48, "uint16"),
-        ("vs", 3 * 272, "int32"), ("vf", 3 * 144, "int32"), ("nx", 3 * 272, "int32"), ("nf", 3 * 144, "int32"),
-        ("oi", 256, "int32"), ("oc", 256, "float16"), ("qo", 128, "int32"), ("qf", 128, "int32"), ("d", 128, "int32"),
-        ("s0", 128, "float32"), ("sg", 4 * 128, "float32"), ("tl", 256, "float32"), ("u", 128, "float32"), ("e", 128, "float32"),
-        ("rr", 128, "float16"), ("r5", 128, "float32"), ("r2", 256, "float32"), ("ns", 256, "int32"), ("cnt", 8, "float32"),
-        ("sgn", 128, "bfloat16"), ("yo", 256, "float32"), ("qi", 256, "int32"), ("qy", 256, "float32")]:
+        ("vs", 6 * 256, "float32"), ("t8", 256, "bfloat16"), ("oc", 256, "float16"), ("w4", 256, "bfloat16"), ("rr", 256, "float16"),
+        ("sg", 256, "bfloat16"), ("tau", 256, "float16"), ("rt", 256, "float16"), ("rf", 256, "float16"), ("u", 256, "float16"),
+        ("kk", 4 * 256, "float16"), ("nw", 512, "float32"), ("ni", 256, "int32"), ("na", 256, "int32"), ("red", 4, "float32"),
+        ("yo", 256, "float32"), ("qy", 256, "float32")]:
     SCRATCH[_n] = ("sbuf", [128, _w], _d)
 for _b in range(8):
     SCRATCH["p%d" % _b] = ("psum", [128, 512], "float32")
-SEMAPHORES = ["eP", "eV", "eS", "eG", "ldu", "lds0", "lds1", "lds2", "lds3", "lsem", "styu0", "styu1", "styq"]
-SEMAPHORES += ["v%d" % r for r in range(3)] + ["n%d" % r for r in range(3)] + ["s0_%d" % h for h in range(4)] + ["s1_0", "s2_0"]
+SCRATCH["sd"] = ("dram", [8, 128, 512], "bfloat16")
+SCRATCH["sl"] = ("dram", [8, 128, 512], "bfloat16")
+SCRATCH["yl"] = ("dram", [8, 128, 128], "float32")
+SCRATCH["ql"] = ("dram", [8, 128, 128], "float32")
+SEMAPHORES = ["eP", "eV", "eS", "eG", "ldu", "lsem", "nu"]
+SEMAPHORES += [k + str(h) for k in ("ld", "lw", "ny", "nq", "oy", "oq", "sy", "sq") for h in range(2)]
+SEMAPHORES += ["ns%d_%d" % (h, s) for h in range(2) for s in range(N)]
 
 CY = 0.00083
-COST = {"V": 0.0302, "S": 0.0645, "P": 0.0405, "lat": 0.161, "self": 0.0428, "send": 0.8, "net": 2.6, "g": 1.8198, "long": 0.2036}
+COST = {"V": 0.03, "S": 0.065, "P": 0.04, "lat": 0.16, "self": 0.043, "send": 0.6, "g": 1.6, "sc": 3.8, "long": 0.2}
 WIN = 0.0124
 
 
 def build(rank):
-    ops, hist, bank, stg = [], {}, {}, [None]
+    ops, hist, bank, pe, stg = [], {}, {}, {}, [None]
+    peers = [s for s in range(N) if s != rank]
 
-    def add(eng, fn, rd, wr, cost, sem=None, amt=1, dep=(), kind="c", lat=None, n=1):
+    def add(eng, fn, rd, wr, cost, sem=None, amt=1, dep=(), kind="c", lat=None):
         i = len(ops)
         deps = set(dep)
         for acc, w in [(a, False) for a in rd] + [(a, True) for a in wr]:
@@ -52,6 +61,9 @@ def build(rank):
                     st[0] = eng
                 deps.update(st[2])
                 st[1].append(i)
+                if eng == "P":
+                    deps.add(pe.get(nm, i))
+                    pe[nm] = i
                 continue
             keep = []
             for (a, b, j, jw) in hist.setdefault(nm, []):
@@ -63,8 +75,7 @@ def build(rank):
             keep.append((lo, hi, i, w))
             hist[nm] = keep
         deps.discard(i)
-        ops.append({"e": eng, "fn": fn, "d": sorted(deps), "c": cost, "sem": sem, "amt": amt, "k": kind, "lat": lat,
-                    "o": [a[0] for a in wr], "s": stg[0], "n": n})
+        ops.append({"e": eng, "fn": fn, "d": sorted(deps), "c": cost, "sem": sem, "amt": amt, "k": kind, "lat": lat, "s": stg[0]})
         return i
 
     def A(nm, lo=0, hi=None, st=1):
@@ -76,8 +87,9 @@ def build(rank):
     def size(a):
         return (a[2] - a[1] + a[3] - 1) // a[3]
 
-    def vcost(n, f=1.0):
-        return COST["V"] + max(64, n * f) * CY
+    def vcost(out, ins, f=1.0):
+        two = all(SCRATCH[a[0]][2].endswith("16") for a in [out] + ins)
+        return COST["V"] + max(64, size(out) * f * (0.5 if two else 1)) * CY
 
     def arg(T, s):
         return ap(T, s) if isinstance(s, tuple) else s
@@ -90,17 +102,20 @@ def build(rank):
             if o2 is None:
                 return g.vector.tensor_scalar(ap(T, out), ap(T, i0), arg(T, s1), None, o1)
             return g.vector.tensor_scalar(ap(T, out), ap(T, i0), arg(T, s1), arg(T, s2), o1, o2)
-        return add("V", fn, [i0] + cols(s1, s2), [out], vcost(size(out)))
+        return add("V", fn, [i0] + cols(s1, s2), [out], vcost(out, [i0]))
 
     def tt(out, i0, i1, op):
-        f = 1 if (i0[0][0] == "p" or i1[0][0] == "p") else 2
-        return add("V", lambda g, T: g.vector.tensor_tensor(ap(T, out), ap(T, i0), ap(T, i1), op), [i0, i1], [out], vcost(size(out), f))
+        f = 1 if (i0[0][1:].isdigit() or i1[0][1:].isdigit()) else 2
+        return add("V", lambda g, T: g.vector.tensor_tensor(ap(T, out), ap(T, i0), ap(T, i1), op), [i0, i1], [out], vcost(out, [i0, i1], f))
 
     def cp(out, i0):
-        return add("V", lambda g, T: g.vector.tensor_copy(ap(T, out), ap(T, i0)), [i0], [out], vcost(size(out)))
+        return add("V", lambda g, T: g.vector.tensor_copy(ap(T, out), ap(T, i0)), [i0], [out], vcost(out, [i0]))
 
-    def scan(out, d0, d1, o0, o1, f=0.5):
-        return add("V", lambda g, T: g.vector.tensor_tensor_scan(ap(T, out), ap(T, d0), ap(T, d1), 0.0, o0, o1), [d0, d1], [out], vcost(size(out), f))
+    def fill(out, v):
+        return add("V", lambda g, T: g.vector.memset(ap(T, out), v), [], [out], vcost(out, []))
+
+    def scan(out, d0, d1, o0, o1):
+        return add("V", lambda g, T: g.vector.tensor_tensor_scan(ap(T, out), ap(T, d0), ap(T, d1), 0.0, o0, o1), [d0, d1], [out], vcost(out, [d0, d1]))
 
     def act(out, i0, func, bias=None, scale=None, acc=None):
         def fn(g, T):
@@ -112,290 +127,365 @@ def build(rank):
             if acc is not None:
                 kw["accum_out"] = ap(T, acc)
             return g.scalar.activation(ap(T, out), ap(T, i0), func, **kw)
-        return add("S", fn, [i0] + cols(bias, scale), [out] + ([acc] if acc else []), COST["S"] + size(out) * CY)
+        return add("S", fn, [i0] + cols(bias, scale), [out] + ([acc] if acc else []), COST["S"] + size(out) * CY + (0.02 if acc else 0))
 
-    def mm(terms, first=True, last=True, dep=()):
+    def lin(eng, out, i0, scale, bias=None):
+        if eng == "S":
+            return act(out, i0, AF.Copy if bias is None else AF.Identity, bias=bias, scale=scale)
+        return ts(out, i0, scale, None, OP.mult) if bias is None else ts(out, i0, scale, bias, OP.mult, OP.add)
+
+    def mm(terms, first=True, last=True):
         def fn(g, T):
             r = None
             for k, (o, l, x) in enumerate(terms):
                 r = g.tensor.matmul(ap(T, o), ap(T, l), ap(T, x), first and k == 0, last and k == len(terms) - 1)
             return r
-        c = sum(max(64, size(o)) * (4 if l[0] == "wa" else 1) for o, l, x in terms) * 0.0007
-        return add("P", fn, [x for tm in terms for x in tm[1:]], [terms[0][0]], COST["P"] + c, n=len(terms), dep=dep)
-
-    def gath(out, win, off, eng):
-        n = size(out)
-        if eng == "S":
-            return add("S", lambda g, T: g.scalar.activation(ap(T, out), ap(T, win).indirect(ap(T, off)), AF.Copy), [win, off], [out], 0.065 + n * CY * COST["g"])
-        return add("V", lambda g, T: g.vector.tensor_copy(ap(T, out), ap(T, win).indirect(ap(T, off))), [win, off], [out], 0.05 + n * CY * COST["g"])
+        c = sum(max(64, size(o)) * (4 if l[0] == "me" else 1) for o, l, x in terms) * 0.0007
+        return add("P", fn, [x for tm in terms for x in tm[1:]], [terms[0][0]], COST["P"] + c)
 
     def MH(k):
-        return A("mh", 128 * k, 128 * k + 128)
+        i = MH_.index(k)
+        return A("mh", 128 * i, 128 * i + 128)
 
     def MB(k):
-        return A("mb", 128 * k, 128 * k + 128)
+        i = MB_.index(k)
+        return A("mb", 128 * i, 128 * i + 128)
 
-    def DA(k):
-        return A("da", 128 * k, 128 * k + 128)
+    fcn = {}
 
-    def FC(k):
-        return A("fc", k, k + 1)
+    def FC(k, n=1, at=0, w=1):
+        if k not in fcn:
+            fcn[k] = sum(v[1] for v in fcn.values()), n
+        return A("fc", fcn[k][0] + at, fcn[k][0] + at + w)
 
-    def iota(out, pat, base, cm, flag=False):
+    def iota(out, pat, base, cm, dep=()):
         def fn(g, T):
-            if flag:
+            if SCRATCH[out[0]][2] != "int32":
                 return g.iota(ap(T, out), pat, base, cm, allow_small_or_imprecise_dtypes=True)
             return g.iota(ap(T, out), pat, base, cm)
-        return add("G", fn, [], [out], 0.13 + 2 * size(out) * CY)
+        return add("G", fn, [], [out], 0.13 + 2 * size(out) * CY, dep=dep)
 
-    def dma(dst, src, rd, wr, sem, lat):
-        return add("Y", lambda g, T: g.sync.dma_start(dst(T), src(T)), rd, wr, 0.1, sem=sem, amt=16, kind="dma", lat=lat)
+    def dma(dst, src, rd, wr, sem, lat, dep=(), eng="Y"):
+        q = (lambda g: g.sync) if eng == "Y" else (lambda g: g.scalar)
+        return add(eng, lambda g, T: q(g).dma_start(dst(T), src(T)), rd, wr, 0.1, sem=sem, amt=16, kind="dma", lat=lat, dep=dep)
 
-    def send(mate, dst, src, here, sem, net, dep=()):
-        i = add("G", (mate, dst, src, sem), [src], [], COST["send"], dep=dep, kind="send")
-        add("N", None, [], [here], 0.0, sem=sem, amt=NE, dep=(i,), kind="net", lat=net)
-        return i
+    def send(dst, src, rd, sem, dep=()):
+        return add("G", (dst, src, sem), rd, [], COST["send"], dep=dep, kind="send")
 
-    def send_shelf(r, cuts, net, dep=()):
-        for h, (a, b) in enumerate(cuts):
-            far = A("sh%d" % (r + 1), a, b)
-            send(rank ^ ROUNDS[r], far, A("sh", a, b), far, "s%d_%d" % (r, a // 1024), net + 3 * h, dep)
+    def landed(i, senders, wr, sem, net):
+        return add("N", senders, [], wr, 0.0, sem=sem, dep=(i,), kind="net", lat=net)
 
-    dma(lambda T: T.uin[:], lambda T: T.units[:], [], [A("uin")], "ldu", 2.5)
-    for h in range(4):
-        a, b = 1024 * h, 1024 * h + 1024
-        dma(lambda T, a=a, b=b: T.sh[:, a:b], lambda T, a=a, b=b: T.shelf[:, a:b], [], [A("sh", a, b)], "lds%d" % h, 3.5 + 1.5 * h)
+    def rows(g):
+        return slice(16 * g, 16 * g + 16)
+
+    stg[0] = -9
+    dma(lambda T: T.uin[:], lambda T: T.units[:], [], [A("uin")], "ldu", 2.0)
+    mine = A("ul", 256 * rank, 256 * rank + 256)
+    ts(mine, A("uin"), -2048.0, None, OP.add)
+    iu_ = send(lambda T, j: ap(T, mine), lambda T, j: ap(T, mine), [mine], lambda j: "nu")
+    landed(iu_, peers, [A("ul", 256 * s, 256 * s + 256) for s in peers], "nu", 3.5)
+    last_send = iu_
+    for h in range(2):
+        stg[0] = -8 + 2 * h
+        st = [dma(lambda T, a=a, b=b: T.sd[a:b], lambda T, a=a, b=b: T.shelf[16 * a:16 * b, :], [], [], "ld%d" % h, 2.6 + h)
+              for a, b in ((4 * h, 4 * h + rank), (4 * h + rank + 1, 4 * h + 4)) if a < b]
+        for b in range(2):
+            o = 4 * b + rank
+            dma(lambda T, o=o, h=h: T["w%d" % h][rows(o), :], lambda T, h=h: T.shelf[rows(4 * h + rank), :], [], [("W%d" % h, o, o + 1)], "lw%d" % h, 2.6 + h)
+        last_send = send(lambda T, j, h=h: T.sl[4 * h + rank], lambda T, j, h=h: T.sd[4 * h + j], [], lambda j, h=h: "ns%d_%d" % (h, rank),
+                         dep=st + [last_send])
+        stg[0] = -4 + h
+        for s in sorted(peers, key=lambda s: s ^ rank != 2):
+            i = landed(last_send, [s], [], "ns%d_%d" % (h, s), (3.0 if s ^ rank == 2 else 5.0) + 2 * h)
+            for b in range(2):
+                o = 4 * b + s
+                dma(lambda T, o=o, h=h: T["w%d" % h][rows(o), :], lambda T, h=h, s=s: T.sl[4 * h + s], [], [("W%d" % h, o, o + 1)], "lw%d" % h, 2.2, dep=(i,))
+    stg[0] = None
     iota(A("ip"), [[1, 1]], 0, 1)
-    iota(A("im"), [[1, 128]], 0, 0)
-    iota(A("jj"), [[0, 64], [1, 16]], 0, 0)
-    iota(A("tie"), [[-1, 256]], 255, 0, True)
-    send_shelf(0, [(0, 1024), (1024, 2048), (2048, 3072)], 8.0)
-    cp(FC(0), A("ip"))
-    ts(A("ii", 0, 1), A("ip"), 4, None, OP.arith_shift_right)
-    cp(FC(1), A("ii", 0, 1))
-    ts(A("ii", 1, 2), A("ip"), 15, None, OP.bitwise_and)
-    cp(FC(2), A("ii", 1, 2))
-    ts(A("mg"), A("im"), 4, None, OP.arith_shift_right)
-    ts(A("bf"), A("mg"), FC(1), None, OP.is_equal)
-    ts(A("gef"), A("im"), FC(0), None, OP.is_ge)
-    tt(A("trif"), A("bf"), A("gef"), OP.mult)
-    ts(A("idf"), A("im"), FC(0), None, OP.is_equal)
-    ts(MH(0), A("trif"), 1.0, None, OP.mult)
-    ts(MH(1), A("idf"), 32.0, None, OP.mult)
-    ts(MH(2), A("idf"), 1.0, None, OP.mult)
-    ts(A("half"), A("im", 0, 8), 0.0, 0.5, OP.mult, OP.add)
-    ts(A("one"), A("im"), 0.0, 1.0, OP.mult, OP.add)
-    ts(DA(0), A("idf"), -2048.0, None, OP.mult)
-    for k, src, f in ((0, "idf", -4096.0), (1, "idf", -8388608.0 + 65536.0), (6, "bf", 1.0), (7, "bf", -1.0), (8, "bf", 256.0),
-                      (9, "bf", -256.0), (10, "bf", 4096.0), (11, "bf", -4096.0), (12, "idf", 1.0)):
-        act(MB(k), A(src), AF.Copy, scale=f)
-    add("V", lambda g, T: g.vector.memset(T.ones[:], 1.0), [], [A("ones")], vcost(128))
-    add("V", lambda g, T: g.vector.memset(T.mhalf[:], -0.5), [], [A("mhalf")], vcost(64))
-    ts(A("rm"), A("jj"), 0, None, OP.is_gt)
-    ts(A("bg"), A("jj"), 0, 256.0, OP.is_equal, OP.mult)
-    ts(A("dm"), A("jj", 0, 64), FC(2), None, OP.is_equal)
-    for t in range(4):
-        ts(A("ii", 2 + t, 3 + t), A("ip"), 8 >> t, None, OP.bitwise_and)
-        ts(FC(3 + t), A("ii", 2 + t, 3 + t), 0, None, OP.is_equal)
-        ts(FC(7 + t), FC(3 + t), -16384.0, 8192.0, OP.mult, OP.add)
-        ts(FC(11 + t), FC(3 + t), 65536.0, -8388608.0 + 65536.0, OP.mult, OP.add)
-        ts(FC(15 + t), FC(3 + t), -1.0, None, OP.mult)
-        ts(MH(3 + t), A("trif"), FC(3 + t), None, OP.mult)
-        ts(MH(7 + t), A("trif"), FC(15 + t), None, OP.mult)
-        ts(MH(11 + t), A("idf"), FC(3 + t), 32.0, OP.mult, OP.mult)
-        ts(MH(15 + t), A("idf"), FC(3 + t), -32.0, OP.mult, OP.mult)
-        act(MB(2 + t), A("idf"), AF.Copy, scale=FC(11 + t))
-    ts(A("wa"), A("bf"), FC(2), 0.5, OP.mult, OP.mult)
-    h1 = A("half", 0, 1)
+    iota(A("iu"), [[1, 256]], 0, 0)
+    iota(A("mg"), [[1, 8], [0, 16]], 0, 0)
+    iota(A("jj", 0, 128), [[0, 8], [256, 16]], 0, 0)
+    iota(A("ms"), [[0, 2], [1, 4], [0, 16]], 0, 0, dep=(last_send,))
+    iota(A("m64"), [[0, 2], [1, 64]], 0, 0, dep=(last_send,))
+    n = 128
+    while n < SL:
+        cp(A("jj", n, 2 * n), A("jj", 0, n))
+        n *= 2
+    ts(A("jn"), A("jj"), -1.0, 256.0, OP.mult, OP.add)
+    im = A("iu", 0, 128)
+    pf, kf, pg = FC("p"), FC("k"), FC("pg")
+    cp(pf, A("ip"))
+    ts(A("ii", 7, 8), A("ip"), 15, None, OP.bitwise_and)
+    cp(kf, A("ii", 7, 8))
+    ts(pg, pf, kf, 1.0 / 16, OP.subtract, OP.mult)
+    for i in range(7):
+        ts(A("ii", i, i + 1), A("ip"), 1 << i, None, OP.bitwise_and)
+    bits = FC("bit", 7, 0, 7)
+    ts(bits, A("ii", 0, 7), 0, None, OP.is_gt)
+    for nm, a, b in (("lam", 2.0, -1.0), ("nl", -2.0, 1.0), ("L", -1.0, 1.0), ("hl", 1.0, -0.5), ("nb", -1.0, 0.0), ("b255", 255.0, 0.0)):
+        ts(FC(nm, 7, 0, 7), bits, a, b, OP.mult, OP.add)
 
-    def pcol(k):
-        return A("p7", 500 + k, 501 + k)
-    mm([(pcol(0), MH(0), h1)])
-    ts(A("bs", 0, 1), pcol(0), 4096.0, 788480.0, OP.mult, OP.add)
-    ts(A("bt", 0, 1), A("bs", 0, 1), P2, -4095.0 / 8192, OP.mult, OP.add)
-    for t in range(4):
-        mm([(pcol(1 + t), MH(0), h1), (pcol(1 + t), MH(3 + t), h1)])
-    ts(A("bs", 1, 5), A("p7", 501, 505), 4096.0, 788480.0, OP.mult, OP.add)
-    ts(A("bt", 1, 5), A("bs", 1, 5), P2, -4095.0 / 8192, OP.mult, OP.add)
-    ts(A("xc"), A("uin"), -2048.0, None, OP.add)
-    a0 = 264 if rank < (rank ^ ROUNDS[0]) else 7
-    ts(A("vs", a0, a0 + 1), A("ip"), 0.0, -2048.0, OP.mult, OP.add)
+    def bit(nm, i):
+        return FC(nm, 7, i)
+    ts(FC("k256"), kf, 256.0, None, OP.mult)
+    ts(FC("k113"), kf, 113.0, None, OP.add)
+    ts(FC("k16"), kf, 1.0 / 16, None, OP.mult)
+    for h in range(2):
+        ts(FC("zc%d" % h), pg, float(4 * h + rank), FC("k113"), OP.is_equal, OP.mult)
+        ts(A("z", 256 * h, 256 * h + 256), A("iu"), FC("zc%d" % h), None, OP.is_equal)
+    ts(FC("bs0"), kf, 2048.0, 2048.0 + 786432.0, OP.mult, OP.add)
+    ts(FC("bt0"), FC("bs0"), P2, -4095.0 / 8192, OP.mult, OP.add)
+    ts(FC("bsA"), FC("bs0"), -5760.0, None, OP.add)
+    ts(FC("btA"), FC("bsA"), P2, -4095.0 / 8192, OP.mult, OP.add)
+    ts(MB("B"), A("mg"), pg, None, OP.is_equal)
+    ts(MB("KLE"), A("jj", 0, 128), FC("k256"), None, OP.is_ge)
+    tt(MH("T"), MB("B"), MB("KLE"), OP.mult)
 
-    def columns(c, lo, hi, k, pre, late, xpt):
-        n = hi - lo
-        x, w, xp = A("p%d" % (2 * c), 0, n), A("p%d" % (2 * c + 1), 0, n), A("p%d" % (2 * c), 384, 384 + n)
-        tb = A("tb", lo, hi)
-        i = mm(pre(x), last=not late(x))
-        if late(x):
-            i = mm(late(x), first=False, dep=(i,))
-        i = mm(pre(w) + late(w), last=False, dep=(i,))
-        ts(tb, x, P2, A("bt", k, k + 1), OP.mult, OP.add)
-        mm([(w, MB(0), tb)], first=False, dep=(i,))
-        mm(xpt(xp))
-        act(A("sq", lo, hi), w, AF.Square, bias=A("bs", k, k + 1))
-        tt(A("yb", lo, hi), A("sq", lo, hi), xp, OP.add)
-        ts(A("cb", lo, hi), A("yb", lo, hi), 5, 4095, OP.arith_shift_right, OP.bitwise_and)
-        cp(A("c16", lo, hi), A("cb", lo, hi))
-
-    def gather_scan(parts):
-        for (a, b, win) in parts:
-            gath(A("gb", 16 * a, 16 * b), A(win), A("c16", a, b), "S")
-        for (a, b, win) in parts:
-            m = 16 * (b - a)
-            scan(A("mx", 16 * a, 16 * b), A("rm", 0, m), A("gb", 16 * a, 16 * b), OP.mult, OP.max)
-            scan(A("mn", 16 * a, 16 * b), A("bg", 0, m), A("gb", 16 * a, 16 * b), OP.max, OP.min)
-
-    def ends(nm, a, b):
-        return A(nm, 16 * a + 15, 16 * b, 16)
-
+    def diag(out, at, f):
+        ts(out, im, at, f, OP.is_equal, OP.mult)
+    for nm, f in (("I", 1.0), ("nI", -1.0), ("I32", 32.0)):
+        diag(MH(nm), pf, f)
+    for nm, f in (("n4096", -4096.0), ("cst", 65536.0 - 8388608.0), ("V+", 8192.0)):
+        diag(MB(nm), pf, f)
+    lin(PAR["mat"], MB("V-"), MB("V+"), -1.0)
+    for i in (4, 5):
+        diag(MB("D%d" % i), pf, bit("lam", i))
+    lin(PAR["mat"], MB("Ko+"), MB("B"), 256.0)
+    lin(PAR["mat"], MB("Ko-"), MB("B"), -256.0)
+    ts(FC("s"), bit("bit", 6), -4.0, pg, OP.mult, OP.add)
+    ts(FC("p64", 2), bit("bit", 6), -64.0, pf, OP.mult, OP.add)
+    ts(FC("p64", 2, 1), FC("p64", 2), 64.0, None, OP.add)
+    ts(FC("b128"), bit("bit", 6), 128.0, None, OP.mult)
+    ts(A("uo"), im, FC("b128"), None, OP.add)
+    for b, nm in ((0, "L"), (1, "bit")):
+        ts(FC("h256", 2, b), bit(nm, 6), 256.0, None, OP.mult)
+        ts(MB("K%d+" % b), A("ms"), FC("s"), FC("h256", 2, b), OP.is_equal, OP.mult)
+        lin(PAR["mat"], MB("K%d-" % b), MB("K%d+" % b), -1.0)
+        ts(MH("R%d" % b), A("m64"), FC("p64", 2), bit(nm, 6), OP.is_equal, OP.mult)
+        ts(A("me", 128 * b, 128 * b + 128), im, FC("p64", 2, b), None, OP.is_equal)
+    for t in (1, 2, 3):
+        ts(MH("TL%d" % t), MH("T"), bit("L", 3 - t), None, OP.mult)
+        ts(MH("IL%d" % t), MH("I32"), bit("L", 3 - t), None, OP.mult)
+    fill(A("ones"), 1.0)
+    fill(A("mhalf"), -0.5)
+    ts(A("rm"), A("jj", 0, 64), 0.0, None, OP.is_gt)
+    ts(A("dm"), A("jj", 0, 64), FC("k256"), None, OP.is_equal)
     for r, m in enumerate(ROUNDS):
-        mate = rank ^ m
-        low = rank < mate
-        for c, (lo, hi) in enumerate(BCH):
-            n = hi - lo
-            stg[0] = 1000 * r + c
-            xs = A("xc", lo, hi)
-            columns(c, lo, hi, 0, lambda x: [(x, MH(0), xs), (x, DA(r), A("one", 0, n))], lambda x: [],
-                    lambda x: [(x, MH(1), xs), (x, MB(1), A("ones", 0, n))])
-            st = n // SUBS // 2 * 2
-            cut = [lo + s * st for s in range(SUBS)] + [hi]
-            gather_scan([(cut[s], cut[s + 1], "sh") for s in range(SUBS)])
-            mx, mn = ends("mx", lo, hi), ends("mn", lo, hi)
-            kp, vp = A("p%d" % (2 * c + 1), 128, 128 + n), A("p%d" % (2 * c + 1), 256, 256 + n)
-            mm([(kp, MB(8 if low else 9), mx), (kp, MB(9 if low else 8), mn), (kp, MB(12), A("tie", lo, hi))])
-            mm([(vp, MB(10), mx), (vp, MB(11), mn), (vp, MH(2), xs)])
-            tt(A("kd", lo, hi), kp, A("dm", 0, n), OP.mult)
-            cp(A("ksb", lo, hi), kp)
-            scan(A("kc", lo, hi), A("rm", 0, n), A("kd", lo, hi), OP.mult, OP.add, 1)
-            ts(A("vu", lo, hi), vp, 2048.0, None, OP.add)
-        stg[0] = 1000 * r + 20
-        for j in range(16):
-            kcol = A("kc", 16 * j + 15, 16 * j + 16)
-            if j < NS:
-                act(A("trash", 256 * (j % 4), 256 * (j % 4) + 256), A("ksb"), AF.Sign, bias=kcol, scale=-1.0, acc=A("acc", j, j + 1))
-            else:
-                ts(A("cmp", 256 * j, 256 * j + 256), A("ksb"), kcol, None, OP.is_gt)
-                scan(A("cs", 256 * j, 256 * j + 256), A("ones"), A("cmp", 256 * j, 256 * j + 256), OP.mult, OP.add)
-        ts(A("rl", 16 * r + NS, 16 * r + 16), A("cs", 256 * NS + 255, 4096, 256), 1.0, None, OP.mult)
-        ts(A("rl", 16 * r, 16 * r + NS), A("acc", 0, NS), -0.5, 127.5, OP.mult, OP.add)
-        rl = A("rl", 16 * r, 16 * r + 16)
-        v0 = 272 * r + 8
-        vw = A("vs", v0, v0 + 256)
-        add("V", lambda g, T, vw=vw, rl=rl: g.vector.tensor_copy(ap(T, vw).indirect(ap(T, rl)), T.vu[:]), [rl, A("vu")], [vw], 0.05 + 256 * CY * 3)
-        mine = v0 + (0 if low else 128)
-        f0 = 144 * r
-        x0 = f0 + (1 if low else 0)
-        far = A("vf", f0, f0 + 129)
-        iv = send(mate, far, A("vs", v0 + 128, v0 + 257) if low else A("vs", v0 - 1, v0 + 128), far, "v%d" % r, COST["net"])
-        mv, fv = A("vs", mine, mine + 128), A("vf", x0, x0 + 128)
-        stg[0] = 1000 * r + 21
-        if r == 0:
-            send_shelf(0, [(3072, 4096)], 6.0, (iv,))
+        pp, hb = FC("pp%d" % r), (5 if m & 2 else 4)
+        if m & 1:
+            ts(pp, bit("nl", 4), 16.0, pf, OP.mult, OP.add)
+        if m & 2:
+            ts(pp, bit("nl", 5), 32.0, pp if m & 1 else pf, OP.mult, OP.add)
+        diag(MH("Pm%d" % r), pp, 1.0)
+        c1, c2, cid, cid4 = (FC("%s%d" % (k, r)) for k in ("c1", "c2", "id", "id4"))
+        ts(c1, pp, pf, bit("L", 3), OP.subtract, OP.mult)
+        ts(c1, c1, pf, None, OP.add)
+        diag(MH("S1%d" % r), c1, 32.0)
+        ts(c2, c1, kf, 1.0 / 16, OP.subtract, OP.mult)
+        ts(MB("tmp"), A("mg"), c2, None, OP.is_equal)
+        tt(MH("T1%d" % r), MB("tmp"), MB("KLE"), OP.mult)
+        ts(cid, pp, pf, kf, OP.min, OP.subtract)
+        ids = A("ids", 128 * r, 128 * r + 128)
+        for k in range(4):
+            v = [16 * min(x, x ^ m) for x in (2 * k, 2 * k + 1)]
+            iota(A("ids", 128 * r + 32 * k, 128 * r + 32 * k + 32), [[v[1] - v[0], 2], [0, 16]], v[0], 0, dep=(last_send,))
+        ts(MB("Q%d+" % r), ids, cid, bit("nl", hb), OP.is_equal, OP.mult)
+        lin(PAR["mat"], MB("Q%d-" % r), MB("Q%d+" % r), -1.0)
         if r < 2:
-            send_shelf(r + 1, [(0, 4096)], 16.0, (len(ops) - 2,))
-        for c, (a, b) in enumerate(TCH):
-            n = b - a
-            stg[0] = 1000 * r + 100 + c
-            L, H = A("oi", 2 * a, 2 * a + n), A("oi", 2 * a + n, 2 * b)
-            cL, cH = A("oc", 2 * a, 2 * a + n), A("oc", 2 * a + n, 2 * b)
-            ow, fr = (L, H) if low else (H, L)
-            cow, cfr = (cL, cH) if low else (cH, cL)
-            ts(ow, A("vs", mine + a, mine + b), 4095, None, OP.bitwise_and)
-            ts(cow, ow, -2048.0, None, OP.add)
-            ts(fr, A("vf", x0 + a, x0 + b), 4095, None, OP.bitwise_and)
-            ts(cfr, fr, -2048.0, None, OP.add)
-            d = A("d", a, b)
-            tt(d, H, L, OP.subtract)
-            ts(d, d, 4095, None, OP.bitwise_and)
-            ts(A("rr", a, b), d, -2048.0, None, OP.add)
-        stg[0] = 1000 * r + 100
-        ac = A("ac", 4 * r + 2, 4 * r + 3)
-        fa = f0 if low else f0 + 128
-        cp(ac, A("vf", fa, fa + 1))
-        ts(DA(3 + r), A("idf"), ac, None, OP.mult)
-        stg[0] = 1000 * r + 103
-        ts(A("qo"), mv, 12, None, OP.arith_shift_right)
-        ts(A("qf"), fv, 12, None, OP.arith_shift_right)
-        qL, qH = (A("qo"), A("qf")) if low else (A("qf"), A("qo"))
-        tt(A("s0"), qL, qH, OP.is_gt)
-        ts(A("s0"), A("s0"), 2.0, -1.0, OP.mult, OP.add)
-        for t in range(4):
-            stg[0] = 1000 * r + 103 + 4 * t
-            ts(A("sg", 128 * t, 128 * t + 128), A("s0"), FC(7 + t), None, OP.mult)
-        tt(A("tl", 0, 128), qL, qH, OP.is_lt)
-        ts(A("tl", 128, 256), A("tl", 0, 128), -1.0, None, OP.add)
-        if r == 2:
-            ts(A("qi"), A("vu"), 12, None, OP.arith_shift_right)
-            cp(A("qy"), A("qi"))
-            dma(lambda T: T.yq[:], lambda T: T.qy[0:128:16, :], [A("qy")], [], "styq", 2.0)
-        dL, dH = (DA(r), DA(3 + r)) if low else (DA(3 + r), DA(r))
-        wL, wH = ("sh", "sh%d" % (r + 1)) if low else ("sh%d" % (r + 1), "sh")
-        for t in range(4):
-            for c, (a, b) in enumerate(TCH):
-                n = b - a
-                lo, mid, hi = 2 * a, 2 * a + n, 2 * b
-                stg[0] = 1000 * r + 100 + 4 * t + c
-                R, oc, one = A("rr", a, b), A("oc", lo, hi), A("one", 0, n)
+            ts(cid4, bit("bit", 6), -64.0, cid, OP.mult, OP.add)
+            cp(A("ids", 384 + 128 * r, 448 + 128 * r), A("ids", 128 * r, 128 * r + 64))
+            cp(A("ids", 448 + 128 * r, 512 + 128 * r), A("ids", 128 * r, 128 * r + 64))
+            ts(MH("W%d" % r), A("ids", 384 + 128 * r, 512 + 128 * r), cid4, FC("k16"), OP.is_equal, OP.mult)
+    for k in range(6):
+        iota(A("vs", 256 * k, 256 * k + 256), [[0, 256]], 0, 0, dep=(last_send,))
 
-                def lh(x):
-                    return (x[0], x[1], x[1] + n, 1), (x[0], x[1] + n, x[1] + 2 * n, 1)
-                columns(c, lo, hi, 1 + t,
-                        lambda x: [(x, MH(0), oc), (lh(x)[0], dL, one), (lh(x)[1], dH, one)],
-                        lambda x: [(lh(x)[0], MH(3 + t), R), (lh(x)[1], MH(7 + t), R)],
-                        lambda x: [(x, MH(1), oc), (x, MB(2 + t), A("ones", 0, 2 * n)), (lh(x)[0], MH(11 + t), R), (lh(x)[1], MH(15 + t), R)])
-                gather_scan([(lo, mid, wL), (mid, hi, wH)])
-                q = A("p%d" % (2 * c + 1), 128, 128 + n)
-                i = mm([(q, MB(12), A("mhalf", 0, n)), (q, MB(6), ends("mx", lo, mid)), (q, MB(7), ends("mn", lo, mid))], last=False)
-                mm([(q, MB(7), ends("mx", mid, hi)), (q, MB(6), ends("mn", mid, hi))], first=False, dep=(i,))
-                stg[0] += 4
-                u, e = A("u", a, b), A("e", a, b)
-                tt(u, q, A("sg", 128 * t + a, 128 * t + b), OP.mult)
-                tt(e, A("d" if t == 0 else "e", a, b), u, OP.min)
-                if t < 3:
-                    ts(R, e, 0.0, -2048.0, OP.max, OP.add)
-                    continue
+    def stream(h):
+        o = 128 * h
+
+        def S(nm, lo=0, hi=128):
+            return A(nm, o + lo, o + hi)
+
+        def X(c, lo, n):
+            return A("p%d" % (4 * h + 2 * c), lo, lo + n)
+
+        def Wb(c, lo, n):
+            return A("p%d" % (4 * h + 2 * c + 1), lo, lo + n)
+
+        def stage(step, c=0):
+            stg[0] = step + PAR["off"] * h + PAR["coff"] * c
+
+        def columns(c, lo, hi, bs, bt, pre, late, xpt):
+            n = hi - lo
+            x, w, xp = X(c, 0, n), Wb(c, 0, n), X(c, 64, n)
+            tb = S("tb", lo, hi)
+            mm([(x,) + a for a in pre], last=not late)
+            if late:
+                mm([(x,) + a for a in late], first=False)
+            mm([(w,) + a for a in pre + late], last=False)
+            lin(PAR["tb"], tb, x, P2, bt)
+            mm([(w, MB("n4096"), tb)], first=False)
+            mm([(xp,) + a for a in xpt] + [(xp, MB("cst"), A("ones", 0, n))])
+            act(S("sq", lo, hi), w, AF.Square, bias=bs)
+            tt(S("yb", lo, hi), S("sq", lo, hi), xp, OP.add)
+            ts(S("cb", lo, hi), S("yb", lo, hi), 5, 4095, OP.arith_shift_right, OP.bitwise_and)
+            cp(S("c16", lo, hi), S("cb", lo, hi))
+
+        def gather_scan(lo, hi):
+            st = (hi - lo) // PAR["subs"] // 2 * 2
+            cut = [lo + s * st for s in range(PAR["subs"])] + [hi]
+            parts = [(o + a, o + b) for a, b in zip(cut, cut[1:])]
+            for (a, b) in parts:
+                out, off = A("gb", 16 * a, 16 * b), A("c16", a, b)
+                add("S", lambda g, T, out=out, off=off: g.scalar.activation(ap(T, out), T["w%d" % h][:, 0:4096].indirect(ap(T, off)), AF.Copy),
+                    [("W%d" % h, 0, 8), off], [out], 0.065 + size(out) * CY * COST["g"])
+            for (a, b) in parts:
+                m = 16 * (b - a)
+                scan(A("mx", 16 * a, 16 * b), A("jj", 0, m), A("gb", 16 * a, 16 * b), OP.min, OP.max)
+                scan(A("mn", 16 * a, 16 * b), A("jn", 0, m), A("gb", 16 * a, 16 * b), OP.max, OP.min)
+            return A("mx", 16 * (o + lo) + 15, 16 * (o + hi), 16), A("mn", 16 * (o + lo) + 15, 16 * (o + hi), 16)
+
+        def home(kind, tile):
+            g_ = 4 * h + rank
+            land = kind + "l"
+            i = send(lambda T, j: T[land][g_], lambda T, j: ap(T, tile), [tile], lambda j: "n%s%d" % (kind, h))
+            got = (landed(i, peers, [], "n%s%d" % (kind, h), 2.6),
+                   dma(lambda T: T[land][g_], lambda T: ap(T, tile), [tile], [], "o%s%d" % (kind, h), 2.0))
+            for b in range(2):
+                a, r0 = 128 * b, 64 * b + 16 * rank
+                if kind == "y":
+                    dma(lambda T, a=a: T.yu[64 * h:64 * h + 64, a:a + 128], lambda T, r0=r0: T.yl[4 * h:4 * h + 4, r0:r0 + 16, :], [], [], "sy%d" % h, 2.0, dep=got)
+                else:
+                    dma(lambda T, a=a: T.yq[4 * h:4 * h + 4, a:a + 128], lambda T, r0=r0: T.ql[4 * h:4 * h + 4, r0, :], [], [], "sq%d" % h, 2.0, dep=got)
+
+        for c, (lo, hi) in enumerate(CH):
+            stage(0, c)
+            n = hi - lo
+            pu = X(c, 448, n)
+            mm([(pu, A("z", 256 * h + 113 - 16 * (4 * b + s), 256 * h + 241 - 16 * (4 * b + s)), A("ul", 256 * s + 128 * b + lo, 256 * s + 128 * b + hi))
+                for s in range(N) for b in range(2)])
+            cp(S("xc", lo, hi), pu)
+        bs, bt = FC("bs0"), FC("bt0")
+        ns = PAR["ns"]
+        for r, m in enumerate(ROUNDS):
+            hb = 5 if m & 2 else 4
+            D = MB("D%d" % hb)
+            for c, (lo, hi) in enumerate(CH):
+                n = hi - lo
+                stage(6 * r, c)
+                xs = S("xc", lo, hi)
+                columns(c, lo, hi, bs, bt, [(MH("T"), xs)], [], [(MH("I32"), xs)])
+            for c, (lo, hi) in enumerate(CH):
+                n = hi - lo
+                stage(6 * r, c)
+                xs = S("xc", lo, hi)
+                mx, mn = gather_scan(lo, hi)
+                kp, vp = Wb(c, 128, n), Wb(c, 192, n)
+                mm([(kp, D, A("uo", lo, hi)), (kp, MB("Ko+"), mx), (kp, MB("Ko-"), mn)])
+                mm([(vp, MH("I"), xs), (vp, MB("V+"), mx), (vp, MB("V-"), mn)])
+                for cc in ([0] if ns == 8 else [1] if ns == 0 else [0, 1]):
+                    for b in range(2):
+                        kt = X(cc, 128 + 128 * b + lo, n)
+                        mm([(kt, D, A("iu", 128 * b + lo, 128 * b + hi)), (kt, MB("K%d+" % b), mx), (kt, MB("K%d-" % b), mn)])
+                tt(S("kd", lo, hi), kp, A("dm", 0, n), OP.mult)
+                scan(S("kc", lo, hi), A("rm", 0, n), S("kd", lo, hi), OP.mult, OP.add)
+                lin(PAR["vu"], S("vu", lo, hi), vp, 1.0)
+                if r == 2:
+                    stage(6 * r + 1.5, c)
+                    qp = Wb(c, 448, n)
+                    mm([(qp, MB("Ko+"), mx), (qp, MB("Ko-"), mn)])
+                    lin(PAR["qy"], S("qy", lo, hi), qp, 1.0 / 256)
+            if r == 2:
+                home("q", S("qy"))
+            stage(6 * r + 1)
+            r0 = 16 * r + 8 * h
+            for j in range(8):
+                kcol = S("kc", 16 * j + 15, 16 * j + 16)
+                if j < ns:
+                    act(A("trash", 256 * (2 * h + j % 2), 256 * (2 * h + j % 2) + 256), X(0, 128, 256), AF.Sign, bias=kcol, scale=-1.0, acc=A("acc", 8 * h + j, 8 * h + j + 1))
+                else:
+                    k = 256 * (8 * h + j)
+                    ts(A("cmp", k, k + 256), X(1, 128, 256), kcol, None, OP.is_gt)
+                    scan(A("cs", k, k + 256), A("ones"), A("cmp", k, k + 256), OP.mult, OP.add)
+            if ns < 8:
+                ts(A("rl", r0 + ns, r0 + 8), A("cs", 256 * (8 * h + ns) + 255, 256 * (8 * h + 8), 256), bit("nl", hb), bit("b255", hb), OP.mult, OP.add)
+            if ns:
+                ts(A("rl", r0, r0 + ns), A("acc", 8 * h, 8 * h + ns), bit("hl", hb), 127.5, OP.mult, OP.add)
+            rl = A("rl", r0, r0 + 8)
+            v0 = 256 * (2 * r + h)
+            vw = A("vs", v0, v0 + 256)
+            add("V", lambda g, T, vw=vw, rl=rl: g.vector.tensor_copy(ap(T, vw).indirect(ap(T, rl)), ap(T, S("vu"))), [rl, S("vu")], [vw], 0.05 + 128 * CY * COST["sc"])
+            for t in range(4):
+                for c, (lo, hi) in enumerate(CH):
+                    n = hi - lo
+                    stage(6 * r + 2 + t, c)
+                    oc, R = S("oc", lo, hi), S("rr", lo, hi)
+                    if t == 0:
+                        vm, t8 = Wb(c, 256, n), S("t8", lo, hi)
+                        mm([(vm, A("me", 128 * b, 128 * b + 128), A("vs", v0 + 2 * lo + b * n, v0 + 2 * lo + b * n + n)) for b in range(2)])
+                        ts(t8, vm, 1.5 * 2.0 ** 36, 1.5 * 2.0 ** 36, OP.add, OP.subtract)
+                        tt(oc, vm, t8, OP.subtract)
+                        columns(c, lo, hi, bs, bt, [(MH("T1%d" % r), oc)], [], [(MH("S1%d" % r), oc)])
+                        stage(6 * r + 2.9, c)
+                        dl, qd, w4 = Wb(c, 320, n), Wb(c, 384, n), S("w4", lo, hi)
+                        mm([(dl, MH("Pm%d" % r), oc), (dl, MH("nI"), oc)])
+                        mm([(qd, MB("Q%d+" % r), t8)])
+                        ts(w4, dl, 1.5 * 2.0 ** 35, 1.5 * 2.0 ** 35, OP.add, OP.subtract)
+                        tt(R, dl, w4, OP.subtract)
+                        ts(S("tau", lo, hi), qd, bit("lam", hb), bit("nb", hb), OP.mult, OP.is_gt)
+                        if PAR["sig"] == "S":
+                            act(S("sg", lo, hi), qd, AF.Sign, bias=FC("mh"))
+                        else:
+                            ts(S("sg", lo, hi), qd, 0.0, 0.5, OP.is_gt, OP.subtract)
+                        stage(6 * r + 2, c)
+                    else:
+                        columns(c, lo, hi, bs, bt, [(MH("T"), oc)], [(MH("TL%d" % t), R)], [(MH("I32"), oc), (MH("IL%d" % t), R)])
+                    if t == 3:
+                        tt(S("rt", lo, hi), R, S("tau", lo, hi), OP.mult)
+                    mx, mn = gather_scan(lo, hi)
+                    q = Wb(c, 64, n)
+                    mm([(q, MH("I"), A("mhalf", 0, n)), (q, MB("Q%d+" % r), mx)], last=False)
+                    mm([(q, MB("Q%d-" % r), mn)], first=False)
+                    stage(6 * r + 3 + t, c)
+                    u, k = S("u", lo, hi), A("kk", 256 * t + o + lo, 256 * t + o + hi)
+                    tt(u, q, S("sg", lo, hi), OP.mult)
+                    ts(k, u, bit("lam", 3 - t), 0.0, OP.mult, OP.is_gt)
+                    if t < 3:
+                        tt(R, R, k, OP.mult)
+                        continue
+                    rf = S("rf", lo, hi)
+                    tt(rf, S("rt", lo, hi), k, OP.mult)
+                    for b in range(2):
+                        pn = X(c, 128 + b * n, n)
+                        mm([(pn, MH("R%d" % b), oc), (pn, MH("R%d" % b), rf)])
+                    lin(PAR["nw"], A("nw", 2 * o + 2 * lo, 2 * o + 2 * hi), X(c, 128, 2 * n), 1.0)
+            stage(6 * r + 6)
+            if r < 2:
+                n = CH[0][1]
+                pa = X(0, 384, n)
+                terms = [(pa, MH("W%d" % r), A("kk", 256 * t + o + lo, 256 * t + o + hi)) for t in range(4) for lo, hi in CH]
+                mm(terms[:-1], last=False)
+                mm(terms[-1:], first=False)
+                red = A("red", 2 * r + h, 2 * r + h + 1)
+                add("V", lambda g, T, red=red, pa=pa: g.vector.tensor_reduce(ap(T, red), ap(T, pa), AX.X, OP.add), [pa], [red], COST["V"] + n * CY)
+                bs, bt = A("bias", 4 * r + 2 * h, 4 * r + 2 * h + 1), A("bias", 4 * r + 2 * h + 1, 4 * r + 2 * h + 2)
+                ts(bt, red, P2, FC("btA"), OP.mult, OP.add)
+                ts(bs, red, FC("bsA"), None, OP.add)
+            nw = A("nw", 2 * o, 2 * o + 256)
+            for c, (lo, hi) in enumerate(CH):
+                stage(6 * r + 6, c)
+                ni, rc = S("ni", lo, hi), A("rl", r0 + lo // 16, r0 + hi // 16)
+                add("V", lambda g, T, ni=ni, rc=rc: g.vector.tensor_scalar(ap(T, ni), ap(T, nw).indirect(ap(T, rc)), 2048.0, None, OP.add),
+                    [rc, nw], [ni], 0.05 + (hi - lo) * CY * COST["g"])
+                ts(S("na", lo, hi), ni, 4095, None, OP.bitwise_and)
                 if r < 2:
-                    act(A("sgn", a, b), e, AF.Sign, bias=0.5, acc=A("cnt", c, c + 1))
-                r5, rL, rH = A("r5", a, b), A("r2", lo, mid), A("r2", mid, hi)
-                ts(r5, e, 0.0, None, OP.max)
-                tt(rL, r5, A("tl", a, b), OP.mult)
-                tt(rH, r5, A("tl", 128 + a, 128 + b), OP.mult)
-                tt(A("ns", lo, hi), A("oi", lo, hi), A("r2", lo, hi), OP.add)
-                sL, sH = A("ns", lo, mid), A("ns", mid, hi)
-                so, sf = (sL, sH) if low else (sH, sL)
-                ts(A("nf", x0 + a, x0 + b), sf, 4095, None, OP.bitwise_and)
-                ts(A("nx", mine + a, mine + b), so, 4095, None, OP.bitwise_and)
-        stg[0] = 1000 * r + 200
-        nw = A("nx", v0, v0 + 256)
-        n0 = 144 * r
-        if r < 2:
-            pa = A("p0", 500, 501)
-            cn = [(pa, A("wa"), A("cnt", c, c + 1)) for c in range(len(TCH))]
-            mm(cn[-1:], first=False, dep=(mm(cn[:-1], last=False),))
-            fcol = n0 if low else n0 + 128
-            ts(A("nf", fcol, fcol + 1), pa, 7680.0, None, OP.add)
-            ts(A("ac", 4 * r, 4 * r + 1), pa, 5632.0, None, OP.add)
-            front, back = A("nx", v0 - 1, v0 + 128), A("nx", v0 + 128, v0 + 257)
-            send(mate, front if low else back, A("nf", n0, n0 + 129), back if low else front, "n%d" % r, COST["net"])
-            rcv = A("nx", v0 + 256, v0 + 257) if low else A("nx", v0 - 1, v0)
-            asum = A("ac", 4 * r + 1, 4 * r + 2)
-            tt(asum, A("ac", 4 * r, 4 * r + 1), rcv, OP.add)
-            ts(DA(r + 1), A("idf"), asum, None, OP.mult)
-            vn = 272 * (r + 1) + 8
-            acol = A("vs", vn + 256, vn + 257) if rank < (rank ^ ROUNDS[r + 1]) else A("vs", vn - 1, vn)
-            cp(acol, asum)
-            for c, (lo, hi) in enumerate(BCH):
-                stg[0] = 1000 * (r + 1) + c
-                xs, rc = A("xc", lo, hi), A("rl", 16 * r + lo // 16, 16 * r + hi // 16)
-                add("V", lambda g, T, xs=xs, rc=rc, nw=nw: g.vector.tensor_scalar(ap(T, xs), ap(T, nw).indirect(ap(T, rc)), -2048.0, None, OP.add),
-                    [rc, nw], [xs], 0.05 + (hi - lo) * CY * COST["g"])
-        else:
-            front, back = A("nx", v0, v0 + 128), A("nx", v0 + 128, v0 + 256)
-            send(mate, front if low else back, A("nf", x0, x0 + 128), back if low else front, "n%d" % r, COST["net"])
-            for h in range(2):
-                a, b = 128 * h, 128 * h + 128
-                gath(A("yo", a, b), nw, A("rl", 16 * r + 8 * h, 16 * r + 8 * h + 8), "V")
-                dma(lambda T, a=a, b=b: T.yu[:, a:b], lambda T, a=a, b=b: T.yo[:, a:b], [A("yo", a, b)], [], "styu%d" % h, 2.0)
+                    ts(S("xc", lo, hi), S("na", lo, hi), -2048.0, None, OP.add)
+                else:
+                    cp(S("yo", lo, hi), S("na", lo, hi))
+        home("y", S("yo"))
+
+    fill(FC("mh"), -0.5)
+    for h in range(2):
+        stream(h)
     return ops
 
 
@@ -433,7 +523,7 @@ def schedule(ops):
                 i = min(lst, key=lambda k: ready[k])
                 s = ready[i]
             else:
-                i = min((k for k in lst if ready[k] <= s0 + WIN), key=lambda k: (ops[k]["c"] > COST["long"], sg[k], -pr[k]))
+                i = min((k for k in lst if ready[k] <= s0 + WIN), key=lambda k: (sg[k] >= 0 and ops[k]["c"] > COST["long"], sg[k], -pr[k]))
                 s = max(f, ready[i])
             if best is None or s < best[0]:
                 best = (s, i, e)
@@ -452,10 +542,20 @@ def schedule(ops):
     return order, start
 
 
+def share(topo, cores, src, dst):
+    near = [c for c in cores if c != src and topo.chip(c) == topo.chip(src)]
+    far = [c for c in cores if topo.chip(c) != topo.chip(src)]
+    taken = topo.engines(src, far[0]) if far else []
+    pool, who = (taken, far) if dst in far else ([e for e in topo.engines(src, dst) if e not in taken], near)
+    k = len(pool) // len(who)
+    return pool[k * who.index(dst):k * who.index(dst) + k]
+
+
 def rank_program(g, core, T, topo):
     rank = T.rank_of(core)
     if rank is None:
         return
+    cores = list(T.cores)
     ops = build(rank)
     order, start = schedule(ops)
     queue = {"P": g.tensor, "V": g.vector, "S": g.scalar, "G": g, "Y": g.sync}
@@ -467,8 +567,9 @@ def rank_program(g, core, T, topo):
         o = ops[i]
         e = o["e"]
         if e == "N":
-            o["at"] = (o["sem"], o["amt"])
-            after[i] = {o["sem"]: o["amt"]}
+            amt = sum(len(share(topo, cores, cores[s], core)) for s in o["fn"])
+            o["at"] = (o["sem"], amt)
+            after[i] = {o["sem"]: amt}
             continue
         kn = known[e]
         need = [ops[j]["at"] + (j,) for j in o["d"]
@@ -480,12 +581,16 @@ def rank_program(g, core, T, topo):
             for s2, v2 in after[j].items():
                 kn[s2] = max(kn.get(s2, 0), v2)
         if o["k"] == "send":
-            mate, dst, src, sem = o["fn"]
-            to = T.cores[mate]
-            rid, pid, ring = topo.addr(to)
-            eng = topo.engines(core, to)[-NE:]
-            g.remote_dma(T[dst[0]][:, dst[1]:dst[2]], T[src[0]][:, src[1]:src[2]], T.sem[sem], T.sem.lsem, pid, rid, sum(1 << x for x in eng))
-            sent += len(eng)
+            dst, src, sem = o["fn"]
+            trs = []
+            for j, to in enumerate(cores):
+                if j != rank:
+                    rid, pid, ring = topo.addr(to)
+                    eng = share(topo, cores, core, to)
+                    trs.append(RemoteDMATransfer(dst_ids=[DstId(rid=rid, pnc=pid)], dma_engine_mask=sum(1 << x for x in eng),
+                                                 remote_sem=T.sem[sem(j)], src=src(T, j), dst=dst(T, j)))
+                    sent += len(eng)
+            g.remote_dma_fused(trs, local_sem=T.sem.lsem)
             after[i] = dict(kn)
             o["at"] = ("lsem", 0)
             continue

@@ -5,24 +5,29 @@ N = 4
 ROUNDS = (1, 2, 3)
 CH = [(0, 64), (64, 128)]
 P2 = 2.0 ** -12
-PAR = {"subs": 2, "ns": 4, "off": 0.0, "tb": "V", "vu": "S", "sig": "S", "nw": "S", "qy": "S", "coff": 0.5, "mat": "S"}
-SL = 512
+BIG = 2.0 ** 22
+PAR = {"cut": [[(32,), (32,)]] * 5, "ns": 6, "off": 0.5, "wv": "", "ua": "", "vu": "S", "sig": "S", "nw": "S", "qy": "S", "coff": 0.2, "mat": "S",
+       "c16": "0123", "dup0": 0, "dup1": 0, "own0": 2816, "own1": 3072, "passes": 3, "rk": 1.0, "ds0": 1.9, "ds1": 2.4,
+       "seq": ("e0", "o0", "e1", "o1", "u0", "t0", "t1", "v0", "v1"), "apart": 2, "sq": 1,
+       "lat": (2.6, 2.6, 3.6, 3.6, 3.5, 0, 0, 5.0, 7.0), "w4": "V", "line": 0, "lag": 0.5, "k0": 0.74, "k1": 0.49, "eg": 0, "rg": 0, "wide": 0.5, "kj": 0.001, "pr": 0, "col": "S", "land": 1,
+       "ahead": (0.02, 0.1, 0.2, 0.3, 0.4, 0.5)}
+SL = 1024
 
 MH_ = ["T", "I", "nI", "I32", "R0", "R1"] + [k + str(i) for k in ("TL", "IL") for i in (1, 2, 3)]
 MH_ += [k + str(r) for k in ("T1", "S1", "Pm") for r in range(3)] + ["W0", "W1"]
-MB_ = ["B", "KLE", "n4096", "cst", "Ko+", "Ko-", "K0+", "K0-", "K1+", "K1-", "D4", "D5", "V+", "V-", "tmp"]
+MB_ = ["B", "KLE", "n4096", "Ko+", "Ko-", "K0+", "K0-", "K1+", "K1-", "D4", "D5", "V+", "V-", "tmp0", "tmp1", "tmp2", "big", "Ib"]
 MB_ += ["Q%d%s" % (r, s) for r in range(3) for s in "+-"]
 SCRATCH = {}
 for _n, _w, _d in [
-        ("w0", 4096, "bfloat16"), ("w1", 4096, "bfloat16"), ("uin", 256, "int32"), ("ul", 4 * 256, "float16"),
-        ("ip", 1, "int32"), ("ii", 8, "int32"), ("fc", 96, "float32"),
+        ("w0", 4096, "bfloat16"), ("w1", 4096, "bfloat16"), ("uin", 256, "int32"), ("ul", 4 * 512, "float16"), ("rg", 256, "bfloat16"),
+        ("ip", 1, "int32"), ("ii", 8, "int32"), ("fc", 112, "float32"),
         ("iu", 256, "bfloat16"), ("uo", 128, "bfloat16"), ("mg", 128, "bfloat16"), ("ms", 128, "bfloat16"), ("m64", 128, "bfloat16"),
         ("ids", 5 * 128, "bfloat16"), ("jj", SL, "bfloat16"), ("jn", SL, "bfloat16"), ("rm", 64, "bfloat16"), ("dm", 64, "bfloat16"),
-        ("mh", len(MH_) * 128, "float16"), ("mb", len(MB_) * 128, "bfloat16"), ("me", 256, "float32"), ("z", 512, "float16"),
+        ("mh", len(MH_) * 128, "float16"), ("mb", len(MB_) * 128, "bfloat16"), ("me", 256, "float32"), ("z", 192, "float16"),
         ("ones", 256, "bfloat16"), ("mhalf", 64, "float16"), ("bias", 16, "float32"),
         ("xc", 256, "float16"), ("tb", 256, "bfloat16"), ("sq", 256, "float32"), ("yb", 256, "int32"),
         ("cb", 256, "int32"), ("c16", 256, "uint16"), ("gb", 4096, "bfloat16"), ("mx", 4096, "bfloat16"), ("mn", 4096, "bfloat16"),
-        ("kd", 256, "float32"), ("kc", 256, "float32"), ("vu", 256, "float32"), ("acc", 16, "float32"),
+        ("kd", 256, "float32"), ("spare", 8, "float32"), ("kc", 256, "float32"), ("vu", 256, "float32"), ("acc", 16, "float32"),
         ("trash", 1024, "bfloat16"), ("cmp", 4096, "bfloat16"), ("cs", 4096, "bfloat16"), ("rl", 48, "uint16"),
         ("vs", 6 * 256, "float32"), ("t8", 256, "bfloat16"), ("oc", 256, "float16"), ("w4", 256, "bfloat16"), ("rr", 256, "float16"),
         ("sg", 256, "bfloat16"), ("tau", 256, "float16"), ("rt", 256, "float16"), ("rf", 256, "float16"), ("u", 256, "float16"),
@@ -31,26 +36,37 @@ for _n, _w, _d in [
     SCRATCH[_n] = ("sbuf", [128, _w], _d)
 for _b in range(8):
     SCRATCH["p%d" % _b] = ("psum", [128, 512], "float32")
-SCRATCH["sd"] = ("dram", [8, 128, 512], "bfloat16")
-SCRATCH["sl"] = ("dram", [8, 128, 512], "bfloat16")
-SCRATCH["yl"] = ("dram", [8, 128, 128], "float32")
-SCRATCH["ql"] = ("dram", [8, 128, 128], "float32")
-SEMAPHORES = ["eP", "eV", "eS", "eG", "ldu", "lsem", "nu"]
-SEMAPHORES += [k + str(h) for k in ("ld", "lw", "ny", "nq", "oy", "oq", "sy", "sq") for h in range(2)]
-SEMAPHORES += ["ns%d_%d" % (h, s) for h in range(2) for s in range(N)]
+SCRATCH["sd"] = ("dram", [N, 128, 1024], "bfloat16")
+SCRATCH["sl"] = ("dram", [N, 128, 1024], "bfloat16")
+SCRATCH["yl"] = ("dram", [N, 128, 256], "float32")
+SCRATCH["ql"] = ("dram", [N, 128, 256], "float32")
+SCRATCH["se"] = ("dram", [8, 128, 512], "bfloat16")
+SCRATCH["sf"] = ("dram", [8, 128, 512], "bfloat16")
+SCRATCH["ym"] = ("dram", [8, 128, 128], "float32")
+SCRATCH["qm"] = ("dram", [8, 128, 128], "float32")
+for _n, _w in (("yt", 64), ("yk", 64), ("qt", 4), ("qk", 4)):
+    SCRATCH[_n] = ("dram", [N, 128, _w], "float32")
+for _n in ("ut", "uk"):
+    SCRATCH[_n] = ("dram", [N, 128, 64], "int32")
+SEMAPHORES = ["lu", "eP", "eV", "eS", "eG", "ldu", "lsem", "ld", "ny", "nq", "oy", "oq", "sy", "sq"]
+SEMAPHORES += [k + str(h) for k in ("lo", "lw", "nr", "ny", "nq", "oy", "oq") for h in range(2)] + ["ns%d" % s for s in range(N)]
+SEMAPHORES += ["nt%d_%d" % (h, s) for h in range(2) for s in range(N)]
 
 CY = 0.00083
-COST = {"V": 0.03, "S": 0.065, "P": 0.04, "lat": 0.16, "self": 0.043, "send": 0.6, "g": 1.6, "sc": 3.8, "long": 0.2}
+COST = {"V": 0.025, "S": 0.065, "P": 0.04, "lat": 0.16, "self": 0.16, "send": 1.0, "g": 1.6, "sc": 3.8, "long": 0.2, "wS": 0.3, "wV": 0.02}
 WIN = 0.0124
 
 
-def build(rank):
-    ops, hist, bank, pe, stg = [], {}, {}, {}, [None]
+def build(rank, near):
+    ops, hist, bank, pe, stg, line = [], {}, {}, {}, [None], []
     peers = [s for s in range(N) if s != rank]
+    early = "a0" in PAR["seq"]
 
     def add(eng, fn, rd, wr, cost, sem=None, amt=1, dep=(), kind="c", lat=None):
         i = len(ops)
         deps = set(dep)
+        prev = pe.get(eng) if eng == "Y" else None
+        pe[eng] = i
         for acc, w in [(a, False) for a in rd] + [(a, True) for a in wr]:
             nm, lo, hi = acc[0], acc[1], acc[2]
             if nm[0] == "p" and nm[1:].isdigit():
@@ -75,7 +91,8 @@ def build(rank):
             keep.append((lo, hi, i, w))
             hist[nm] = keep
         deps.discard(i)
-        ops.append({"e": eng, "fn": fn, "d": sorted(deps), "c": cost, "sem": sem, "amt": amt, "k": kind, "lat": lat, "s": stg[0]})
+        ops.append({"e": eng, "fn": fn, "d": sorted(deps), "c": cost, "sem": sem, "amt": amt, "k": kind, "lat": lat, "s": stg[0],
+                    "o": [] if prev is None or prev in deps or (stg[0] or 0) >= 0 else [prev]})
         return i
 
     def A(nm, lo=0, hi=None, st=1):
@@ -179,34 +196,108 @@ def build(rank):
         return slice(16 * g, 16 * g + 16)
 
     stg[0] = -9
-    dma(lambda T: T.uin[:], lambda T: T.units[:], [], [A("uin")], "ldu", 2.0)
-    mine = A("ul", 256 * rank, 256 * rank + 256)
-    ts(mine, A("uin"), -2048.0, None, OP.add)
-    iu_ = send(lambda T, j: ap(T, mine), lambda T, j: ap(T, mine), [mine], lambda j: "nu")
-    landed(iu_, peers, [A("ul", 256 * s, 256 * s + 256) for s in peers], "nu", 3.5)
-    last_send = iu_
-    for h in range(2):
-        stg[0] = -8 + 2 * h
-        st = [dma(lambda T, a=a, b=b: T.sd[a:b], lambda T, a=a, b=b: T.shelf[16 * a:16 * b, :], [], [], "ld%d" % h, 2.6 + h)
-              for a, b in ((4 * h, 4 * h + rank), (4 * h + rank + 1, 4 * h + 4)) if a < b]
+    packed = "x0" in PAR["seq"]
+    if not packed:
+        dma(lambda T: T.uin[:], lambda T: T.units[:], [], [A("uin")], "ldu", 2.0)
+
+    def double(w, cut, step):
+        for a in range(0, cut, step):
+            b = min(cut, a + step)
+            add("V", lambda g, T, a=a, b=b: g.vector.tensor_copy(T[w][64:128, a:b], T[w][0:64, a:b]), [(w.upper(), 0, 4)], [(w.upper(), 8 + a, 8 + b)],
+                COST["V"] + (b - a) * CY / 2)
+        for a in range(cut, 4096, step):
+            b = min(4096, a + step)
+            add("S", lambda g, T, a=a, b=b: g.scalar.activation(T[w][64:128, a:b], T[w][0:64, a:b], AF.Copy), [(w.upper(), 0, 4)],
+                [(w.upper(), 8 + a, 8 + b)], COST["S"] + (b - a) * CY)
+    if not packed:
+        ts(A("ni"), A("uin"), 2048.0, None, OP.add)
+        ts(A("na"), A("ni"), 4095, None, OP.bitwise_and)
+    for h in range(0 if packed else 2):
         for b in range(2):
-            o = 4 * b + rank
-            dma(lambda T, o=o, h=h: T["w%d" % h][rows(o), :], lambda T, h=h: T.shelf[rows(4 * h + rank), :], [], [("W%d" % h, o, o + 1)], "lw%d" % h, 2.6 + h)
-        last_send = send(lambda T, j, h=h: T.sl[4 * h + rank], lambda T, j, h=h: T.sd[4 * h + j], [], lambda j, h=h: "ns%d_%d" % (h, rank),
-                         dep=st + [last_send])
-        stg[0] = -4 + h
-        for s in sorted(peers, key=lambda s: s ^ rank != 2):
-            i = landed(last_send, [s], [], "ns%d_%d" % (h, s), (3.0 if s ^ rank == 2 else 5.0) + 2 * h)
-            for b in range(2):
-                o = 4 * b + s
-                dma(lambda T, o=o, h=h: T["w%d" % h][rows(o), :], lambda T, h=h, s=s: T.sl[4 * h + s], [], [("W%d" % h, o, o + 1)], "lw%d" % h, 2.2, dep=(i,))
+            a = 512 * rank + (256 if early else 128) * h
+            add("V", lambda g, T, h=h, b=b, a=a: g.vector.tensor_scalar(T.ul[64 * b:64 * b + 64, a:a + 128], T.na[64 * h:64 * h + 64, 128 * b:128 * b + 128],
+                                                                        -2048.0, None, OP.add),
+                [A("na")], [A("ul", a, a + 128)], COST["V"] + 128 * CY)
+    staged, got, last = [], {}, []
+
+    def start(step, lat):
+        kind, h = step[0], int(step[1])
+        w = "w%d" % h
+        stg[0] = -9
+        if kind == "a":
+            dma(lambda T: T[w][0:64, :], lambda T: T.shelf[64 * h:64 * h + 64, :], [], [(w.upper(), 0, 4)], "lo%d" % h, lat)
+            stg[0] = -4 + 1.8 * h
+            double(w, PAR["own%d" % h], 2048 - 1024 * h)
+        elif kind == "d":
+            staged.extend(dma(lambda T, a=a, b=b: T.sd[a:b, 64 * h:64 * h + 64, :], lambda T, a=a, b=b: T.shelf[64 * h + 16 * a:64 * h + 16 * b, :],
+                              [], [], "ld", lat) for a, b in ((0, rank), (rank + 1, N)) if a < b)
+        elif kind == "s":
+            last[:] = [send(lambda T, j: T.sl[rank], lambda T, j: T.sd[j], [], lambda j: "ns%d" % rank, dep=staged)]
+            for s in peers:
+                got[s] = landed(last[0], [s], [], "ns%d" % s, lat)
+        elif kind == "w":
+            for s in peers:
+                for o in range(s, 4 if PAR["dup%d" % h] else 8, 4):
+                    dma(lambda T, o=o: T[w][rows(o), :], lambda T, s=s: T.sl[s, 64 * h:64 * h + 64, :], [], [(w.upper(), o, o + 1)], "lw%d" % h,
+                        lat, dep=(got[s],))
+            if PAR["dup%d" % h]:
+                stg[0] = PAR["ds%d" % h]
+                double(w, PAR["dup%d" % h], 512)
+        elif kind == "e":
+            staged[:] = [dma(lambda T, a=a, b=b: T.se[4 * h + a:4 * h + b], lambda T, a=a, b=b: T.shelf[64 * h + 16 * a:64 * h + 16 * b, :],
+                             [], [], "lo%d" % h, lat) for a, b in ((0, rank), (rank + 1, N)) if a < b]
+            got[h] = list(staged)
+        elif kind == "o":
+            for o in range(rank, 4 if PAR["dup%d" % h] else 8, 4):
+                dma(lambda T, o=o: T[w][rows(o), :], lambda T: T.shelf[rows(4 * h + rank), :], [], [(w.upper(), o, o + 1)], "lw%d" % h, lat)
+        elif kind == "t":
+            last[:] = [send(lambda T, j: T.sf[4 * h + rank], lambda T, j: T.se[4 * h + j], [], lambda j: "nt%d_%d" % (h, rank), dep=got[h] + last)]
+            got[h] = last[0]
+        elif kind == "v":
+            for s in near + [s for s in peers if s not in near]:
+                i = landed(got[h], [s], [], "nt%d_%d" % (h, s), lat - 2 * (s in near))
+                for o in range(s, 4 if PAR["dup%d" % h] else 8, 4):
+                    dma(lambda T, o=o: T[w][rows(o), :], lambda T, s=s: T.sf[4 * h + s], [], [(w.upper(), o, o + 1)], "lw%d" % h, 2.2, dep=(i,))
+            if PAR["dup%d" % h]:
+                stg[0] = PAR["ds%d" % h]
+                double(w, PAR["dup%d" % h], 512)
+        elif kind == "x":
+            got["x"] = [dma(lambda T, q=q: T.ut[:, 32 * q:32 * q + 32, :], lambda T, q=q: T.units[64 * (q // 2):64 * (q // 2) + 64, 128 * (q % 2):128 * (q % 2) + 128],
+                            [], [], "ldu", lat, eng="S") for q in range(4)]
+        elif kind == "y":
+            last[:] = [send(lambda T, j: T.uk[rank], lambda T, j: T.ut[j], [], lambda j: "nr0", dep=got["x"] + last)]
+            both = (landed(last[0], peers, [], "nr0", lat), dma(lambda T: T.uk[rank], lambda T: T.ut[rank], [], [], "ld", 1.8, dep=got["x"], eng="S"))
+            for q in range(4):
+                a = 128 * (q // 2)
+                dma(lambda T, q=q, a=a: T.uin[64 * (q % 2):64 * (q % 2) + 64, a:a + 128], lambda T, q=q: T.uk[:, 32 * q:32 * q + 32, :],
+                    [], [("UIN", q, q + 1)], "nr1" if a else "lu", 1.8, dep=both, eng="S")
+            for q in range(2):
+                stg[0] = -5 + q
+                a, b = 128 * q, 128 * q + 128
+                add("V", lambda g, T, a=a, b=b: g.vector.tensor_scalar(T.ni[:, a:b], T.uin[:, a:b], 2048.0, None, OP.add), [("UIN", 2 * q, 2 * q + 2)],
+                    [A("ni", a, b)], COST["V"] + 128 * CY)
+                ts(A("na", a, b), A("ni", a, b), 4095, None, OP.bitwise_and)
+                ts(A("xc", a, b), A("na", a, b), -2048.0, None, OP.add)
+        elif kind == "u":
+            tile = A("ul", 512 * rank, 512 * rank + 256)
+            last[:] = [send(lambda T, j: ap(T, tile), lambda T, j: ap(T, tile), [tile], lambda j: "nr0", dep=last)]
+            landed(last[0], peers, [A("ul", 512 * s, 512 * s + 256) for s in peers], "nr0", lat)
+        else:
+            stream(h, True)
+            tile = A("ul", 512 * rank + 256 * h, 512 * rank + 256 * h + 256)
+            last[:] = [send(lambda T, j: ap(T, tile), lambda T, j: ap(T, tile), [tile], lambda j: "n" + step, dep=last)]
+            landed(last[0], peers, [A("ul", 512 * s + 256 * h, 512 * s + 256 * h + 256) for s in peers], "n" + step, lat)
+    steps = list(zip(PAR["seq"], PAR["lat"]))
+    while not last:
+        start(*steps.pop(0))
+    first_send = last[0]
     stg[0] = None
     iota(A("ip"), [[1, 1]], 0, 1)
     iota(A("iu"), [[1, 256]], 0, 0)
     iota(A("mg"), [[1, 8], [0, 16]], 0, 0)
     iota(A("jj", 0, 128), [[0, 8], [256, 16]], 0, 0)
-    iota(A("ms"), [[0, 2], [1, 4], [0, 16]], 0, 0, dep=(last_send,))
-    iota(A("m64"), [[0, 2], [1, 64]], 0, 0, dep=(last_send,))
+    iota(A("ms"), [[0, 2], [1, 4], [0, 16]], 0, 0)
+    iota(A("m64"), [[0, 2], [1, 64]], 0, 0)
     n = 128
     while n < SL:
         cp(A("jj", n, 2 * n), A("jj", 0, n))
@@ -222,43 +313,43 @@ def build(rank):
         ts(A("ii", i, i + 1), A("ip"), 1 << i, None, OP.bitwise_and)
     bits = FC("bit", 7, 0, 7)
     ts(bits, A("ii", 0, 7), 0, None, OP.is_gt)
-    for nm, a, b in (("lam", 2.0, -1.0), ("nl", -2.0, 1.0), ("L", -1.0, 1.0), ("hl", 1.0, -0.5), ("nb", -1.0, 0.0), ("b255", 255.0, 0.0)):
-        ts(FC(nm, 7, 0, 7), bits, a, b, OP.mult, OP.add)
+
+    def col(out, i0, scale, bias=None):
+        lin(PAR["col"], out, i0, scale, bias)
+    for nm, a, b in (("lam", 2.0, -1.0), ("nl", -2.0, 1.0), ("L", -1.0, 1.0), ("hl", 1.0, -0.5), ("nb", -1.0, None), ("b255", 255.0, None),
+                     ("lb", 16384.0, -8192.0)):
+        col(FC(nm, 7, 0, 7), bits, a, b)
 
     def bit(nm, i):
         return FC(nm, 7, i)
-    ts(FC("k256"), kf, 256.0, None, OP.mult)
-    ts(FC("k113"), kf, 113.0, None, OP.add)
-    ts(FC("k16"), kf, 1.0 / 16, None, OP.mult)
-    for h in range(2):
-        ts(FC("zc%d" % h), pg, float(4 * h + rank), FC("k113"), OP.is_equal, OP.mult)
-        ts(A("z", 256 * h, 256 * h + 256), A("iu"), FC("zc%d" % h), None, OP.is_equal)
-    ts(FC("bs0"), kf, 2048.0, 2048.0 + 786432.0, OP.mult, OP.add)
-    ts(FC("bt0"), FC("bs0"), P2, -4095.0 / 8192, OP.mult, OP.add)
-    ts(FC("bsA"), FC("bs0"), -5760.0, None, OP.add)
-    ts(FC("btA"), FC("bsA"), P2, -4095.0 / 8192, OP.mult, OP.add)
+    col(FC("k256"), kf, 256.0)
+    col(FC("k16"), kf, 1.0 / 16)
+    col(FC("nk16"), kf, -1.0 / 16)
+    col(FC("s"), bit("bit", 6), -4.0, pg)
+    col(FC("p49"), pf, 1.0, 49.0 - 16 * rank)
+    ts(FC("zc"), FC("s"), float(rank), FC("p49"), OP.is_equal, OP.mult)
+    ts(A("z"), A("iu", 0, 192), FC("zc"), None, OP.is_equal)
     ts(MB("B"), A("mg"), pg, None, OP.is_equal)
     ts(MB("KLE"), A("jj", 0, 128), FC("k256"), None, OP.is_ge)
     tt(MH("T"), MB("B"), MB("KLE"), OP.mult)
 
     def diag(out, at, f):
         ts(out, im, at, f, OP.is_equal, OP.mult)
-    for nm, f in (("I", 1.0), ("nI", -1.0), ("I32", 32.0)):
+    for nm, f in (("I", 1.0), ("I32", 32.0)):
         diag(MH(nm), pf, f)
-    for nm, f in (("n4096", -4096.0), ("cst", 65536.0 - 8388608.0), ("V+", 8192.0)):
+    for nm, f in (("n4096", -1.0), ("V+", 8192.0)):
         diag(MB(nm), pf, f)
     lin(PAR["mat"], MB("V-"), MB("V+"), -1.0)
     for i in (4, 5):
         diag(MB("D%d" % i), pf, bit("lam", i))
     lin(PAR["mat"], MB("Ko+"), MB("B"), 256.0)
     lin(PAR["mat"], MB("Ko-"), MB("B"), -256.0)
-    ts(FC("s"), bit("bit", 6), -4.0, pg, OP.mult, OP.add)
-    ts(FC("p64", 2), bit("bit", 6), -64.0, pf, OP.mult, OP.add)
-    ts(FC("p64", 2, 1), FC("p64", 2), 64.0, None, OP.add)
-    ts(FC("b128"), bit("bit", 6), 128.0, None, OP.mult)
-    ts(A("uo"), im, FC("b128"), None, OP.add)
+    col(FC("p64", 2), bit("bit", 6), -64.0, pf)
+    col(FC("p64", 2, 1), bit("L", 6), 64.0, pf)
+    col(FC("b128"), bit("bit", 6), 128.0)
+    lin(PAR["mat"], A("uo"), im, 1.0, FC("b128"))
     for b, nm in ((0, "L"), (1, "bit")):
-        ts(FC("h256", 2, b), bit(nm, 6), 256.0, None, OP.mult)
+        col(FC("h256", 2, b), bit(nm, 6), 256.0)
         ts(MB("K%d+" % b), A("ms"), FC("s"), FC("h256", 2, b), OP.is_equal, OP.mult)
         lin(PAR["mat"], MB("K%d-" % b), MB("K%d+" % b), -1.0)
         ts(MH("R%d" % b), A("m64"), FC("p64", 2), bit(nm, 6), OP.is_equal, OP.mult)
@@ -268,38 +359,39 @@ def build(rank):
         ts(MH("IL%d" % t), MH("I32"), bit("L", 3 - t), None, OP.mult)
     fill(A("ones"), 1.0)
     fill(A("mhalf"), -0.5)
-    ts(A("rm"), A("jj", 0, 64), 0.0, None, OP.is_gt)
-    ts(A("dm"), A("jj", 0, 64), FC("k256"), None, OP.is_equal)
+    ts(A("rm"), A("jj", 0, 64), 0.0, -2 * BIG, OP.is_equal, OP.mult)
+    ts(A("dm"), A("jj", 0, 64), FC("k256"), -BIG, OP.not_equal, OP.mult)
+    diag(MB("Ib"), pf, 1.0)
+    col(FC("d16"), bit("nl", 4), 16.0)
     for r, m in enumerate(ROUNDS):
-        pp, hb = FC("pp%d" % r), (5 if m & 2 else 4)
-        if m & 1:
-            ts(pp, bit("nl", 4), 16.0, pf, OP.mult, OP.add)
+        pp, dd, hb = FC("pp%d" % r), FC("dd%d" % r), (5 if m & 2 else 4)
         if m & 2:
-            ts(pp, bit("nl", 5), 32.0, pp if m & 1 else pf, OP.mult, OP.add)
-        diag(MH("Pm%d" % r), pp, 1.0)
+            col(dd, bit("nl", 5), 32.0, FC("d16") if m & 1 else None)
+        else:
+            dd = FC("d16")
+        col(pp, dd, 1.0, pf)
+        diag(MH("nI"), pp, 1.0)
+        tt(MH("Pm%d" % r), MH("nI"), MH("I"), OP.subtract)
         c1, c2, cid, cid4 = (FC("%s%d" % (k, r)) for k in ("c1", "c2", "id", "id4"))
-        ts(c1, pp, pf, bit("L", 3), OP.subtract, OP.mult)
-        ts(c1, c1, pf, None, OP.add)
+        col(c1, dd, bit("L", 3), pf)
         diag(MH("S1%d" % r), c1, 32.0)
-        ts(c2, c1, kf, 1.0 / 16, OP.subtract, OP.mult)
-        ts(MB("tmp"), A("mg"), c2, None, OP.is_equal)
-        tt(MH("T1%d" % r), MB("tmp"), MB("KLE"), OP.mult)
+        col(c2, c1, 1.0 / 16, FC("nk16"))
+        ts(MB("tmp%d" % r), A("mg"), c2, None, OP.is_equal)
+        tt(MH("T1%d" % r), MB("tmp%d" % r), MB("KLE"), OP.mult)
         ts(cid, pp, pf, kf, OP.min, OP.subtract)
-        ids = A("ids", 128 * r, 128 * r + 128)
-        for k in range(4):
-            v = [16 * min(x, x ^ m) for x in (2 * k, 2 * k + 1)]
-            iota(A("ids", 128 * r + 32 * k, 128 * r + 32 * k + 32), [[v[1] - v[0], 2], [0, 16]], v[0], 0, dep=(last_send,))
-        ts(MB("Q%d+" % r), ids, cid, bit("nl", hb), OP.is_equal, OP.mult)
+        for base, wrap in ((128 * r, 7), (384 + 128 * r, 3))[:2 if r < 2 else 1]:
+            for k in range(4):
+                v = [16 * min(x & wrap, (x ^ m) & wrap) for x in (2 * k, 2 * k + 1)]
+                iota(A("ids", base + 32 * k, base + 32 * k + 32), [[v[1] - v[0], 2], [0, 16]], v[0], 0, dep=(first_send,))
+        ts(MB("Q%d+" % r), A("ids", 128 * r, 128 * r + 128), cid, bit("nl", hb), OP.is_equal, OP.mult)
         lin(PAR["mat"], MB("Q%d-" % r), MB("Q%d+" % r), -1.0)
         if r < 2:
-            ts(cid4, bit("bit", 6), -64.0, cid, OP.mult, OP.add)
-            cp(A("ids", 384 + 128 * r, 448 + 128 * r), A("ids", 128 * r, 128 * r + 64))
-            cp(A("ids", 448 + 128 * r, 512 + 128 * r), A("ids", 128 * r, 128 * r + 64))
+            col(cid4, bit("bit", 6), -64.0, cid)
             ts(MH("W%d" % r), A("ids", 384 + 128 * r, 512 + 128 * r), cid4, FC("k16"), OP.is_equal, OP.mult)
     for k in range(6):
-        iota(A("vs", 256 * k, 256 * k + 256), [[0, 256]], 0, 0, dep=(last_send,))
+        iota(A("vs", 256 * k, 256 * k + 256), [[0, 256]], 0, 0, dep=(first_send,))
 
-    def stream(h):
+    def stream(h, first):
         o = 128 * h
 
         def S(nm, lo=0, hi=128):
@@ -314,57 +406,64 @@ def build(rank):
         def stage(step, c=0):
             stg[0] = step + PAR["off"] * h + PAR["coff"] * c
 
-        def columns(c, lo, hi, bs, bt, pre, late, xpt):
+        def columns(c, lo, hi, bs, bt, pre, late, xpt, kind):
             n = hi - lo
             x, w, xp = X(c, 0, n), Wb(c, 0, n), X(c, 64, n)
             tb = S("tb", lo, hi)
             mm([(x,) + a for a in pre], last=not late)
             if late:
                 mm([(x,) + a for a in late], first=False)
-            mm([(w,) + a for a in pre + late], last=False)
-            lin(PAR["tb"], tb, x, P2, bt)
-            mm([(w, MB("n4096"), tb)], first=False)
-            mm([(xp,) + a for a in xpt] + [(xp, MB("cst"), A("ones", 0, n))])
+            if kind in PAR["wv"]:
+                xp, w = w, S("kd", lo, hi)
+                mm([(xp,) + a for a in xpt])
+                ts(tb, x, bt, None, OP.add)
+                tt(w, x, tb, OP.subtract)
+            else:
+                mm([(w,) + a for a in pre + late], last=False)
+                ts(tb, x, bt, None, OP.add)
+                mm([(w, MB("n4096"), tb)], first=False)
+                mm([(xp,) + a for a in xpt])
             act(S("sq", lo, hi), w, AF.Square, bias=bs)
             tt(S("yb", lo, hi), S("sq", lo, hi), xp, OP.add)
             ts(S("cb", lo, hi), S("yb", lo, hi), 5, 4095, OP.arith_shift_right, OP.bitwise_and)
-            cp(S("c16", lo, hi), S("cb", lo, hi))
+            if kind not in PAR["c16"]:
+                cp(S("c16", lo, hi), S("cb", lo, hi))
+            else:
+                src, dst = S("cb", lo, hi), S("c16", lo, hi)
+                add("G", lambda g, T: g.affine_select(ap(T, dst), ap(T, src), [[0, n]], OP.is_ge, 0.0, 0, 0), [src], [dst], 0.17 + 2 * n * CY)
 
-        def gather_scan(lo, hi):
-            st = (hi - lo) // PAR["subs"] // 2 * 2
-            cut = [lo + s * st for s in range(PAR["subs"])] + [hi]
+        def gather_scan(step, lo, hi, win="w%d" % h, cut=None):
+            cut = [lo] + [lo + x for x in PAR["cut"][step % 5][lo // 64]] + [hi]
             parts = [(o + a, o + b) for a, b in zip(cut, cut[1:])]
             for (a, b) in parts:
                 out, off = A("gb", 16 * a, 16 * b), A("c16", a, b)
-                add("S", lambda g, T, out=out, off=off: g.scalar.activation(ap(T, out), T["w%d" % h][:, 0:4096].indirect(ap(T, off)), AF.Copy),
-                    [("W%d" % h, 0, 8), off], [out], 0.065 + size(out) * CY * COST["g"])
+                i = add("S", lambda g, T, out=out, off=off: g.scalar.activation(ap(T, out), T[win][:, 0:4096].indirect(ap(T, off)), AF.Copy),
+                        [(win.upper(), 0, 9999), off], [out], 0.065 + size(out) * CY * COST["g"])
+                at = step + step // 5 * (PAR["eg"] + PAR["rg"]) + (step % 5 > 0) * PAR["rg"]
+                line.append((at + PAR["lag"] * h + (a - o) / 128 * PAR["wide"], i))
             for (a, b) in parts:
                 m = 16 * (b - a)
                 scan(A("mx", 16 * a, 16 * b), A("jj", 0, m), A("gb", 16 * a, 16 * b), OP.min, OP.max)
                 scan(A("mn", 16 * a, 16 * b), A("jn", 0, m), A("gb", 16 * a, 16 * b), OP.max, OP.min)
             return A("mx", 16 * (o + lo) + 15, 16 * (o + hi), 16), A("mn", 16 * (o + lo) + 15, 16 * (o + hi), 16)
 
-        def home(kind, tile):
-            g_ = 4 * h + rank
-            land = kind + "l"
-            i = send(lambda T, j: T[land][g_], lambda T, j: ap(T, tile), [tile], lambda j: "n%s%d" % (kind, h))
-            got = (landed(i, peers, [], "n%s%d" % (kind, h), 2.6),
-                   dma(lambda T: T[land][g_], lambda T: ap(T, tile), [tile], [], "o%s%d" % (kind, h), 2.0))
-            for b in range(2):
-                a, r0 = 128 * b, 64 * b + 16 * rank
-                if kind == "y":
-                    dma(lambda T, a=a: T.yu[64 * h:64 * h + 64, a:a + 128], lambda T, r0=r0: T.yl[4 * h:4 * h + 4, r0:r0 + 16, :], [], [], "sy%d" % h, 2.0, dep=got)
-                else:
-                    dma(lambda T, a=a: T.yq[4 * h:4 * h + 4, a:a + 128], lambda T, r0=r0: T.ql[4 * h:4 * h + 4, r0, :], [], [], "sq%d" % h, 2.0, dep=got)
+        bs, bt = 786432.0, 786432.0 - 2047.5
+        if first:
+            for c, (lo, hi) in enumerate(CH):
+                stg[0] = -3 + h + 0.5 * c
+                a = 512 * rank + 2 * o
+                xs = A("ul", a + lo, a + hi)
+                columns(c, lo, hi, bs, bt, [(MH("T"), xs)], [], [(MH("I32"), xs)], "b")
+                mx, mn = gather_scan(0, lo, hi)
+                tt(A("ul", a + 128 + lo, a + 128 + hi), mx, mn, OP.subtract)
+            return
 
-        for c, (lo, hi) in enumerate(CH):
+        def pick(lo, hi):
+            return [(A("z", 49 - 16 * s, 177 - 16 * s), A("ul", 512 * s + (1 + early) * o + lo, 512 * s + (1 + early) * o + hi)) for s in range(N)]
+        for c, (lo, hi) in enumerate([] if packed else CH):
             stage(0, c)
-            n = hi - lo
-            pu = X(c, 448, n)
-            mm([(pu, A("z", 256 * h + 113 - 16 * (4 * b + s), 256 * h + 241 - 16 * (4 * b + s)), A("ul", 256 * s + 128 * b + lo, 256 * s + 128 * b + hi))
-                for s in range(N) for b in range(2)])
-            cp(S("xc", lo, hi), pu)
-        bs, bt = FC("bs0"), FC("bt0")
+            mm([(X(c, 384, hi - lo),) + a for a in pick(128 * early + lo, 128 * early + hi)])
+            cp(S("rg" if early else "xc", lo, hi), X(c, 384, hi - lo))
         ns = PAR["ns"]
         for r, m in enumerate(ROUNDS):
             hb = 5 if m & 2 else 4
@@ -373,35 +472,49 @@ def build(rank):
                 n = hi - lo
                 stage(6 * r, c)
                 xs = S("xc", lo, hi)
-                columns(c, lo, hi, bs, bt, [(MH("T"), xs)], [], [(MH("I32"), xs)])
+                if r or not early:
+                    columns(c, lo, hi, bs, bt, [(MH("T"), xs)], [], [(MH("I32"), xs)], "b")
+                mm([(Wb(c, 128, n), D, A("uo", lo, hi)), (Wb(c, 128, n), MB("Ib"), A("dm", 0, n))], last=False)
+            tiles = [0] if ns == 8 else [1] if ns == 0 else [0, 1]
+            for cc in tiles:
+                mm([(X(cc, 128, 256), D, A("iu"))], last=False)
             for c, (lo, hi) in enumerate(CH):
                 n = hi - lo
                 stage(6 * r, c)
                 xs = S("xc", lo, hi)
-                mx, mn = gather_scan(lo, hi)
+                ends = list(zip("+-", gather_scan(5 * r, lo, hi))) if r or not early else [("+", S("rg", lo, hi))]
                 kp, vp = Wb(c, 128, n), Wb(c, 192, n)
-                mm([(kp, D, A("uo", lo, hi)), (kp, MB("Ko+"), mx), (kp, MB("Ko-"), mn)])
-                mm([(vp, MH("I"), xs), (vp, MB("V+"), mx), (vp, MB("V-"), mn)])
-                for cc in ([0] if ns == 8 else [1] if ns == 0 else [0, 1]):
-                    for b in range(2):
-                        kt = X(cc, 128 + 128 * b + lo, n)
-                        mm([(kt, D, A("iu", 128 * b + lo, 128 * b + hi)), (kt, MB("K%d+" % b), mx), (kt, MB("K%d-" % b), mn)])
-                tt(S("kd", lo, hi), kp, A("dm", 0, n), OP.mult)
-                scan(S("kc", lo, hi), A("rm", 0, n), S("kd", lo, hi), OP.mult, OP.add)
+                for sign, e in ends:
+                    mm([(kp, MB("Ko" + sign), e)], first=False, last=e == ends[-1][1])
+                    for cc in tiles:
+                        mm([(X(cc, 128 + 128 * b + lo, n), MB("K%d%s" % (b, sign)), e) for b in range(2)], first=False, last=e == ends[-1][1] and hi == 128)
+                scan(S("kc", lo, hi), A("rm", 0, n), kp, OP.add, OP.max)
+                mm([(vp,) + a for a in ([(MH("I"), xs)] if r or not early else pick(lo, hi)) + [(MB("V" + sign), e) for sign, e in ends]])
+                mx, mn = ends[0][1], ends[-1][1]
                 lin(PAR["vu"], S("vu", lo, hi), vp, 1.0)
                 if r == 2:
                     stage(6 * r + 1.5, c)
                     qp = Wb(c, 448, n)
                     mm([(qp, MB("Ko+"), mx), (qp, MB("Ko-"), mn)])
-                    lin(PAR["qy"], S("qy", lo, hi), qp, 1.0 / 256)
-            if r == 2:
-                home("q", S("qy"))
-            stage(6 * r + 1)
+                    if PAR["apart"] < 2:
+                        lin(PAR["qy"], S("qy", lo, hi), qp, 1.0 / 256)
+                        continue
+                    for b in range(2):
+                        add("S", lambda g, T, b=b, qp=qp, lo=lo, hi=hi: g.scalar.activation(
+                            T.qy[64 * h:64 * h + 64, 128 * b + lo:128 * b + hi], T[qp[0]][64 * b:64 * b + 64, qp[1]:qp[2]], AF.Copy, scale=1.0 / 256),
+                            [qp], [("QY", h, h + 1)], COST["S"] + n * CY)
+            if r == 2 and PAR["apart"] == 1:
+                home1("q", "qy", h)
+            elif r == 2 and h:
+                (home2 if PAR["apart"] else home)("q", "qy")
+            stage(6 * r + PAR["rk"])
             r0 = 16 * r + 8 * h
             for j in range(8):
                 kcol = S("kc", 16 * j + 15, 16 * j + 16)
                 if j < ns:
-                    act(A("trash", 256 * (2 * h + j % 2), 256 * (2 * h + j % 2) + 256), X(0, 128, 256), AF.Sign, bias=kcol, scale=-1.0, acc=A("acc", 8 * h + j, 8 * h + j + 1))
+                    i = act(A("trash", 256 * (2 * h + j % 2), 256 * (2 * h + j % 2) + 256), X(0, 128, 256), AF.Sign, bias=kcol, scale=-1.0,
+                            acc=A("acc", 8 * h + j, 8 * h + j + 1))
+                    line.append((r * (5 + PAR["eg"] + PAR["rg"]) + PAR["lag"] * h + PAR["k%d" % h] + j * PAR["kj"], i))
                 else:
                     k = 256 * (8 * h + j)
                     ts(A("cmp", k, k + 256), X(1, 128, 256), kcol, None, OP.is_gt)
@@ -424,10 +537,10 @@ def build(rank):
                         mm([(vm, A("me", 128 * b, 128 * b + 128), A("vs", v0 + 2 * lo + b * n, v0 + 2 * lo + b * n + n)) for b in range(2)])
                         ts(t8, vm, 1.5 * 2.0 ** 36, 1.5 * 2.0 ** 36, OP.add, OP.subtract)
                         tt(oc, vm, t8, OP.subtract)
-                        columns(c, lo, hi, bs, bt, [(MH("T1%d" % r), oc)], [], [(MH("S1%d" % r), oc)])
+                        columns(c, lo, hi, bs, bt, [(MH("T1%d" % r), oc)], [], [(MH("S1%d" % r), oc)], "0")
                         stage(6 * r + 2.9, c)
                         dl, qd, w4 = Wb(c, 320, n), Wb(c, 384, n), S("w4", lo, hi)
-                        mm([(dl, MH("Pm%d" % r), oc), (dl, MH("nI"), oc)])
+                        mm([(dl, MH("Pm%d" % r), oc)])
                         mm([(qd, MB("Q%d+" % r), t8)])
                         ts(w4, dl, 1.5 * 2.0 ** 35, 1.5 * 2.0 ** 35, OP.add, OP.subtract)
                         tt(R, dl, w4, OP.subtract)
@@ -438,17 +551,23 @@ def build(rank):
                             ts(S("sg", lo, hi), qd, 0.0, 0.5, OP.is_gt, OP.subtract)
                         stage(6 * r + 2, c)
                     else:
-                        columns(c, lo, hi, bs, bt, [(MH("T"), oc)], [(MH("TL%d" % t), R)], [(MH("I32"), oc), (MH("IL%d" % t), R)])
+                        columns(c, lo, hi, bs, bt, [(MH("T"), oc)], [(MH("TL%d" % t), R)], [(MH("I32"), oc), (MH("IL%d" % t), R)], str(t))
                     if t == 3:
                         tt(S("rt", lo, hi), R, S("tau", lo, hi), OP.mult)
-                    mx, mn = gather_scan(lo, hi)
+                    mx, mn = gather_scan(5 * r + 1 + t, lo, hi)
                     q = Wb(c, 64, n)
-                    mm([(q, MH("I"), A("mhalf", 0, n)), (q, MB("Q%d+" % r), mx)], last=False)
+                    ab = str(t) in PAR["ua"]
+                    mm([(q, MH("I"), A("mhalf", 0, n))] + [(q, MB("V+"), S("sg", lo, hi))] * ab, last=False)
+                    mm([(q, MB("Q%d+" % r), mx)], first=False, last=False)
                     mm([(q, MB("Q%d-" % r), mn)], first=False)
                     stage(6 * r + 3 + t, c)
                     u, k = S("u", lo, hi), A("kk", 256 * t + o + lo, 256 * t + o + hi)
-                    tt(u, q, S("sg", lo, hi), OP.mult)
-                    ts(k, u, bit("lam", 3 - t), 0.0, OP.mult, OP.is_gt)
+                    if ab:
+                        act(S("kd", lo, hi), q, AF.Abs)
+                        ts(k, S("kd", lo, hi), bit("lam", 3 - t), bit("lb", 3 - t), OP.mult, OP.is_gt)
+                    else:
+                        tt(u, q, S("sg", lo, hi), OP.mult)
+                        ts(k, u, bit("lam", 3 - t), 0.0, OP.mult, OP.is_gt)
                     if t < 3:
                         tt(R, R, k, OP.mult)
                         continue
@@ -468,45 +587,139 @@ def build(rank):
                 red = A("red", 2 * r + h, 2 * r + h + 1)
                 add("V", lambda g, T, red=red, pa=pa: g.vector.tensor_reduce(ap(T, red), ap(T, pa), AX.X, OP.add), [pa], [red], COST["V"] + n * CY)
                 bs, bt = A("bias", 4 * r + 2 * h, 4 * r + 2 * h + 1), A("bias", 4 * r + 2 * h + 1, 4 * r + 2 * h + 2)
-                ts(bt, red, P2, FC("btA"), OP.mult, OP.add)
-                ts(bs, red, FC("bsA"), None, OP.add)
+                ts(bt, red, 786432.0 - 5760 - 2047.5, None, OP.add)
+                ts(bs, red, 786432.0 - 5760, None, OP.add)
             nw = A("nw", 2 * o, 2 * o + 256)
             for c, (lo, hi) in enumerate(CH):
                 stage(6 * r + 6, c)
                 ni, rc = S("ni", lo, hi), A("rl", r0 + lo // 16, r0 + hi // 16)
-                add("V", lambda g, T, ni=ni, rc=rc: g.vector.tensor_scalar(ap(T, ni), ap(T, nw).indirect(ap(T, rc)), 2048.0, None, OP.add),
+                add("V", lambda g, T, ni=ni, rc=rc, f=2048.0 * (r < 2): g.vector.tensor_scalar(ap(T, ni), ap(T, nw).indirect(ap(T, rc)), f, None, OP.add),
                     [rc, nw], [ni], 0.05 + (hi - lo) * CY * COST["g"])
                 ts(S("na", lo, hi), ni, 4095, None, OP.bitwise_and)
                 if r < 2:
                     ts(S("xc", lo, hi), S("na", lo, hi), -2048.0, None, OP.add)
-                else:
+                elif PAR["apart"] < 2:
                     cp(S("yo", lo, hi), S("na", lo, hi))
-        home("y", S("yo"))
+                else:
+                    for b in range(2):
+                        add("V", lambda g, T, b=b, lo=lo, hi=hi: g.vector.tensor_copy(
+                            T.yo[64 * h:64 * h + 64, 128 * b + lo:128 * b + hi], T.na[64 * b:64 * b + 64, o + lo:o + hi]),
+                            [S("na", lo, hi)], [("YO", h + (2 * c + b) / 4, h + (2 * c + b + 1) / 4)], COST["V"] + 64 * CY)
+
+    def home(kind, nm):
+        land, tile = kind + "l", A(nm)
+        i = send(lambda T, j: T[land][rank], lambda T, j: ap(T, tile), [tile], lambda j: "n" + kind)
+        both = (landed(i, peers, [], "n" + kind, 3.5), dma(lambda T: T[land][rank], lambda T: ap(T, tile), [tile], [], "o" + kind, 2.0))
+        k, out = (16, "yu") if kind == "y" else (1, "yq")
+        for h in range(2):
+            for b in range(2):
+                r0 = 64 * b + 16 * rank
+                dma(lambda T, h=h, b=b: T[out][4 * k * h:4 * k * h + 4 * k, 128 * b:128 * b + 128],
+                    lambda T, h=h, r0=r0: T[land][:, r0:r0 + k, 128 * h:128 * h + 128], [], [], "s" + kind, 2.0, dep=both,
+                    eng="S" if b and kind == "y" and PAR["sq"] else "Y")
+
+    def home2(kind, nm):
+        k, out, w = (1, "yu", 64) if kind == "y" else (16, "yq", 4)
+        st, both = [], []
+        for h in range(2):
+            rd = [(nm.upper(), h, h + 1)]
+            st.append(dma(lambda T, h=h: T[kind + "t"][:, 64 * h:64 * h + 64, :], lambda T, h=h: T[nm][64 * h:64 * h + 64:k, :], rd, [], "o%s%d" % (kind, h), 1.8))
+            r0 = 64 * h + 16 * rank
+            both.append(dma(lambda T, h=h: T[kind + "k"][rank, 64 * h:64 * h + 64, :], lambda T, r0=r0: T[nm][r0:r0 + 16:k, :], rd, [], "o" + kind, 1.8,
+                            eng="S" if kind == "y" and PAR["sq"] else "Y"))
+        i = send(lambda T, j: T[kind + "k"][rank], lambda T, j: T[kind + "t"][j], [], lambda j: "n" + kind, dep=st)
+        both.append(landed(i, peers, [], "n" + kind, 2.5))
+        for h in range(2):
+            dma(lambda T, h=h: T[out][64 // k * h:64 // k * (h + 1), :], lambda T, h=h: T[kind + "k"][:, 64 * h:64 * h + 64, :], [], [], "s" + kind, 2.0, dep=both,
+                eng="S" if h and kind == "y" and PAR["sq"] else "Y")
+
+    def home1(kind, nm, h):
+        land, tile, g_ = kind + "m", A(nm, 128 * h, 128 * h + 128), 4 * h + rank
+        i = send(lambda T, j: T[land][g_], lambda T, j: ap(T, tile), [tile], lambda j: "n%s%d" % (kind, h))
+        both = (landed(i, peers, [], "n%s%d" % (kind, h), 3.5), dma(lambda T: T[land][g_], lambda T: ap(T, tile), [tile], [], "o%s%d" % (kind, h), 2.0))
+        k, out = (16, "yu") if kind == "y" else (1, "yq")
+        for b in range(2):
+            r0 = 64 * b + 16 * rank
+            dma(lambda T, b=b: T[out][4 * k * h:4 * k * h + 4 * k, 128 * b:128 * b + 128],
+                lambda T, r0=r0: T[land][4 * h:4 * h + 4, r0:r0 + k, :], [], [], "s" + kind, 2.0, dep=both)
 
     fill(FC("mh"), -0.5)
+    for step in steps:
+        start(*step)
     for h in range(2):
-        stream(h)
+        stream(h, False)
+        if PAR["apart"] == 1:
+            home1("y", "yo", h)
+    if PAR["apart"] != 1:
+        (home2 if PAR["apart"] else home)("y", "yo")
+    line.sort()
+    for (a, i), (b, j) in zip(line, line[1:]):
+        if PAR["line"] and i not in ops[j]["d"]:
+            ops[j]["o"].append(i)
     return ops
 
 
-def schedule(ops):
+def latency(ops, j, i):
+    if j in ops[i]["o"] or ops[j]["e"] == ops[i]["e"] == "P":
+        return 0.0
+    if ops[j]["lat"] is not None:
+        return ops[j]["lat"]
+    return COST["self"] if ops[j]["e"] == ops[i]["e"] else COST["lat"]
+
+
+def justify(ops, start, passes):
+    n = len(ops)
+    pre = [[(j, latency(ops, j, i)) for j in o["d"] + o["o"]] for i, o in enumerate(ops)]
+    suc = [[] for _ in ops]
+    for i in range(n):
+        for j, d in pre[i]:
+            suc[j].append((i, d))
+
+    def place(key, before):
+        at, busy = [0.0] * n, {}
+        for i in sorted(range(n), key=key):
+            c, t = ops[i]["c"], max([at[j] + ops[j]["c"] + d for j, d in before[i]] + [0.0])
+            if ops[i]["e"] != "N":
+                lst = busy.setdefault(ops[i]["e"], [])
+                k = len(lst)
+                while k and lst[k - 1][1] > t:
+                    k -= 1
+                while k < len(lst) and lst[k][0] < t + c - 1e-9:
+                    t = max(t, lst[k][1])
+                    k += 1
+                lst.insert(k, (t, t + c))
+            at[i] = t
+        return at, max(at[i] + ops[i]["c"] for i in range(n))
+    best = (max(start[i] + ops[i]["c"] for i in range(n)), start)
+    for _ in range(passes):
+        back, span = place(lambda i: (-start[i] - ops[i]["c"], -i), suc)
+        start, span = place(lambda i: (-back[i] - ops[i]["c"], i), pre)
+        best = min(best, (span, start))
+    return best[0], sorted(range(n), key=lambda i: (best[1][i], i))
+
+
+def schedule(ops, ahead):
     n = len(ops)
     succ = [[] for _ in ops]
     for i, o in enumerate(ops):
-        for j in o["d"]:
+        for j in o["d"] + o["o"]:
             succ[j].append(i)
 
     def lat(j, i):
-        if ops[j]["lat"] is not None:
-            return ops[j]["lat"]
-        return COST["self"] if ops[j]["e"] == ops[i]["e"] else COST["lat"]
+        return latency(ops, j, i)
     pr = [0.0] * n
     sg = [9999 if o["s"] is None else o["s"] for o in ops]
-    for i in range(n - 1, -1, -1):
+    left, todo = [len(s) for s in succ], [i for i in range(n) if not succ[i]]
+    for i in todo:
+        for j in ops[i]["d"] + ops[i]["o"]:
+            left[j] -= 1
+            if left[j] == 0:
+                todo.append(j)
+    for i in todo:
         pr[i] = ops[i]["c"] + max([pr[s] + lat(i, s) for s in succ[i]] + [0.0])
         if ops[i]["s"] is None:
             sg[i] = min([sg[x] for x in succ[i]] + [9999])
-    cnt = [len(o["d"]) for o in ops]
+    cnt = [len(o["d"] + o["o"]) for o in ops]
     ready, start = [0.0] * n, [0.0] * n
     free, avail, order = {}, {}, []
     for i in range(n):
@@ -523,7 +736,7 @@ def schedule(ops):
                 i = min(lst, key=lambda k: ready[k])
                 s = ready[i]
             else:
-                i = min((k for k in lst if ready[k] <= s0 + WIN), key=lambda k: (sg[k] >= 0 and ops[k]["c"] > COST["long"], sg[k], -pr[k]))
+                i = min((k for k in lst if ready[k] <= s0 + (ahead if e == "S" else WIN)), key=lambda k: -pr[k] if PAR["pr"] else (sg[k] >= 0 and ops[k]["c"] > COST["long"], sg[k], -pr[k]))
                 s = max(f, ready[i])
             if best is None or s < best[0]:
                 best = (s, i, e)
@@ -556,8 +769,9 @@ def rank_program(g, core, T, topo):
     if rank is None:
         return
     cores = list(T.cores)
-    ops = build(rank)
-    order, start = schedule(ops)
+    near = [s for s in range(N) if s != rank and topo.chip(cores[s]) == topo.chip(core)]
+    ops = build(rank, near)
+    span, order = min(justify(ops, schedule(ops, ahead)[1], PAR["passes"]) for ahead in PAR["ahead"])
     queue = {"P": g.tensor, "V": g.vector, "S": g.scalar, "G": g, "Y": g.sync}
     own = {"P": "eP", "V": "eV", "S": "eS", "G": "eG"}
     known = {e: {} for e in queue}
@@ -583,7 +797,8 @@ def rank_program(g, core, T, topo):
         if o["k"] == "send":
             dst, src, sem = o["fn"]
             trs = []
-            for j, to in enumerate(cores):
+            for j in sorted(range(N), key=lambda j: j in near):
+                to = cores[j]
                 if j != rank:
                     rid, pid, ring = topo.addr(to)
                     eng = share(topo, cores, core, to)

@@ -4,30 +4,29 @@ from concourse.mybir import AluOpType as OP, ActivationFunctionType as AF, AxisL
 N = 4
 ROUNDS = (1, 2, 3)
 CH = [(0, 64), (64, 128)]
-P2 = 2.0 ** -12
+NS = 5
 BIG = 2.0 ** 22
-PAR = {"cut": [[(32,), (32,)]] * 5, "ns": 6, "off": 0.5, "wv": "", "ua": "", "vu": "S", "sig": "S", "nw": "S", "qy": "S", "coff": 0.2, "mat": "S",
-       "c16": "0123", "dup0": 0, "dup1": 0, "own0": 2816, "own1": 3072, "passes": 3, "rk": 1.0, "ds0": 1.9, "ds1": 2.4,
-       "seq": ("e0", "o0", "e1", "o1", "u0", "t0", "t1", "v0", "v1"), "apart": 2, "sq": 1,
-       "lat": (2.6, 2.6, 3.6, 3.6, 3.5, 0, 0, 5.0, 7.0), "w4": "V", "line": 0, "lag": 0.5, "k0": 0.74, "k1": 0.49, "eg": 0, "rg": 0, "wide": 0.5, "kj": 0.001, "pr": 0, "col": "S", "land": 1,
-       "ahead": (0.02, 0.1, 0.2, 0.3, 0.4, 0.5)}
-SL = 1024
+OFF = 786432.0
+SUM0 = 5760.0
+START = (("stage", 0, 2.2), ("own", 0, 3.7), ("own", 1, 5.2), ("stage", 1, 6.2), ("deal", 0, 0), ("first", 0, 3.5), ("first", 1, 3.5),
+         ("deal", 1, 0), ("fill", 0, 6.0), ("fill", 1, 6.0))
 
-MH_ = ["T", "I", "nI", "I32", "R0", "R1"] + [k + str(i) for k in ("TL", "IL") for i in (1, 2, 3)]
+MH_ = ["T", "I", "tmp", "I32", "R0", "R1"] + [k + str(i) for k in ("TL", "IL") for i in (1, 2, 3)]
 MH_ += [k + str(r) for k in ("T1", "S1", "Pm") for r in range(3)] + ["W0", "W1"]
-MB_ = ["B", "KLE", "n4096", "Ko+", "Ko-", "K0+", "K0-", "K1+", "K1-", "D4", "D5", "V+", "V-", "tmp0", "tmp1", "tmp2", "big", "Ib"]
+MB_ = ["B", "KLE", "nI", "Ko+", "Ko-", "K0+", "K0-", "K1+", "K1-", "D4", "D5", "V+", "V-", "tmp0", "tmp1", "tmp2", "Ib"]
 MB_ += ["Q%d%s" % (r, s) for r in range(3) for s in "+-"]
 SCRATCH = {}
 for _n, _w, _d in [
         ("w0", 4096, "bfloat16"), ("w1", 4096, "bfloat16"), ("uin", 256, "int32"), ("ul", 4 * 512, "float16"), ("rg", 256, "bfloat16"),
-        ("ip", 1, "int32"), ("ii", 8, "int32"), ("fc", 112, "float32"),
+        ("ip", 1, "int32"), ("ii", 8, "int32"), ("fc", 96, "float32"),
         ("iu", 256, "bfloat16"), ("uo", 128, "bfloat16"), ("mg", 128, "bfloat16"), ("ms", 128, "bfloat16"), ("m64", 128, "bfloat16"),
-        ("ids", 5 * 128, "bfloat16"), ("jj", SL, "bfloat16"), ("jn", SL, "bfloat16"), ("rm", 64, "bfloat16"), ("dm", 64, "bfloat16"),
+        ("ids", 5 * 128, "bfloat16"), ("jj", 512, "bfloat16"), ("jn", 512, "bfloat16"), ("rm", 64, "bfloat16"), ("dm", 64, "bfloat16"),
         ("mh", len(MH_) * 128, "float16"), ("mb", len(MB_) * 128, "bfloat16"), ("me", 256, "float32"), ("z", 192, "float16"),
-        ("ones", 256, "bfloat16"), ("mhalf", 64, "float16"), ("bias", 16, "float32"),
+        ("ones", 256, "bfloat16"), ("mhalf", 64, "float16"), ("bias", 4, "float32"),
         ("xc", 256, "float16"), ("tb", 256, "bfloat16"), ("sq", 256, "float32"), ("yb", 256, "int32"),
         ("cb", 256, "int32"), ("c16", 256, "uint16"), ("gb", 4096, "bfloat16"), ("mx", 4096, "bfloat16"), ("mn", 4096, "bfloat16"),
-        ("kd", 256, "float32"), ("spare", 8, "float32"), ("kc", 256, "float32"), ("vu", 256, "float32"), ("acc", 16, "float32"),
+        ("old", 256, "float32"), ("t4", 256, "float32"), ("de0", 256, "float16"), ("de1", 256, "float16"),
+        ("kc", 256, "float32"), ("vu", 256, "float32"), ("acc", 16, "float32"),
         ("trash", 1024, "bfloat16"), ("cmp", 4096, "bfloat16"), ("cs", 4096, "bfloat16"), ("rl", 48, "uint16"),
         ("vs", 6 * 256, "float32"), ("t8", 256, "bfloat16"), ("oc", 256, "float16"), ("w4", 256, "bfloat16"), ("rr", 256, "float16"),
         ("sg", 256, "bfloat16"), ("tau", 256, "float16"), ("rt", 256, "float16"), ("rf", 256, "float16"), ("u", 256, "float16"),
@@ -36,37 +35,28 @@ for _n, _w, _d in [
     SCRATCH[_n] = ("sbuf", [128, _w], _d)
 for _b in range(8):
     SCRATCH["p%d" % _b] = ("psum", [128, 512], "float32")
-SCRATCH["sd"] = ("dram", [N, 128, 1024], "bfloat16")
-SCRATCH["sl"] = ("dram", [N, 128, 1024], "bfloat16")
-SCRATCH["yl"] = ("dram", [N, 128, 256], "float32")
-SCRATCH["ql"] = ("dram", [N, 128, 256], "float32")
 SCRATCH["se"] = ("dram", [8, 128, 512], "bfloat16")
 SCRATCH["sf"] = ("dram", [8, 128, 512], "bfloat16")
 SCRATCH["ym"] = ("dram", [8, 128, 128], "float32")
 SCRATCH["qm"] = ("dram", [8, 128, 128], "float32")
-for _n, _w in (("yt", 64), ("yk", 64), ("qt", 4), ("qk", 4)):
-    SCRATCH[_n] = ("dram", [N, 128, _w], "float32")
-for _n in ("ut", "uk"):
-    SCRATCH[_n] = ("dram", [N, 128, 64], "int32")
-SEMAPHORES = ["lu", "eP", "eV", "eS", "eG", "ldu", "lsem", "ld", "ny", "nq", "oy", "oq", "sy", "sq"]
-SEMAPHORES += [k + str(h) for k in ("lo", "lw", "nr", "ny", "nq", "oy", "oq") for h in range(2)] + ["ns%d" % s for s in range(N)]
+SEMAPHORES = ["eP", "eV", "eS", "eG", "ldu", "lsem", "sy", "sq"]
+SEMAPHORES += [k + str(h) for k in ("lo", "le", "lw", "nr", "ny", "nq", "oy", "oq") for h in range(2)]
 SEMAPHORES += ["nt%d_%d" % (h, s) for h in range(2) for s in range(N)]
 
 CY = 0.00083
-COST = {"V": 0.025, "S": 0.065, "P": 0.04, "lat": 0.16, "self": 0.16, "send": 1.0, "g": 1.6, "sc": 3.8, "long": 0.2, "wS": 0.3, "wV": 0.02}
-WIN = 0.0124
+COST = {"V": 0.018, "S": 0.065, "P": 0.04, "lat": 0.18, "self": 0.26, "send": 0.8, "g": 1.6, "sc": 3.8, "long": 0.2}
+WIN, AHEAD, PASSES = 0.0124, 0.55, 2
 
 
 def build(rank, near):
-    ops, hist, bank, pe, stg, line = [], {}, {}, {}, [None], []
+    ops, hist, bank, prior, stg = [], {}, {}, {}, [None]
     peers = [s for s in range(N) if s != rank]
-    early = "a0" in PAR["seq"]
 
     def add(eng, fn, rd, wr, cost, sem=None, amt=1, dep=(), kind="c", lat=None):
         i = len(ops)
         deps = set(dep)
-        prev = pe.get(eng) if eng == "Y" else None
-        pe[eng] = i
+        prev = prior.get(eng) if eng == "Y" else None
+        prior[eng] = i
         for acc, w in [(a, False) for a in rd] + [(a, True) for a in wr]:
             nm, lo, hi = acc[0], acc[1], acc[2]
             if nm[0] == "p" and nm[1:].isdigit():
@@ -78,8 +68,8 @@ def build(rank, near):
                 deps.update(st[2])
                 st[1].append(i)
                 if eng == "P":
-                    deps.add(pe.get(nm, i))
-                    pe[nm] = i
+                    deps.add(prior.get(nm, i))
+                    prior[nm] = i
                 continue
             keep = []
             for (a, b, j, jw) in hist.setdefault(nm, []):
@@ -128,6 +118,9 @@ def build(rank, near):
     def cp(out, i0):
         return add("V", lambda g, T: g.vector.tensor_copy(ap(T, out), ap(T, i0)), [i0], [out], vcost(out, [i0]))
 
+    def nearest(out, i0, m):
+        return ts(out, i0, 1.5 * 2.0 ** 23 * m, 1.5 * 2.0 ** 23 * m, OP.add, OP.subtract)
+
     def fill(out, v):
         return add("V", lambda g, T: g.vector.memset(ap(T, out), v), [], [out], vcost(out, []))
 
@@ -146,10 +139,8 @@ def build(rank, near):
             return g.scalar.activation(ap(T, out), ap(T, i0), func, **kw)
         return add("S", fn, [i0] + cols(bias, scale), [out] + ([acc] if acc else []), COST["S"] + size(out) * CY + (0.02 if acc else 0))
 
-    def lin(eng, out, i0, scale, bias=None):
-        if eng == "S":
-            return act(out, i0, AF.Copy if bias is None else AF.Identity, bias=bias, scale=scale)
-        return ts(out, i0, scale, None, OP.mult) if bias is None else ts(out, i0, scale, bias, OP.mult, OP.add)
+    def lin(out, i0, scale, bias=None):
+        return act(out, i0, AF.Copy if bias is None else AF.Identity, bias=bias, scale=scale)
 
     def mm(terms, first=True, last=True):
         def fn(g, T):
@@ -182,9 +173,8 @@ def build(rank, near):
             return g.iota(ap(T, out), pat, base, cm)
         return add("G", fn, [], [out], 0.13 + 2 * size(out) * CY, dep=dep)
 
-    def dma(dst, src, rd, wr, sem, lat, dep=(), eng="Y"):
-        q = (lambda g: g.sync) if eng == "Y" else (lambda g: g.scalar)
-        return add(eng, lambda g, T: q(g).dma_start(dst(T), src(T)), rd, wr, 0.1, sem=sem, amt=16, kind="dma", lat=lat, dep=dep)
+    def dma(dst, src, rd, wr, sem, lat, dep=()):
+        return add("Y", lambda g, T: g.sync.dma_start(dst(T), src(T)), rd, wr, 0.1, sem=sem, amt=16, kind="dma", lat=lat, dep=dep)
 
     def send(dst, src, rd, sem, dep=()):
         return add("G", (dst, src, sem), rd, [], COST["send"], dep=dep, kind="send")
@@ -192,102 +182,41 @@ def build(rank, near):
     def landed(i, senders, wr, sem, net):
         return add("N", senders, [], wr, 0.0, sem=sem, dep=(i,), kind="net", lat=net)
 
-    def rows(g):
-        return slice(16 * g, 16 * g + 16)
-
     stg[0] = -9
-    packed = "x0" in PAR["seq"]
-    if not packed:
-        dma(lambda T: T.uin[:], lambda T: T.units[:], [], [A("uin")], "ldu", 2.0)
-
-    def double(w, cut, step):
-        for a in range(0, cut, step):
-            b = min(cut, a + step)
-            add("V", lambda g, T, a=a, b=b: g.vector.tensor_copy(T[w][64:128, a:b], T[w][0:64, a:b]), [(w.upper(), 0, 4)], [(w.upper(), 8 + a, 8 + b)],
-                COST["V"] + (b - a) * CY / 2)
-        for a in range(cut, 4096, step):
-            b = min(4096, a + step)
-            add("S", lambda g, T, a=a, b=b: g.scalar.activation(T[w][64:128, a:b], T[w][0:64, a:b], AF.Copy), [(w.upper(), 0, 4)],
-                [(w.upper(), 8 + a, 8 + b)], COST["S"] + (b - a) * CY)
-    if not packed:
-        ts(A("ni"), A("uin"), 2048.0, None, OP.add)
-        ts(A("na"), A("ni"), 4095, None, OP.bitwise_and)
-    for h in range(0 if packed else 2):
+    dma(lambda T: T.uin[:], lambda T: T.units[:], [], [A("uin")], "ldu", 2.0)
+    ts(A("ni"), A("uin"), 2048.0, None, OP.add)
+    ts(A("na"), A("ni"), 4095, None, OP.bitwise_and)
+    for h in range(2):
         for b in range(2):
-            a = 512 * rank + (256 if early else 128) * h
+            a = 512 * rank + 256 * h
             add("V", lambda g, T, h=h, b=b, a=a: g.vector.tensor_scalar(T.ul[64 * b:64 * b + 64, a:a + 128], T.na[64 * h:64 * h + 64, 128 * b:128 * b + 128],
                                                                         -2048.0, None, OP.add),
                 [A("na")], [A("ul", a, a + 128)], COST["V"] + 128 * CY)
-    staged, got, last = [], {}, []
+    got, last = {}, []
 
-    def start(step, lat):
-        kind, h = step[0], int(step[1])
-        w = "w%d" % h
+    def start(kind, h, lat):
+        w, W = "w%d" % h, "W%d" % h
         stg[0] = -9
-        if kind == "a":
-            dma(lambda T: T[w][0:64, :], lambda T: T.shelf[64 * h:64 * h + 64, :], [], [(w.upper(), 0, 4)], "lo%d" % h, lat)
-            stg[0] = -4 + 1.8 * h
-            double(w, PAR["own%d" % h], 2048 - 1024 * h)
-        elif kind == "d":
-            staged.extend(dma(lambda T, a=a, b=b: T.sd[a:b, 64 * h:64 * h + 64, :], lambda T, a=a, b=b: T.shelf[64 * h + 16 * a:64 * h + 16 * b, :],
-                              [], [], "ld", lat) for a, b in ((0, rank), (rank + 1, N)) if a < b)
-        elif kind == "s":
-            last[:] = [send(lambda T, j: T.sl[rank], lambda T, j: T.sd[j], [], lambda j: "ns%d" % rank, dep=staged)]
-            for s in peers:
-                got[s] = landed(last[0], [s], [], "ns%d" % s, lat)
-        elif kind == "w":
-            for s in peers:
-                for o in range(s, 4 if PAR["dup%d" % h] else 8, 4):
-                    dma(lambda T, o=o: T[w][rows(o), :], lambda T, s=s: T.sl[s, 64 * h:64 * h + 64, :], [], [(w.upper(), o, o + 1)], "lw%d" % h,
-                        lat, dep=(got[s],))
-            if PAR["dup%d" % h]:
-                stg[0] = PAR["ds%d" % h]
-                double(w, PAR["dup%d" % h], 512)
-        elif kind == "e":
-            staged[:] = [dma(lambda T, a=a, b=b: T.se[4 * h + a:4 * h + b], lambda T, a=a, b=b: T.shelf[64 * h + 16 * a:64 * h + 16 * b, :],
-                             [], [], "lo%d" % h, lat) for a, b in ((0, rank), (rank + 1, N)) if a < b]
-            got[h] = list(staged)
-        elif kind == "o":
-            for o in range(rank, 4 if PAR["dup%d" % h] else 8, 4):
-                dma(lambda T, o=o: T[w][rows(o), :], lambda T: T.shelf[rows(4 * h + rank), :], [], [(w.upper(), o, o + 1)], "lw%d" % h, lat)
-        elif kind == "t":
-            last[:] = [send(lambda T, j: T.sf[4 * h + rank], lambda T, j: T.se[4 * h + j], [], lambda j: "nt%d_%d" % (h, rank), dep=got[h] + last)]
+        if kind == "own":
+            for b in range(2):
+                dma(lambda T, b=b: T[w][64 * b:64 * b + 64, :], lambda T: T.shelf[64 * h:64 * h + 64, :], [], [(W, 4 * b, 4 * b + 4)], "lo%d" % h, lat + 1.2 * b)
+        elif kind == "stage":
+            got[h] = [dma(lambda T, a=a, b=b: T.se[4 * h + a:4 * h + b], lambda T, a=a, b=b: T.shelf[64 * h + 16 * a:64 * h + 16 * b, :],
+                          [], [], "le%d" % h, lat) for a, b in ((0, rank), (rank + 1, N)) if a < b]
+        elif kind == "deal":
+            last[:] = [send(lambda T, j: T.sf[4 * h + rank], lambda T, j: T.se[4 * h + j], [], "nt%d_%d" % (h, rank), dep=got[h] + last)]
             got[h] = last[0]
-        elif kind == "v":
+        elif kind == "fill":
             for s in near + [s for s in peers if s not in near]:
                 i = landed(got[h], [s], [], "nt%d_%d" % (h, s), lat - 2 * (s in near))
-                for o in range(s, 4 if PAR["dup%d" % h] else 8, 4):
-                    dma(lambda T, o=o: T[w][rows(o), :], lambda T, s=s: T.sf[4 * h + s], [], [(w.upper(), o, o + 1)], "lw%d" % h, 2.2, dep=(i,))
-            if PAR["dup%d" % h]:
-                stg[0] = PAR["ds%d" % h]
-                double(w, PAR["dup%d" % h], 512)
-        elif kind == "x":
-            got["x"] = [dma(lambda T, q=q: T.ut[:, 32 * q:32 * q + 32, :], lambda T, q=q: T.units[64 * (q // 2):64 * (q // 2) + 64, 128 * (q % 2):128 * (q % 2) + 128],
-                            [], [], "ldu", lat, eng="S") for q in range(4)]
-        elif kind == "y":
-            last[:] = [send(lambda T, j: T.uk[rank], lambda T, j: T.ut[j], [], lambda j: "nr0", dep=got["x"] + last)]
-            both = (landed(last[0], peers, [], "nr0", lat), dma(lambda T: T.uk[rank], lambda T: T.ut[rank], [], [], "ld", 1.8, dep=got["x"], eng="S"))
-            for q in range(4):
-                a = 128 * (q // 2)
-                dma(lambda T, q=q, a=a: T.uin[64 * (q % 2):64 * (q % 2) + 64, a:a + 128], lambda T, q=q: T.uk[:, 32 * q:32 * q + 32, :],
-                    [], [("UIN", q, q + 1)], "nr1" if a else "lu", 1.8, dep=both, eng="S")
-            for q in range(2):
-                stg[0] = -5 + q
-                a, b = 128 * q, 128 * q + 128
-                add("V", lambda g, T, a=a, b=b: g.vector.tensor_scalar(T.ni[:, a:b], T.uin[:, a:b], 2048.0, None, OP.add), [("UIN", 2 * q, 2 * q + 2)],
-                    [A("ni", a, b)], COST["V"] + 128 * CY)
-                ts(A("na", a, b), A("ni", a, b), 4095, None, OP.bitwise_and)
-                ts(A("xc", a, b), A("na", a, b), -2048.0, None, OP.add)
-        elif kind == "u":
-            tile = A("ul", 512 * rank, 512 * rank + 256)
-            last[:] = [send(lambda T, j: ap(T, tile), lambda T, j: ap(T, tile), [tile], lambda j: "nr0", dep=last)]
-            landed(last[0], peers, [A("ul", 512 * s, 512 * s + 256) for s in peers], "nr0", lat)
+                for o in (s, 4 + s):
+                    dma(lambda T, o=o: T[w][16 * o:16 * o + 16, :], lambda T, s=s: T.sf[4 * h + s], [], [(W, o, o + 1)], "lw%d" % h, 2.2, dep=(i,))
         else:
             stream(h, True)
             tile = A("ul", 512 * rank + 256 * h, 512 * rank + 256 * h + 256)
-            last[:] = [send(lambda T, j: ap(T, tile), lambda T, j: ap(T, tile), [tile], lambda j: "n" + step, dep=last)]
-            landed(last[0], peers, [A("ul", 512 * s + 256 * h, 512 * s + 256 * h + 256) for s in peers], "n" + step, lat)
-    steps = list(zip(PAR["seq"], PAR["lat"]))
+            last[:] = [send(lambda T, j: ap(T, tile), lambda T, j: ap(T, tile), [tile], "nr%d" % h, dep=last)]
+            landed(last[0], peers, [A("ul", 512 * s + 256 * h, 512 * s + 256 * h + 256) for s in peers], "nr%d" % h, lat)
+    steps = list(START)
     while not last:
         start(*steps.pop(0))
     first_send = last[0]
@@ -298,10 +227,8 @@ def build(rank, near):
     iota(A("jj", 0, 128), [[0, 8], [256, 16]], 0, 0)
     iota(A("ms"), [[0, 2], [1, 4], [0, 16]], 0, 0)
     iota(A("m64"), [[0, 2], [1, 64]], 0, 0)
-    n = 128
-    while n < SL:
+    for n in (128, 256):
         cp(A("jj", n, 2 * n), A("jj", 0, n))
-        n *= 2
     ts(A("jn"), A("jj"), -1.0, 256.0, OP.mult, OP.add)
     im = A("iu", 0, 128)
     pf, kf, pg = FC("p"), FC("k"), FC("pg")
@@ -313,20 +240,16 @@ def build(rank, near):
         ts(A("ii", i, i + 1), A("ip"), 1 << i, None, OP.bitwise_and)
     bits = FC("bit", 7, 0, 7)
     ts(bits, A("ii", 0, 7), 0, None, OP.is_gt)
-
-    def col(out, i0, scale, bias=None):
-        lin(PAR["col"], out, i0, scale, bias)
-    for nm, a, b in (("lam", 2.0, -1.0), ("nl", -2.0, 1.0), ("L", -1.0, 1.0), ("hl", 1.0, -0.5), ("nb", -1.0, None), ("b255", 255.0, None),
-                     ("lb", 16384.0, -8192.0)):
-        col(FC(nm, 7, 0, 7), bits, a, b)
+    for nm, a, b in (("lam", 2.0, -1.0), ("nl", -2.0, 1.0), ("L", -1.0, 1.0), ("hl", 1.0, -0.5), ("nb", -1.0, None), ("b255", 255.0, None)):
+        lin(FC(nm, 7, 0, 7), bits, a, b)
 
     def bit(nm, i):
         return FC(nm, 7, i)
-    col(FC("k256"), kf, 256.0)
-    col(FC("k16"), kf, 1.0 / 16)
-    col(FC("nk16"), kf, -1.0 / 16)
-    col(FC("s"), bit("bit", 6), -4.0, pg)
-    col(FC("p49"), pf, 1.0, 49.0 - 16 * rank)
+    lin(FC("k256"), kf, 256.0)
+    lin(FC("k16"), kf, 1.0 / 16)
+    lin(FC("nk16"), kf, -1.0 / 16)
+    lin(FC("s"), bit("bit", 6), -4.0, pg)
+    lin(FC("p49"), pf, 1.0, 49.0 - 16 * rank)
     ts(FC("zc"), FC("s"), float(rank), FC("p49"), OP.is_equal, OP.mult)
     ts(A("z"), A("iu", 0, 192), FC("zc"), None, OP.is_equal)
     ts(MB("B"), A("mg"), pg, None, OP.is_equal)
@@ -335,23 +258,21 @@ def build(rank, near):
 
     def diag(out, at, f):
         ts(out, im, at, f, OP.is_equal, OP.mult)
-    for nm, f in (("I", 1.0), ("I32", 32.0)):
-        diag(MH(nm), pf, f)
-    for nm, f in (("n4096", -1.0), ("V+", 8192.0)):
-        diag(MB(nm), pf, f)
-    lin(PAR["mat"], MB("V-"), MB("V+"), -1.0)
+    for out, f in ((MH("I"), 1.0), (MH("I32"), 32.0), (MB("nI"), -1.0), (MB("V+"), 16384.0)):
+        diag(out, pf, f)
+    lin(MB("V-"), MB("V+"), -1.0)
     for i in (4, 5):
         diag(MB("D%d" % i), pf, bit("lam", i))
-    lin(PAR["mat"], MB("Ko+"), MB("B"), 256.0)
-    lin(PAR["mat"], MB("Ko-"), MB("B"), -256.0)
-    col(FC("p64", 2), bit("bit", 6), -64.0, pf)
-    col(FC("p64", 2, 1), bit("L", 6), 64.0, pf)
-    col(FC("b128"), bit("bit", 6), 128.0)
-    lin(PAR["mat"], A("uo"), im, 1.0, FC("b128"))
+    lin(MB("Ko+"), MB("B"), 256.0)
+    lin(MB("Ko-"), MB("B"), -256.0)
+    lin(FC("p64", 2), bit("bit", 6), -64.0, pf)
+    lin(FC("p64", 2, 1), bit("L", 6), 64.0, pf)
+    lin(FC("b128"), bit("bit", 6), 128.0)
+    lin(A("uo"), im, 1.0, FC("b128"))
     for b, nm in ((0, "L"), (1, "bit")):
-        col(FC("h256", 2, b), bit(nm, 6), 256.0)
+        lin(FC("h256", 2, b), bit(nm, 6), 256.0)
         ts(MB("K%d+" % b), A("ms"), FC("s"), FC("h256", 2, b), OP.is_equal, OP.mult)
-        lin(PAR["mat"], MB("K%d-" % b), MB("K%d+" % b), -1.0)
+        lin(MB("K%d-" % b), MB("K%d+" % b), -1.0)
         ts(MH("R%d" % b), A("m64"), FC("p64", 2), bit(nm, 6), OP.is_equal, OP.mult)
         ts(A("me", 128 * b, 128 * b + 128), im, FC("p64", 2, b), None, OP.is_equal)
     for t in (1, 2, 3):
@@ -362,20 +283,20 @@ def build(rank, near):
     ts(A("rm"), A("jj", 0, 64), 0.0, -2 * BIG, OP.is_equal, OP.mult)
     ts(A("dm"), A("jj", 0, 64), FC("k256"), -BIG, OP.not_equal, OP.mult)
     diag(MB("Ib"), pf, 1.0)
-    col(FC("d16"), bit("nl", 4), 16.0)
+    lin(FC("d16"), bit("nl", 4), 16.0)
     for r, m in enumerate(ROUNDS):
         pp, dd, hb = FC("pp%d" % r), FC("dd%d" % r), (5 if m & 2 else 4)
         if m & 2:
-            col(dd, bit("nl", 5), 32.0, FC("d16") if m & 1 else None)
+            lin(dd, bit("nl", 5), 32.0, FC("d16") if m & 1 else None)
         else:
             dd = FC("d16")
-        col(pp, dd, 1.0, pf)
-        diag(MH("nI"), pp, 1.0)
-        tt(MH("Pm%d" % r), MH("nI"), MH("I"), OP.subtract)
+        lin(pp, dd, 1.0, pf)
+        diag(MH("tmp"), pp, 1.0)
+        tt(MH("Pm%d" % r), MH("tmp"), MH("I"), OP.subtract)
         c1, c2, cid, cid4 = (FC("%s%d" % (k, r)) for k in ("c1", "c2", "id", "id4"))
-        col(c1, dd, bit("L", 3), pf)
+        lin(c1, dd, bit("L", 3), pf)
         diag(MH("S1%d" % r), c1, 32.0)
-        col(c2, c1, 1.0 / 16, FC("nk16"))
+        lin(c2, c1, 1.0 / 16, FC("nk16"))
         ts(MB("tmp%d" % r), A("mg"), c2, None, OP.is_equal)
         tt(MH("T1%d" % r), MB("tmp%d" % r), MB("KLE"), OP.mult)
         ts(cid, pp, pf, kf, OP.min, OP.subtract)
@@ -384,15 +305,15 @@ def build(rank, near):
                 v = [16 * min(x & wrap, (x ^ m) & wrap) for x in (2 * k, 2 * k + 1)]
                 iota(A("ids", base + 32 * k, base + 32 * k + 32), [[v[1] - v[0], 2], [0, 16]], v[0], 0, dep=(first_send,))
         ts(MB("Q%d+" % r), A("ids", 128 * r, 128 * r + 128), cid, bit("nl", hb), OP.is_equal, OP.mult)
-        lin(PAR["mat"], MB("Q%d-" % r), MB("Q%d+" % r), -1.0)
+        lin(MB("Q%d-" % r), MB("Q%d+" % r), -1.0)
         if r < 2:
-            col(cid4, bit("bit", 6), -64.0, cid)
+            lin(cid4, bit("bit", 6), -64.0, cid)
             ts(MH("W%d" % r), A("ids", 384 + 128 * r, 512 + 128 * r), cid4, FC("k16"), OP.is_equal, OP.mult)
     for k in range(6):
         iota(A("vs", 256 * k, 256 * k + 256), [[0, 256]], 0, 0, dep=(first_send,))
 
     def stream(h, first):
-        o = 128 * h
+        o, win = 128 * h, "w%d" % h
 
         def S(nm, lo=0, hi=128):
             return A(nm, o + lo, o + hi)
@@ -404,125 +325,109 @@ def build(rank, near):
             return A("p%d" % (4 * h + 2 * c + 1), lo, lo + n)
 
         def stage(step, c=0):
-            stg[0] = step + PAR["off"] * h + PAR["coff"] * c
+            stg[0] = step + 0.5 * h + 0.2 * c
 
-        def columns(c, lo, hi, bs, bt, pre, late, xpt, kind):
+        def columns(c, lo, hi, bs, bt, pre, late, xpt):
             n = hi - lo
             x, w, xp = X(c, 0, n), Wb(c, 0, n), X(c, 64, n)
-            tb = S("tb", lo, hi)
+            tb, cb, c16 = S("tb", lo, hi), S("cb", lo, hi), S("c16", lo, hi)
             mm([(x,) + a for a in pre], last=not late)
             if late:
                 mm([(x,) + a for a in late], first=False)
-            if kind in PAR["wv"]:
-                xp, w = w, S("kd", lo, hi)
-                mm([(xp,) + a for a in xpt])
-                ts(tb, x, bt, None, OP.add)
-                tt(w, x, tb, OP.subtract)
-            else:
-                mm([(w,) + a for a in pre + late], last=False)
-                ts(tb, x, bt, None, OP.add)
-                mm([(w, MB("n4096"), tb)], first=False)
-                mm([(xp,) + a for a in xpt])
+            mm([(w,) + a for a in pre + late], last=False)
+            ts(tb, x, bt, OFF - SUM0 - 2047.5, OP.add, OP.add)
+            mm([(w, MB("nI"), tb)], first=False)
+            mm([(xp,) + a for a in xpt])
             act(S("sq", lo, hi), w, AF.Square, bias=bs)
             tt(S("yb", lo, hi), S("sq", lo, hi), xp, OP.add)
-            ts(S("cb", lo, hi), S("yb", lo, hi), 5, 4095, OP.arith_shift_right, OP.bitwise_and)
-            if kind not in PAR["c16"]:
-                cp(S("c16", lo, hi), S("cb", lo, hi))
-            else:
-                src, dst = S("cb", lo, hi), S("c16", lo, hi)
-                add("G", lambda g, T: g.affine_select(ap(T, dst), ap(T, src), [[0, n]], OP.is_ge, 0.0, 0, 0), [src], [dst], 0.17 + 2 * n * CY)
+            ts(cb, S("yb", lo, hi), 5, 4095, OP.arith_shift_right, OP.bitwise_and)
+            add("G", lambda g, T: g.affine_select(ap(T, c16), ap(T, cb), [[0, n]], OP.is_ge, 0.0, 0, 0), [cb], [c16], 0.17 + 2 * n * CY)
 
-        def gather_scan(step, lo, hi, win="w%d" % h, cut=None):
-            cut = [lo] + [lo + x for x in PAR["cut"][step % 5][lo // 64]] + [hi]
-            parts = [(o + a, o + b) for a, b in zip(cut, cut[1:])]
+        def gather_scan(lo, hi):
+            parts = [(o + lo, o + lo + 32), (o + lo + 32, o + hi)]
             for (a, b) in parts:
                 out, off = A("gb", 16 * a, 16 * b), A("c16", a, b)
-                i = add("S", lambda g, T, out=out, off=off: g.scalar.activation(ap(T, out), T[win][:, 0:4096].indirect(ap(T, off)), AF.Copy),
-                        [(win.upper(), 0, 9999), off], [out], 0.065 + size(out) * CY * COST["g"])
-                at = step + step // 5 * (PAR["eg"] + PAR["rg"]) + (step % 5 > 0) * PAR["rg"]
-                line.append((at + PAR["lag"] * h + (a - o) / 128 * PAR["wide"], i))
+                add("S", lambda g, T, out=out, off=off: g.scalar.activation(ap(T, out), T[win][:, 0:4096].indirect(ap(T, off)), AF.Copy),
+                    [(win.upper(), 0, 9999), off], [out], 0.065 + size(out) * CY * COST["g"])
             for (a, b) in parts:
                 m = 16 * (b - a)
                 scan(A("mx", 16 * a, 16 * b), A("jj", 0, m), A("gb", 16 * a, 16 * b), OP.min, OP.max)
                 scan(A("mn", 16 * a, 16 * b), A("jn", 0, m), A("gb", 16 * a, 16 * b), OP.max, OP.min)
             return A("mx", 16 * (o + lo) + 15, 16 * (o + hi), 16), A("mn", 16 * (o + lo) + 15, 16 * (o + hi), 16)
 
-        bs, bt = 786432.0, 786432.0 - 2047.5
+        def home(kind, nm):
+            land, tile, g_ = kind + "m", S(nm), 4 * h + rank
+            i = send(lambda T, j: T[land][g_], lambda T, j: ap(T, tile), [tile], "n%s%d" % (kind, h))
+            both = (landed(i, peers, [], "n%s%d" % (kind, h), 3.5), dma(lambda T: T[land][g_], lambda T: ap(T, tile), [tile], [], "o%s%d" % (kind, h), 2.0))
+            k, out = (16, "yu") if kind == "y" else (1, "yq")
+            for b in range(2):
+                r0 = 64 * b + 16 * rank
+                dma(lambda T, b=b: T[out][4 * k * h:4 * k * h + 4 * k, 128 * b:128 * b + 128],
+                    lambda T, r0=r0: T[land][4 * h:4 * h + 4, r0:r0 + k, :], [], [], "s" + kind, 2.0, dep=both)
+
+        bs, bt = OFF, SUM0
         if first:
             for c, (lo, hi) in enumerate(CH):
                 stg[0] = -3 + h + 0.5 * c
                 a = 512 * rank + 2 * o
                 xs = A("ul", a + lo, a + hi)
-                columns(c, lo, hi, bs, bt, [(MH("T"), xs)], [], [(MH("I32"), xs)], "b")
-                mx, mn = gather_scan(0, lo, hi)
+                columns(c, lo, hi, bs, bt, [(MH("T"), xs)], [], [(MH("I32"), xs)])
+                mx, mn = gather_scan(lo, hi)
                 tt(A("ul", a + 128 + lo, a + 128 + hi), mx, mn, OP.subtract)
             return
 
         def pick(lo, hi):
-            return [(A("z", 49 - 16 * s, 177 - 16 * s), A("ul", 512 * s + (1 + early) * o + lo, 512 * s + (1 + early) * o + hi)) for s in range(N)]
-        for c, (lo, hi) in enumerate([] if packed else CH):
+            return [(A("z", 49 - 16 * s, 177 - 16 * s), A("ul", 512 * s + 2 * o + lo, 512 * s + 2 * o + hi)) for s in range(N)]
+        for c, (lo, hi) in enumerate(CH):
             stage(0, c)
-            mm([(X(c, 384, hi - lo),) + a for a in pick(128 * early + lo, 128 * early + hi)])
-            cp(S("rg" if early else "xc", lo, hi), X(c, 384, hi - lo))
-        ns = PAR["ns"]
+            mm([(X(c, 384, hi - lo),) + a for a in pick(128 + lo, 128 + hi)])
+            cp(S("rg", lo, hi), X(c, 384, hi - lo))
         for r, m in enumerate(ROUNDS):
             hb = 5 if m & 2 else 4
             D = MB("D%d" % hb)
+            parts = ("xc", "de0", "de1")[:r + 1]
             for c, (lo, hi) in enumerate(CH):
                 n = hi - lo
                 stage(6 * r, c)
-                xs = S("xc", lo, hi)
-                if r or not early:
-                    columns(c, lo, hi, bs, bt, [(MH("T"), xs)], [], [(MH("I32"), xs)], "b")
+                xs = [S(k, lo, hi) for k in parts]
+                if r:
+                    columns(c, lo, hi, bs, bt, [(MH("T"), a) for a in xs[:r]], [(MH("T"), xs[r])], [(MH("I32"), a) for a in xs])
                 mm([(Wb(c, 128, n), D, A("uo", lo, hi)), (Wb(c, 128, n), MB("Ib"), A("dm", 0, n))], last=False)
-            tiles = [0] if ns == 8 else [1] if ns == 0 else [0, 1]
-            for cc in tiles:
+            for cc in range(2):
                 mm([(X(cc, 128, 256), D, A("iu"))], last=False)
             for c, (lo, hi) in enumerate(CH):
                 n = hi - lo
                 stage(6 * r, c)
-                xs = S("xc", lo, hi)
-                ends = list(zip("+-", gather_scan(5 * r, lo, hi))) if r or not early else [("+", S("rg", lo, hi))]
+                ends = list(zip("+-", gather_scan(lo, hi))) if r else [("+", S("rg", lo, hi))]
                 kp, vp = Wb(c, 128, n), Wb(c, 192, n)
                 for sign, e in ends:
                     mm([(kp, MB("Ko" + sign), e)], first=False, last=e == ends[-1][1])
-                    for cc in tiles:
+                    for cc in range(2):
                         mm([(X(cc, 128 + 128 * b + lo, n), MB("K%d%s" % (b, sign)), e) for b in range(2)], first=False, last=e == ends[-1][1] and hi == 128)
                 scan(S("kc", lo, hi), A("rm", 0, n), kp, OP.add, OP.max)
-                mm([(vp,) + a for a in ([(MH("I"), xs)] if r or not early else pick(lo, hi)) + [(MB("V" + sign), e) for sign, e in ends]])
-                mx, mn = ends[0][1], ends[-1][1]
-                lin(PAR["vu"], S("vu", lo, hi), vp, 1.0)
+                xs = [(MH("I"), S(k, lo, hi)) for k in parts] if r else pick(lo, hi)
+                mm([(vp,) + a for a in xs + [(MB("V" + sign), e) for sign, e in ends]])
+                cp(S("vu", lo, hi), vp)
                 if r == 2:
                     stage(6 * r + 1.5, c)
                     qp = Wb(c, 448, n)
-                    mm([(qp, MB("Ko+"), mx), (qp, MB("Ko-"), mn)])
-                    if PAR["apart"] < 2:
-                        lin(PAR["qy"], S("qy", lo, hi), qp, 1.0 / 256)
-                        continue
-                    for b in range(2):
-                        add("S", lambda g, T, b=b, qp=qp, lo=lo, hi=hi: g.scalar.activation(
-                            T.qy[64 * h:64 * h + 64, 128 * b + lo:128 * b + hi], T[qp[0]][64 * b:64 * b + 64, qp[1]:qp[2]], AF.Copy, scale=1.0 / 256),
-                            [qp], [("QY", h, h + 1)], COST["S"] + n * CY)
-            if r == 2 and PAR["apart"] == 1:
-                home1("q", "qy", h)
-            elif r == 2 and h:
-                (home2 if PAR["apart"] else home)("q", "qy")
-            stage(6 * r + PAR["rk"])
+                    mm([(qp, MB("Ko" + sign), e) for sign, e in ends])
+                    ts(S("qy", lo, hi), qp, 1.0 / 256, None, OP.mult)
+            if r == 2:
+                home("q", "qy")
+            stage(6 * r + 0.6)
             r0 = 16 * r + 8 * h
             for j in range(8):
                 kcol = S("kc", 16 * j + 15, 16 * j + 16)
-                if j < ns:
-                    i = act(A("trash", 256 * (2 * h + j % 2), 256 * (2 * h + j % 2) + 256), X(0, 128, 256), AF.Sign, bias=kcol, scale=-1.0,
-                            acc=A("acc", 8 * h + j, 8 * h + j + 1))
-                    line.append((r * (5 + PAR["eg"] + PAR["rg"]) + PAR["lag"] * h + PAR["k%d" % h] + j * PAR["kj"], i))
+                if j < NS:
+                    k = 256 * (2 * h + j % 2)
+                    act(A("trash", k, k + 256), X(0, 128, 256), AF.Sign, bias=kcol, scale=-1.0, acc=A("acc", 8 * h + j, 8 * h + j + 1))
                 else:
                     k = 256 * (8 * h + j)
                     ts(A("cmp", k, k + 256), X(1, 128, 256), kcol, None, OP.is_gt)
                     scan(A("cs", k, k + 256), A("ones"), A("cmp", k, k + 256), OP.mult, OP.add)
-            if ns < 8:
-                ts(A("rl", r0 + ns, r0 + 8), A("cs", 256 * (8 * h + ns) + 255, 256 * (8 * h + 8), 256), bit("nl", hb), bit("b255", hb), OP.mult, OP.add)
-            if ns:
-                ts(A("rl", r0, r0 + ns), A("acc", 8 * h, 8 * h + ns), bit("hl", hb), 127.5, OP.mult, OP.add)
+            ts(A("rl", r0 + NS, r0 + 8), A("cs", 256 * (8 * h + NS) + 255, 256 * (8 * h + 8), 256), bit("nl", hb), bit("b255", hb), OP.mult, OP.add)
+            ts(A("rl", r0, r0 + NS), A("acc", 8 * h, 8 * h + NS), bit("hl", hb), 127.5, OP.mult, OP.add)
             rl = A("rl", r0, r0 + 8)
             v0 = 256 * (2 * r + h)
             vw = A("vs", v0, v0 + 256)
@@ -533,50 +438,47 @@ def build(rank, near):
                     stage(6 * r + 2 + t, c)
                     oc, R = S("oc", lo, hi), S("rr", lo, hi)
                     if t == 0:
-                        vm, t8 = Wb(c, 256, n), S("t8", lo, hi)
+                        vm, t8, t4 = Wb(c, 256, n), S("t8", lo, hi), S("t4", lo, hi)
                         mm([(vm, A("me", 128 * b, 128 * b + 128), A("vs", v0 + 2 * lo + b * n, v0 + 2 * lo + b * n + n)) for b in range(2)])
-                        ts(t8, vm, 1.5 * 2.0 ** 36, 1.5 * 2.0 ** 36, OP.add, OP.subtract)
-                        tt(oc, vm, t8, OP.subtract)
-                        columns(c, lo, hi, bs, bt, [(MH("T1%d" % r), oc)], [], [(MH("S1%d" % r), oc)], "0")
+                        if r:
+                            nearest(t4, vm, 4096)
+                        nearest(t8, vm, 16384)
+                        tt(oc, vm, t4 if r else t8, OP.subtract)
+                        columns(c, lo, hi, bs, bt, [(MH("T1%d" % r), oc)], [], [(MH("S1%d" % r), oc)])
                         stage(6 * r + 2.9, c)
                         dl, qd, w4 = Wb(c, 320, n), Wb(c, 384, n), S("w4", lo, hi)
                         mm([(dl, MH("Pm%d" % r), oc)])
                         mm([(qd, MB("Q%d+" % r), t8)])
-                        ts(w4, dl, 1.5 * 2.0 ** 35, 1.5 * 2.0 ** 35, OP.add, OP.subtract)
+                        nearest(w4, dl, 4096)
                         tt(R, dl, w4, OP.subtract)
                         ts(S("tau", lo, hi), qd, bit("lam", hb), bit("nb", hb), OP.mult, OP.is_gt)
-                        if PAR["sig"] == "S":
-                            act(S("sg", lo, hi), qd, AF.Sign, bias=FC("mh"))
-                        else:
-                            ts(S("sg", lo, hi), qd, 0.0, 0.5, OP.is_gt, OP.subtract)
+                        ts(S("sg", lo, hi), qd, 0.0, 0.5, OP.is_gt, OP.subtract)
+                        if r != 1:
+                            pu = Wb(c, 448, n)
+                            mm([(pu,) + a for a in ([(MH("I"), S(k, lo, hi)) for k in parts] if r else pick(lo, hi))])
+                            cp(S("old" if r else "xc", lo, hi), pu)
                         stage(6 * r + 2, c)
                     else:
-                        columns(c, lo, hi, bs, bt, [(MH("T"), oc)], [(MH("TL%d" % t), R)], [(MH("I32"), oc), (MH("IL%d" % t), R)], str(t))
+                        columns(c, lo, hi, bs, bt, [(MH("T"), oc)], [(MH("TL%d" % t), R)], [(MH("I32"), oc), (MH("IL%d" % t), R)])
                     if t == 3:
                         tt(S("rt", lo, hi), R, S("tau", lo, hi), OP.mult)
-                    mx, mn = gather_scan(5 * r + 1 + t, lo, hi)
+                    mx, mn = gather_scan(lo, hi)
                     q = Wb(c, 64, n)
-                    ab = str(t) in PAR["ua"]
-                    mm([(q, MH("I"), A("mhalf", 0, n))] + [(q, MB("V+"), S("sg", lo, hi))] * ab, last=False)
+                    mm([(q, MH("I"), A("mhalf", 0, n))], last=False)
                     mm([(q, MB("Q%d+" % r), mx)], first=False, last=False)
                     mm([(q, MB("Q%d-" % r), mn)], first=False)
                     stage(6 * r + 3 + t, c)
                     u, k = S("u", lo, hi), A("kk", 256 * t + o + lo, 256 * t + o + hi)
-                    if ab:
-                        act(S("kd", lo, hi), q, AF.Abs)
-                        ts(k, S("kd", lo, hi), bit("lam", 3 - t), bit("lb", 3 - t), OP.mult, OP.is_gt)
-                    else:
-                        tt(u, q, S("sg", lo, hi), OP.mult)
-                        ts(k, u, bit("lam", 3 - t), 0.0, OP.mult, OP.is_gt)
+                    tt(u, q, S("sg", lo, hi), OP.mult)
+                    ts(k, u, bit("lam", 3 - t), 0.0, OP.mult, OP.is_gt)
                     if t < 3:
                         tt(R, R, k, OP.mult)
                         continue
                     rf = S("rf", lo, hi)
                     tt(rf, S("rt", lo, hi), k, OP.mult)
                     for b in range(2):
-                        pn = X(c, 128 + b * n, n)
-                        mm([(pn, MH("R%d" % b), oc), (pn, MH("R%d" % b), rf)])
-                    lin(PAR["nw"], A("nw", 2 * o + 2 * lo, 2 * o + 2 * hi), X(c, 128, 2 * n), 1.0)
+                        mm([(X(c, 128 + b * n, n), MH("R%d" % b), rf)])
+                    lin(A("nw", 2 * o + 2 * lo, 2 * o + 2 * hi), X(c, 128, 2 * n), 1.0)
             stage(6 * r + 6)
             if r < 2:
                 n = CH[0][1]
@@ -584,78 +486,28 @@ def build(rank, near):
                 terms = [(pa, MH("W%d" % r), A("kk", 256 * t + o + lo, 256 * t + o + hi)) for t in range(4) for lo, hi in CH]
                 mm(terms[:-1], last=False)
                 mm(terms[-1:], first=False)
-                red = A("red", 2 * r + h, 2 * r + h + 1)
-                add("V", lambda g, T, red=red, pa=pa: g.vector.tensor_reduce(ap(T, red), ap(T, pa), AX.X, OP.add), [pa], [red], COST["V"] + n * CY)
-                bs, bt = A("bias", 4 * r + 2 * h, 4 * r + 2 * h + 1), A("bias", 4 * r + 2 * h + 1, 4 * r + 2 * h + 2)
-                ts(bt, red, 786432.0 - 5760 - 2047.5, None, OP.add)
-                ts(bs, red, 786432.0 - 5760, None, OP.add)
+                bs, bt = A("bias", 2 * r + h, 2 * r + h + 1), A("red", 2 * r + h, 2 * r + h + 1)
+                add("V", lambda g, T, bt=bt, pa=pa: g.vector.tensor_reduce(ap(T, bt), ap(T, pa), AX.X, OP.add), [pa], [bt], COST["V"] + n * CY)
+                ts(bs, bt, OFF - SUM0, None, OP.add)
             nw = A("nw", 2 * o, 2 * o + 256)
             for c, (lo, hi) in enumerate(CH):
                 stage(6 * r + 6, c)
-                ni, rc = S("ni", lo, hi), A("rl", r0 + lo // 16, r0 + hi // 16)
-                add("V", lambda g, T, ni=ni, rc=rc, f=2048.0 * (r < 2): g.vector.tensor_scalar(ap(T, ni), ap(T, nw).indirect(ap(T, rc)), f, None, OP.add),
-                    [rc, nw], [ni], 0.05 + (hi - lo) * CY * COST["g"])
-                ts(S("na", lo, hi), ni, 4095, None, OP.bitwise_and)
+                ni, rc, old = S("ni", lo, hi), A("rl", r0 + lo // 16, r0 + hi // 16), S("old", lo, hi)
                 if r < 2:
-                    ts(S("xc", lo, hi), S("na", lo, hi), -2048.0, None, OP.add)
-                elif PAR["apart"] < 2:
-                    cp(S("yo", lo, hi), S("na", lo, hi))
-                else:
-                    for b in range(2):
-                        add("V", lambda g, T, b=b, lo=lo, hi=hi: g.vector.tensor_copy(
-                            T.yo[64 * h:64 * h + 64, 128 * b + lo:128 * b + hi], T.na[64 * b:64 * b + 64, o + lo:o + hi]),
-                            [S("na", lo, hi)], [("YO", h + (2 * c + b) / 4, h + (2 * c + b + 1) / 4)], COST["V"] + 64 * CY)
+                    de = S("de%d" % r, lo, hi)
+                    add("V", lambda g, T, de=de, rc=rc: g.vector.tensor_copy(ap(T, de), ap(T, nw).indirect(ap(T, rc))),
+                        [rc, nw], [de], 0.05 + (hi - lo) * CY * COST["g"])
+                    continue
+                add("V", lambda g, T, ni=ni, rc=rc, old=old: g.vector.tensor_tensor(ap(T, ni), ap(T, nw).indirect(ap(T, rc)), ap(T, old), OP.add),
+                    [rc, nw, old], [ni], 0.05 + (hi - lo) * CY * COST["g"])
+                ts(S("na", lo, hi), ni, 4095, None, OP.bitwise_and)
+                cp(S("yo", lo, hi), S("na", lo, hi))
+        home("y", "yo")
 
-    def home(kind, nm):
-        land, tile = kind + "l", A(nm)
-        i = send(lambda T, j: T[land][rank], lambda T, j: ap(T, tile), [tile], lambda j: "n" + kind)
-        both = (landed(i, peers, [], "n" + kind, 3.5), dma(lambda T: T[land][rank], lambda T: ap(T, tile), [tile], [], "o" + kind, 2.0))
-        k, out = (16, "yu") if kind == "y" else (1, "yq")
-        for h in range(2):
-            for b in range(2):
-                r0 = 64 * b + 16 * rank
-                dma(lambda T, h=h, b=b: T[out][4 * k * h:4 * k * h + 4 * k, 128 * b:128 * b + 128],
-                    lambda T, h=h, r0=r0: T[land][:, r0:r0 + k, 128 * h:128 * h + 128], [], [], "s" + kind, 2.0, dep=both,
-                    eng="S" if b and kind == "y" and PAR["sq"] else "Y")
-
-    def home2(kind, nm):
-        k, out, w = (1, "yu", 64) if kind == "y" else (16, "yq", 4)
-        st, both = [], []
-        for h in range(2):
-            rd = [(nm.upper(), h, h + 1)]
-            st.append(dma(lambda T, h=h: T[kind + "t"][:, 64 * h:64 * h + 64, :], lambda T, h=h: T[nm][64 * h:64 * h + 64:k, :], rd, [], "o%s%d" % (kind, h), 1.8))
-            r0 = 64 * h + 16 * rank
-            both.append(dma(lambda T, h=h: T[kind + "k"][rank, 64 * h:64 * h + 64, :], lambda T, r0=r0: T[nm][r0:r0 + 16:k, :], rd, [], "o" + kind, 1.8,
-                            eng="S" if kind == "y" and PAR["sq"] else "Y"))
-        i = send(lambda T, j: T[kind + "k"][rank], lambda T, j: T[kind + "t"][j], [], lambda j: "n" + kind, dep=st)
-        both.append(landed(i, peers, [], "n" + kind, 2.5))
-        for h in range(2):
-            dma(lambda T, h=h: T[out][64 // k * h:64 // k * (h + 1), :], lambda T, h=h: T[kind + "k"][:, 64 * h:64 * h + 64, :], [], [], "s" + kind, 2.0, dep=both,
-                eng="S" if h and kind == "y" and PAR["sq"] else "Y")
-
-    def home1(kind, nm, h):
-        land, tile, g_ = kind + "m", A(nm, 128 * h, 128 * h + 128), 4 * h + rank
-        i = send(lambda T, j: T[land][g_], lambda T, j: ap(T, tile), [tile], lambda j: "n%s%d" % (kind, h))
-        both = (landed(i, peers, [], "n%s%d" % (kind, h), 3.5), dma(lambda T: T[land][g_], lambda T: ap(T, tile), [tile], [], "o%s%d" % (kind, h), 2.0))
-        k, out = (16, "yu") if kind == "y" else (1, "yq")
-        for b in range(2):
-            r0 = 64 * b + 16 * rank
-            dma(lambda T, b=b: T[out][4 * k * h:4 * k * h + 4 * k, 128 * b:128 * b + 128],
-                lambda T, r0=r0: T[land][4 * h:4 * h + 4, r0:r0 + k, :], [], [], "s" + kind, 2.0, dep=both)
-
-    fill(FC("mh"), -0.5)
     for step in steps:
         start(*step)
     for h in range(2):
         stream(h, False)
-        if PAR["apart"] == 1:
-            home1("y", "yo", h)
-    if PAR["apart"] != 1:
-        (home2 if PAR["apart"] else home)("y", "yo")
-    line.sort()
-    for (a, i), (b, j) in zip(line, line[1:]):
-        if PAR["line"] and i not in ops[j]["d"]:
-            ops[j]["o"].append(i)
     return ops
 
 
@@ -667,7 +519,55 @@ def latency(ops, j, i):
     return COST["self"] if ops[j]["e"] == ops[i]["e"] else COST["lat"]
 
 
-def justify(ops, start, passes):
+def schedule(ops):
+    n = len(ops)
+    succ = [[] for _ in ops]
+    for i, o in enumerate(ops):
+        for j in o["d"] + o["o"]:
+            succ[j].append(i)
+    pr = [0.0] * n
+    sg = [9999 if o["s"] is None else o["s"] for o in ops]
+    for i in range(n - 1, -1, -1):
+        pr[i] = ops[i]["c"] + max([pr[s] + latency(ops, i, s) for s in succ[i]] + [0.0])
+        if ops[i]["s"] is None:
+            sg[i] = min([sg[x] for x in succ[i]] + [9999])
+    cnt = [len(o["d"] + o["o"]) for o in ops]
+    ready, start = [0.0] * n, [0.0] * n
+    free, avail = {}, {}
+    for i in range(n):
+        if cnt[i] == 0:
+            avail.setdefault(ops[i]["e"], []).append(i)
+    for _ in range(n):
+        best = None
+        for e, lst in avail.items():
+            if not lst:
+                continue
+            f = free.get(e, 0.0)
+            s0 = max(f, min(ready[k] for k in lst))
+            if e == "N":
+                i = min(lst, key=lambda k: ready[k])
+                s = ready[i]
+            else:
+                i = min((k for k in lst if ready[k] <= s0 + (AHEAD if e == "S" else WIN)),
+                        key=lambda k: (sg[k] >= 0 and ops[k]["c"] > COST["long"], sg[k], -pr[k]))
+                s = max(f, ready[i])
+            if best is None or s < best[0]:
+                best = (s, i, e)
+        s, i, e = best
+        avail[e].remove(i)
+        start[i] = s
+        end = s + ops[i]["c"]
+        if e != "N":
+            free[e] = end
+        for k in succ[i]:
+            ready[k] = max(ready[k], end + latency(ops, i, k))
+            cnt[k] -= 1
+            if cnt[k] == 0:
+                avail.setdefault(ops[k]["e"], []).append(k)
+    return start
+
+
+def justify(ops, start):
     n = len(ops)
     pre = [[(j, latency(ops, j, i)) for j in o["d"] + o["o"]] for i, o in enumerate(ops)]
     suc = [[] for _ in ops]
@@ -691,68 +591,11 @@ def justify(ops, start, passes):
             at[i] = t
         return at, max(at[i] + ops[i]["c"] for i in range(n))
     best = (max(start[i] + ops[i]["c"] for i in range(n)), start)
-    for _ in range(passes):
+    for _ in range(PASSES):
         back, span = place(lambda i: (-start[i] - ops[i]["c"], -i), suc)
         start, span = place(lambda i: (-back[i] - ops[i]["c"], i), pre)
         best = min(best, (span, start))
-    return best[0], sorted(range(n), key=lambda i: (best[1][i], i))
-
-
-def schedule(ops, ahead):
-    n = len(ops)
-    succ = [[] for _ in ops]
-    for i, o in enumerate(ops):
-        for j in o["d"] + o["o"]:
-            succ[j].append(i)
-
-    def lat(j, i):
-        return latency(ops, j, i)
-    pr = [0.0] * n
-    sg = [9999 if o["s"] is None else o["s"] for o in ops]
-    left, todo = [len(s) for s in succ], [i for i in range(n) if not succ[i]]
-    for i in todo:
-        for j in ops[i]["d"] + ops[i]["o"]:
-            left[j] -= 1
-            if left[j] == 0:
-                todo.append(j)
-    for i in todo:
-        pr[i] = ops[i]["c"] + max([pr[s] + lat(i, s) for s in succ[i]] + [0.0])
-        if ops[i]["s"] is None:
-            sg[i] = min([sg[x] for x in succ[i]] + [9999])
-    cnt = [len(o["d"] + o["o"]) for o in ops]
-    ready, start = [0.0] * n, [0.0] * n
-    free, avail, order = {}, {}, []
-    for i in range(n):
-        if cnt[i] == 0:
-            avail.setdefault(ops[i]["e"], []).append(i)
-    while len(order) < n:
-        best = None
-        for e, lst in avail.items():
-            if not lst:
-                continue
-            f = free.get(e, 0.0)
-            s0 = max(f, min(ready[k] for k in lst))
-            if e == "N":
-                i = min(lst, key=lambda k: ready[k])
-                s = ready[i]
-            else:
-                i = min((k for k in lst if ready[k] <= s0 + (ahead if e == "S" else WIN)), key=lambda k: -pr[k] if PAR["pr"] else (sg[k] >= 0 and ops[k]["c"] > COST["long"], sg[k], -pr[k]))
-                s = max(f, ready[i])
-            if best is None or s < best[0]:
-                best = (s, i, e)
-        s, i, e = best
-        avail[e].remove(i)
-        start[i] = s
-        end = s + ops[i]["c"]
-        if e != "N":
-            free[e] = end
-        order.append(i)
-        for k in succ[i]:
-            ready[k] = max(ready[k], end + lat(i, k))
-            cnt[k] -= 1
-            if cnt[k] == 0:
-                avail.setdefault(ops[k]["e"], []).append(k)
-    return order, start
+    return sorted(range(n), key=lambda i: (best[1][i], i))
 
 
 def share(topo, cores, src, dst):
@@ -771,13 +614,12 @@ def rank_program(g, core, T, topo):
     cores = list(T.cores)
     near = [s for s in range(N) if s != rank and topo.chip(cores[s]) == topo.chip(core)]
     ops = build(rank, near)
-    span, order = min(justify(ops, schedule(ops, ahead)[1], PAR["passes"]) for ahead in PAR["ahead"])
     queue = {"P": g.tensor, "V": g.vector, "S": g.scalar, "G": g, "Y": g.sync}
     own = {"P": "eP", "V": "eV", "S": "eS", "G": "eG"}
     known = {e: {} for e in queue}
     after = {}
     count, sent = {}, 0
-    for i in order:
+    for i in justify(ops, schedule(ops)):
         o = ops[i]
         e = o["e"]
         if e == "N":
@@ -798,12 +640,11 @@ def rank_program(g, core, T, topo):
             dst, src, sem = o["fn"]
             trs = []
             for j in sorted(range(N), key=lambda j: j in near):
-                to = cores[j]
                 if j != rank:
-                    rid, pid, ring = topo.addr(to)
-                    eng = share(topo, cores, core, to)
+                    rid, pid, ring = topo.addr(cores[j])
+                    eng = share(topo, cores, core, cores[j])
                     trs.append(RemoteDMATransfer(dst_ids=[DstId(rid=rid, pnc=pid)], dma_engine_mask=sum(1 << x for x in eng),
-                                                 remote_sem=T.sem[sem(j)], src=src(T, j), dst=dst(T, j)))
+                                                 remote_sem=T.sem[sem], src=src(T, j), dst=dst(T, j)))
                     sent += len(eng)
             g.remote_dma_fused(trs, local_sem=T.sem.lsem)
             after[i] = dict(kn)

from concourse.bass import DstId, RemoteDMATransfer
from concourse.mybir import AluOpType as OP, ActivationFunctionType as AF, AxisListType as AX

N = 4
ROUNDS = (1, 2, 3)
CH = [(0, 64), (64, 128)]
NS = 5
BIG = 2.0 ** 22
OFF = 786432.0
SUM0 = 5760.0
START = (("stage", 0, 2.2), ("own", 0, 3.7), ("own", 1, 5.2), ("stage", 1, 6.2), ("deal", 0, 0), ("first", 0, 3.5), ("first", 1, 3.5),
         ("deal", 1, 0), ("fill", 0, 6.0), ("fill", 1, 6.0))

MH_ = ["T", "I", "tmp", "I32", "R0", "R1"] + [k + str(i) for k in ("TL", "IL") for i in (1, 2, 3)]
MH_ += [k + str(r) for k in ("T1", "S1", "Pm") for r in range(3)] + ["W0", "W1"]
MB_ = ["B", "KLE", "nI", "Ko+", "Ko-", "K0+", "K0-", "K1+", "K1-", "D4", "D5", "V+", "V-", "tmp0", "tmp1", "tmp2", "Ib"]
MB_ += ["Q%d%s" % (r, s) for r in range(3) for s in "+-"]
SCRATCH = {}
for _n, _w, _d in [
        ("w0", 4096, "bfloat16"), ("w1", 4096, "bfloat16"), ("uin", 256, "int32"), ("ul", 4 * 512, "float16"), ("rg", 256, "bfloat16"),
        ("ip", 1, "int32"), ("ii", 8, "int32"), ("fc", 96, "float32"),
        ("iu", 256, "bfloat16"), ("uo", 128, "bfloat16"), ("mg", 128, "bfloat16"), ("ms", 128, "bfloat16"), ("m64", 128, "bfloat16"),
        ("ids", 5 * 128, "bfloat16"), ("jj", 512, "bfloat16"), ("jn", 512, "bfloat16"), ("rm", 64, "bfloat16"), ("dm", 64, "bfloat16"),
        ("mh", len(MH_) * 128, "float16"), ("mb", len(MB_) * 128, "bfloat16"), ("me", 256, "float32"), ("z", 192, "float16"),
        ("ones", 256, "bfloat16"), ("mhalf", 64, "float16"), ("bias", 4, "float32"),
        ("xc", 256, "float16"), ("tb", 256, "bfloat16"), ("sq", 256, "float32"), ("yb", 256, "int32"),
        ("cb", 256, "int32"), ("c16", 256, "uint16"), ("gb", 4096, "bfloat16"), ("mx", 4096, "bfloat16"), ("mn", 4096, "bfloat16"),
        ("old", 256, "float32"), ("t4", 256, "float32"), ("de0", 256, "float16"), ("de1", 256, "float16"),
        ("kc", 256, "float32"), ("vu", 256, "float32"), ("acc", 16, "float32"),
        ("trash", 1024, "bfloat16"), ("cmp", 4096, "bfloat16"), ("cs", 4096, "bfloat16"), ("rl", 48, "uint16"),
        ("vs", 6 * 256, "float32"), ("t8", 256, "bfloat16"), ("oc", 256, "float16"), ("w4", 256, "bfloat16"), ("rr", 256, "float16"),
        ("sg", 256, "bfloat16"), ("tau", 256, "float16"), ("rt", 256, "float16"), ("rf", 256, "float16"), ("u", 256, "float16"),
        ("kk", 4 * 256, "float16"), ("nw", 512, "float32"), ("ni", 256, "int32"), ("na", 256, "int32"), ("red", 4, "float32"),
        ("yo", 256, "float32"), ("qy", 256, "float32")]:
    SCRATCH[_n] = ("sbuf", [128, _w], _d)
for _b in range(8):
    SCRATCH["p%d" % _b] = ("psum", [128, 512], "float32")
SCRATCH["se"] = ("dram", [8, 128, 512], "bfloat16")
SCRATCH["sf"] = ("dram", [8, 128, 512], "bfloat16")
SCRATCH["ym"] = ("dram", [8, 128, 128], "float32")
SCRATCH["qm"] = ("dram", [8, 128, 128], "float32")
SEMAPHORES = ["eP", "eV", "eS", "eG", "ldu", "lsem", "sy", "sq"]
SEMAPHORES += [k + str(h) for k in ("lo", "le", "lw", "nr", "ny", "nq", "oy", "oq") for h in range(2)]
SEMAPHORES += ["nt%d_%d" % (h, s) for h in range(2) for s in range(N)]

CY = 0.00083
COST = {"V": 0.018, "S": 0.065, "P": 0.04, "lat": 0.18, "self": 0.26, "send": 0.8, "g": 1.6, "sc": 3.8, "long": 0.2}
WIN, AHEAD, PASSES = 0.0124, 0.55, 2


def build(rank, near):
    ops, hist, bank, prior, stg = [], {}, {}, {}, [None]
    peers = [s for s in range(N) if s != rank]

    def add(eng, fn, rd, wr, cost, sem=None, amt=1, dep=(), kind="c", lat=None):
        i = len(ops)
        deps = set(dep)
        prev = prior.get(eng) if eng == "Y" else None
        prior[eng] = i
        for acc, w in [(a, False) for a in rd] + [(a, True) for a in wr]:
            nm, lo, hi = acc[0], acc[1], acc[2]
            if nm[0] == "p" and nm[1:].isdigit():
                st = bank.setdefault(nm, [None, [], []])
                if st[0] != eng:
                    st[2] = st[1]
                    st[1] = []
                    st[0] = eng
                deps.update(st[2])
                st[1].append(i)
                if eng == "P":
                    deps.add(prior.get(nm, i))
                    prior[nm] = i
                continue
            keep = []
            for (a, b, j, jw) in hist.setdefault(nm, []):
                over = a < hi and lo < b and j != i
                if over and (w or jw):
                    deps.add(j)
                if not (over and w and lo <= a and b <= hi):
                    keep.append((a, b, j, jw))
            keep.append((lo, hi, i, w))
            hist[nm] = keep
        deps.discard(i)
        ops.append({"e": eng, "fn": fn, "d": sorted(deps), "c": cost, "sem": sem, "amt": amt, "k": kind, "lat": lat, "s": stg[0],
                    "o": [] if prev is None or prev in deps or (stg[0] or 0) >= 0 else [prev]})
        return i

    def A(nm, lo=0, hi=None, st=1):
        return (nm, lo, SCRATCH[nm][1][1] if hi is None else hi, st)

    def ap(T, a):
        return T[a[0]][:, a[1]:a[2]:a[3]] if a[3] != 1 else T[a[0]][:, a[1]:a[2]]

    def size(a):
        return (a[2] - a[1] + a[3] - 1) // a[3]

    def vcost(out, ins, f=1.0):
        two = all(SCRATCH[a[0]][2].endswith("16") for a in [out] + ins)
        return COST["V"] + max(64, size(out) * f * (0.5 if two else 1)) * CY

    def arg(T, s):
        return ap(T, s) if isinstance(s, tuple) else s

    def cols(*xs):
        return [s for s in xs if isinstance(s, tuple)]

    def ts(out, i0, s1, s2, o1, o2=None):
        def fn(g, T):
            if o2 is None:
                return g.vector.tensor_scalar(ap(T, out), ap(T, i0), arg(T, s1), None, o1)
            return g.vector.tensor_scalar(ap(T, out), ap(T, i0), arg(T, s1), arg(T, s2), o1, o2)
        return add("V", fn, [i0] + cols(s1, s2), [out], vcost(out, [i0]))

    def tt(out, i0, i1, op):
        f = 1 if (i0[0][1:].isdigit() or i1[0][1:].isdigit()) else 2
        return add("V", lambda g, T: g.vector.tensor_tensor(ap(T, out), ap(T, i0), ap(T, i1), op), [i0, i1], [out], vcost(out, [i0, i1], f))

    def cp(out, i0):
        return add("V", lambda g, T: g.vector.tensor_copy(ap(T, out), ap(T, i0)), [i0], [out], vcost(out, [i0]))

    def nearest(out, i0, m):
        return ts(out, i0, 1.5 * 2.0 ** 23 * m, 1.5 * 2.0 ** 23 * m, OP.add, OP.subtract)

    def fill(out, v):
        return add("V", lambda g, T: g.vector.memset(ap(T, out), v), [], [out], vcost(out, []))

    def scan(out, d0, d1, o0, o1):
        return add("V", lambda g, T: g.vector.tensor_tensor_scan(ap(T, out), ap(T, d0), ap(T, d1), 0.0, o0, o1), [d0, d1], [out], vcost(out, [d0, d1]))

    def act(out, i0, func, bias=None, scale=None, acc=None):
        def fn(g, T):
            kw = {}
            if bias is not None:
                kw["bias"] = arg(T, bias)
            if scale is not None:
                kw["scale"] = arg(T, scale)
            if acc is not None:
                kw["accum_out"] = ap(T, acc)
            return g.scalar.activation(ap(T, out), ap(T, i0), func, **kw)
        return add("S", fn, [i0] + cols(bias, scale), [out] + ([acc] if acc else []), COST["S"] + size(out) * CY + (0.02 if acc else 0))

    def lin(out, i0, scale, bias=None):
        return act(out, i0, AF.Copy if bias is None else AF.Identity, bias=bias, scale=scale)

    def mm(terms, first=True, last=True):
        def fn(g, T):
            r = None
            for k, (o, l, x) in enumerate(terms):
                r = g.tensor.matmul(ap(T, o), ap(T, l), ap(T, x), first and k == 0, last and k == len(terms) - 1)
            return r
        c = sum(max(64, size(o)) * (4 if l[0] == "me" else 1) for o, l, x in terms) * 0.0007
        return add("P", fn, [x for tm in terms for x in tm[1:]], [terms[0][0]], COST["P"] + c)

    def MH(k):
        i = MH_.index(k)
        return A("mh", 128 * i, 128 * i + 128)

    def MB(k):
        i = MB_.index(k)
        return A("mb", 128 * i, 128 * i + 128)

    fcn = {}

    def FC(k, n=1, at=0, w=1):
        if k not in fcn:
            fcn[k] = sum(v[1] for v in fcn.values()), n
        return A("fc", fcn[k][0] + at, fcn[k][0] + at + w)

    def iota(out, pat, base, cm, dep=()):
        def fn(g, T):
            if SCRATCH[out[0]][2] != "int32":
                return g.iota(ap(T, out), pat, base, cm, allow_small_or_imprecise_dtypes=True)
            return g.iota(ap(T, out), pat, base, cm)
        return add("G", fn, [], [out], 0.13 + 2 * size(out) * CY, dep=dep)

    def dma(dst, src, rd, wr, sem, lat, dep=()):
        return add("Y", lambda g, T: g.sync.dma_start(dst(T), src(T)), rd, wr, 0.1, sem=sem, amt=16, kind="dma", lat=lat, dep=dep)

    def send(dst, src, rd, sem, dep=()):
        return add("G", (dst, src, sem), rd, [], COST["send"], dep=dep, kind="send")

    def landed(i, senders, wr, sem, net):
        return add("N", senders, [], wr, 0.0, sem=sem, dep=(i,), kind="net", lat=net)

    stg[0] = -9
    dma(lambda T: T.uin[:], lambda T: T.units[:], [], [A("uin")], "ldu", 2.0)
    ts(A("ni"), A("uin"), 2048.0, None, OP.add)
    ts(A("na"), A("ni"), 4095, None, OP.bitwise_and)
    for h in range(2):
        for b in range(2):
            a = 512 * rank + 256 * h
            add("V", lambda g, T, h=h, b=b, a=a: g.vector.tensor_scalar(T.ul[64 * b:64 * b + 64, a:a + 128], T.na[64 * h:64 * h + 64, 128 * b:128 * b + 128],
                                                                        -2048.0, None, OP.add),
                [A("na")], [A("ul", a, a + 128)], COST["V"] + 128 * CY)
    got, last = {}, []

    def start(kind, h, lat):
        w, W = "w%d" % h, "W%d" % h
        stg[0] = -9
        if kind == "own":
            for b in range(2):
                dma(lambda T, b=b: T[w][64 * b:64 * b + 64, :], lambda T: T.shelf[64 * h:64 * h + 64, :], [], [(W, 4 * b, 4 * b + 4)], "lo%d" % h, lat + 1.2 * b)
        elif kind == "stage":
            got[h] = [dma(lambda T, a=a, b=b: T.se[4 * h + a:4 * h + b], lambda T, a=a, b=b: T.shelf[64 * h + 16 * a:64 * h + 16 * b, :],
                          [], [], "le%d" % h, lat) for a, b in ((0, rank), (rank + 1, N)) if a < b]
        elif kind == "deal":
            last[:] = [send(lambda T, j: T.sf[4 * h + rank], lambda T, j: T.se[4 * h + j], [], "nt%d_%d" % (h, rank), dep=got[h] + last)]
            got[h] = last[0]
        elif kind == "fill":
            for s in near + [s for s in peers if s not in near]:
                i = landed(got[h], [s], [], "nt%d_%d" % (h, s), lat - 2 * (s in near))
                for o in (s, 4 + s):
                    dma(lambda T, o=o: T[w][16 * o:16 * o + 16, :], lambda T, s=s: T.sf[4 * h + s], [], [(W, o, o + 1)], "lw%d" % h, 2.2, dep=(i,))
        else:
            stream(h, True)
            tile = A("ul", 512 * rank + 256 * h, 512 * rank + 256 * h + 256)
            last[:] = [send(lambda T, j: ap(T, tile), lambda T, j: ap(T, tile), [tile], "nr%d" % h, dep=last)]
            landed(last[0], peers, [A("ul", 512 * s + 256 * h, 512 * s + 256 * h + 256) for s in peers], "nr%d" % h, lat)
    steps = list(START)
    while not last:
        start(*steps.pop(0))
    first_send = last[0]
    stg[0] = None
    iota(A("ip"), [[1, 1]], 0, 1)
    iota(A("iu"), [[1, 256]], 0, 0)
    iota(A("mg"), [[1, 8], [0, 16]], 0, 0)
    iota(A("jj", 0, 128), [[0, 8], [256, 16]], 0, 0)
    iota(A("ms"), [[0, 2], [1, 4], [0, 16]], 0, 0)
    iota(A("m64"), [[0, 2], [1, 64]], 0, 0)
    for n in (128, 256):
        cp(A("jj", n, 2 * n), A("jj", 0, n))
    ts(A("jn"), A("jj"), -1.0, 256.0, OP.mult, OP.add)
    im = A("iu", 0, 128)
    pf, kf, pg = FC("p"), FC("k"), FC("pg")
    cp(pf, A("ip"))
    ts(A("ii", 7, 8), A("ip"), 15, None, OP.bitwise_and)
    cp(kf, A("ii", 7, 8))
    ts(pg, pf, kf, 1.0 / 16, OP.subtract, OP.mult)
    for i in range(7):
        ts(A("ii", i, i + 1), A("ip"), 1 << i, None, OP.bitwise_and)
    bits = FC("bit", 7, 0, 7)
    ts(bits, A("ii", 0, 7), 0, None, OP.is_gt)
    for nm, a, b in (("lam", 2.0, -1.0), ("nl", -2.0, 1.0), ("L", -1.0, 1.0), ("hl", 1.0, -0.5), ("nb", -1.0, None), ("b255", 255.0, None)):
        lin(FC(nm, 7, 0, 7), bits, a, b)

    def bit(nm, i):
        return FC(nm, 7, i)
    lin(FC("k256"), kf, 256.0)
    lin(FC("k16"), kf, 1.0 / 16)
    lin(FC("nk16"), kf, -1.0 / 16)
    lin(FC("s"), bit("bit", 6), -4.0, pg)
    lin(FC("p49"), pf, 1.0, 49.0 - 16 * rank)
    ts(FC("zc"), FC("s"), float(rank), FC("p49"), OP.is_equal, OP.mult)
    ts(A("z"), A("iu", 0, 192), FC("zc"), None, OP.is_equal)
    ts(MB("B"), A("mg"), pg, None, OP.is_equal)
    ts(MB("KLE"), A("jj", 0, 128), FC("k256"), None, OP.is_ge)
    tt(MH("T"), MB("B"), MB("KLE"), OP.mult)

    def diag(out, at, f):
        ts(out, im, at, f, OP.is_equal, OP.mult)
    for out, f in ((MH("I"), 1.0), (MH("I32"), 32.0), (MB("nI"), -1.0), (MB("V+"), 16384.0)):
        diag(out, pf, f)
    lin(MB("V-"), MB("V+"), -1.0)
    for i in (4, 5):
        diag(MB("D%d" % i), pf, bit("lam", i))
    lin(MB("Ko+"), MB("B"), 256.0)
    lin(MB("Ko-"), MB("B"), -256.0)
    lin(FC("p64", 2), bit("bit", 6), -64.0, pf)
    lin(FC("p64", 2, 1), bit("L", 6), 64.0, pf)
    lin(FC("b128"), bit("bit", 6), 128.0)
    lin(A("uo"), im, 1.0, FC("b128"))
    for b, nm in ((0, "L"), (1, "bit")):
        lin(FC("h256", 2, b), bit(nm, 6), 256.0)
        ts(MB("K%d+" % b), A("ms"), FC("s"), FC("h256", 2, b), OP.is_equal, OP.mult)
        lin(MB("K%d-" % b), MB("K%d+" % b), -1.0)
        ts(MH("R%d" % b), A("m64"), FC("p64", 2), bit(nm, 6), OP.is_equal, OP.mult)
        ts(A("me", 128 * b, 128 * b + 128), im, FC("p64", 2, b), None, OP.is_equal)
    for t in (1, 2, 3):
        ts(MH("TL%d" % t), MH("T"), bit("L", 3 - t), None, OP.mult)
        ts(MH("IL%d" % t), MH("I32"), bit("L", 3 - t), None, OP.mult)
    fill(A("ones"), 1.0)
    fill(A("mhalf"), -0.5)
    ts(A("rm"), A("jj", 0, 64), 0.0, -2 * BIG, OP.is_equal, OP.mult)
    ts(A("dm"), A("jj", 0, 64), FC("k256"), -BIG, OP.not_equal, OP.mult)
    diag(MB("Ib"), pf, 1.0)
    lin(FC("d16"), bit("nl", 4), 16.0)
    for r, m in enumerate(ROUNDS):
        pp, dd, hb = FC("pp%d" % r), FC("dd%d" % r), (5 if m & 2 else 4)
        if m & 2:
            lin(dd, bit("nl", 5), 32.0, FC("d16") if m & 1 else None)
        else:
            dd = FC("d16")
        lin(pp, dd, 1.0, pf)
        diag(MH("tmp"), pp, 1.0)
        tt(MH("Pm%d" % r), MH("tmp"), MH("I"), OP.subtract)
        c1, c2, cid, cid4 = (FC("%s%d" % (k, r)) for k in ("c1", "c2", "id", "id4"))
        lin(c1, dd, bit("L", 3), pf)
        diag(MH("S1%d" % r), c1, 32.0)
        lin(c2, c1, 1.0 / 16, FC("nk16"))
        ts(MB("tmp%d" % r), A("mg"), c2, None, OP.is_equal)
        tt(MH("T1%d" % r), MB("tmp%d" % r), MB("KLE"), OP.mult)
        ts(cid, pp, pf, kf, OP.min, OP.subtract)
        for base, wrap in ((128 * r, 7), (384 + 128 * r, 3))[:2 if r < 2 else 1]:
            for k in range(4):
                v = [16 * min(x & wrap, (x ^ m) & wrap) for x in (2 * k, 2 * k + 1)]
                iota(A("ids", base + 32 * k, base + 32 * k + 32), [[v[1] - v[0], 2], [0, 16]], v[0], 0, dep=(first_send,))
        ts(MB("Q%d+" % r), A("ids", 128 * r, 128 * r + 128), cid, bit("nl", hb), OP.is_equal, OP.mult)
        lin(MB("Q%d-" % r), MB("Q%d+" % r), -1.0)
        if r < 2:
            lin(cid4, bit("bit", 6), -64.0, cid)
            ts(MH("W%d" % r), A("ids", 384 + 128 * r, 512 + 128 * r), cid4, FC("k16"), OP.is_equal, OP.mult)
    for k in range(6):
        iota(A("vs", 256 * k, 256 * k + 256), [[0, 256]], 0, 0, dep=(first_send,))

    def stream(h, first):
        o, win = 128 * h, "w%d" % h

        def S(nm, lo=0, hi=128):
            return A(nm, o + lo, o + hi)

        def X(c, lo, n):
            return A("p%d" % (4 * h + 2 * c), lo, lo + n)

        def Wb(c, lo, n):
            return A("p%d" % (4 * h + 2 * c + 1), lo, lo + n)

        def stage(step, c=0):
            stg[0] = step + 0.5 * h + 0.2 * c

        def columns(c, lo, hi, bs, bt, pre, late, xpt):
            n = hi - lo
            x, w, xp = X(c, 0, n), Wb(c, 0, n), X(c, 64, n)
            tb, cb, c16 = S("tb", lo, hi), S("cb", lo, hi), S("c16", lo, hi)
            mm([(x,) + a for a in pre], last=not late)
            if late:
                mm([(x,) + a for a in late], first=False)
            mm([(w,) + a for a in pre + late], last=False)
            ts(tb, x, bt, OFF - SUM0 - 2047.5, OP.add, OP.add)
            mm([(w, MB("nI"), tb)], first=False)
            mm([(xp,) + a for a in xpt])
            act(S("sq", lo, hi), w, AF.Square, bias=bs)
            tt(S("yb", lo, hi), S("sq", lo, hi), xp, OP.add)
            ts(cb, S("yb", lo, hi), 5, 4095, OP.arith_shift_right, OP.bitwise_and)
            add("G", lambda g, T: g.affine_select(ap(T, c16), ap(T, cb), [[0, n]], OP.is_ge, 0.0, 0, 0), [cb], [c16], 0.17 + 2 * n * CY)

        def gather_scan(lo, hi):
            parts = [(o + lo, o + lo + 32), (o + lo + 32, o + hi)]
            for (a, b) in parts:
                out, off = A("gb", 16 * a, 16 * b), A("c16", a, b)
                add("S", lambda g, T, out=out, off=off: g.scalar.activation(ap(T, out), T[win][:, 0:4096].indirect(ap(T, off)), AF.Copy),
                    [(win.upper(), 0, 9999), off], [out], 0.065 + size(out) * CY * COST["g"])
            for (a, b) in parts:
                m = 16 * (b - a)
                scan(A("mx", 16 * a, 16 * b), A("jj", 0, m), A("gb", 16 * a, 16 * b), OP.min, OP.max)
                scan(A("mn", 16 * a, 16 * b), A("jn", 0, m), A("gb", 16 * a, 16 * b), OP.max, OP.min)
            return A("mx", 16 * (o + lo) + 15, 16 * (o + hi), 16), A("mn", 16 * (o + lo) + 15, 16 * (o + hi), 16)

        def home(kind, nm):
            land, tile, g_ = kind + "m", S(nm), 4 * h + rank
            i = send(lambda T, j: T[land][g_], lambda T, j: ap(T, tile), [tile], "n%s%d" % (kind, h))
            both = (landed(i, peers, [], "n%s%d" % (kind, h), 3.5), dma(lambda T: T[land][g_], lambda T: ap(T, tile), [tile], [], "o%s%d" % (kind, h), 2.0))
            k, out = (16, "yu") if kind == "y" else (1, "yq")
            for b in range(2):
                r0 = 64 * b + 16 * rank
                dma(lambda T, b=b: T[out][4 * k * h:4 * k * h + 4 * k, 128 * b:128 * b + 128],
                    lambda T, r0=r0: T[land][4 * h:4 * h + 4, r0:r0 + k, :], [], [], "s" + kind, 2.0, dep=both)

        bs, bt = OFF, SUM0
        if first:
            for c, (lo, hi) in enumerate(CH):
                stg[0] = -3 + h + 0.5 * c
                a = 512 * rank + 2 * o
                xs = A("ul", a + lo, a + hi)
                columns(c, lo, hi, bs, bt, [(MH("T"), xs)], [], [(MH("I32"), xs)])
                mx, mn = gather_scan(lo, hi)
                tt(A("ul", a + 128 + lo, a + 128 + hi), mx, mn, OP.subtract)
            return

        def pick(lo, hi):
            return [(A("z", 49 - 16 * s, 177 - 16 * s), A("ul", 512 * s + 2 * o + lo, 512 * s + 2 * o + hi)) for s in range(N)]
        for c, (lo, hi) in enumerate(CH):
            stage(0, c)
            mm([(X(c, 384, hi - lo),) + a for a in pick(128 + lo, 128 + hi)])
            cp(S("rg", lo, hi), X(c, 384, hi - lo))
        for r, m in enumerate(ROUNDS):
            hb = 5 if m & 2 else 4
            D = MB("D%d" % hb)
            parts = ("xc", "de0", "de1")[:r + 1]
            for c, (lo, hi) in enumerate(CH):
                n = hi - lo
                stage(6 * r, c)
                xs = [S(k, lo, hi) for k in parts]
                if r:
                    columns(c, lo, hi, bs, bt, [(MH("T"), a) for a in xs[:r]], [(MH("T"), xs[r])], [(MH("I32"), a) for a in xs])
                mm([(Wb(c, 128, n), D, A("uo", lo, hi)), (Wb(c, 128, n), MB("Ib"), A("dm", 0, n))], last=False)
            for cc in range(2):
                mm([(X(cc, 128, 256), D, A("iu"))], last=False)
            for c, (lo, hi) in enumerate(CH):
                n = hi - lo
                stage(6 * r, c)
                ends = list(zip("+-", gather_scan(lo, hi))) if r else [("+", S("rg", lo, hi))]
                kp, vp = Wb(c, 128, n), Wb(c, 192, n)
                for sign, e in ends:
                    mm([(kp, MB("Ko" + sign), e)], first=False, last=e == ends[-1][1])
                    for cc in range(2):
                        mm([(X(cc, 128 + 128 * b + lo, n), MB("K%d%s" % (b, sign)), e) for b in range(2)], first=False, last=e == ends[-1][1] and hi == 128)
                scan(S("kc", lo, hi), A("rm", 0, n), kp, OP.add, OP.max)
                xs = [(MH("I"), S(k, lo, hi)) for k in parts] if r else pick(lo, hi)
                mm([(vp,) + a for a in xs + [(MB("V" + sign), e) for sign, e in ends]])
                cp(S("vu", lo, hi), vp)
                if r == 2:
                    stage(6 * r + 1.5, c)
                    qp = Wb(c, 448, n)
                    mm([(qp, MB("Ko" + sign), e) for sign, e in ends])
                    ts(S("qy", lo, hi), qp, 1.0 / 256, None, OP.mult)
            if r == 2:
                home("q", "qy")
            stage(6 * r + 0.6)
            r0 = 16 * r + 8 * h
            for j in range(8):
                kcol = S("kc", 16 * j + 15, 16 * j + 16)
                if j < NS:
                    k = 256 * (2 * h + j % 2)
                    act(A("trash", k, k + 256), X(0, 128, 256), AF.Sign, bias=kcol, scale=-1.0, acc=A("acc", 8 * h + j, 8 * h + j + 1))
                else:
                    k = 256 * (8 * h + j)
                    ts(A("cmp", k, k + 256), X(1, 128, 256), kcol, None, OP.is_gt)
                    scan(A("cs", k, k + 256), A("ones"), A("cmp", k, k + 256), OP.mult, OP.add)
            ts(A("rl", r0 + NS, r0 + 8), A("cs", 256 * (8 * h + NS) + 255, 256 * (8 * h + 8), 256), bit("nl", hb), bit("b255", hb), OP.mult, OP.add)
            ts(A("rl", r0, r0 + NS), A("acc", 8 * h, 8 * h + NS), bit("hl", hb), 127.5, OP.mult, OP.add)
            rl = A("rl", r0, r0 + 8)
            v0 = 256 * (2 * r + h)
            vw = A("vs", v0, v0 + 256)
            add("V", lambda g, T, vw=vw, rl=rl: g.vector.tensor_copy(ap(T, vw).indirect(ap(T, rl)), ap(T, S("vu"))), [rl, S("vu")], [vw], 0.05 + 128 * CY * COST["sc"])
            for t in range(4):
                for c, (lo, hi) in enumerate(CH):
                    n = hi - lo
                    stage(6 * r + 2 + t, c)
                    oc, R = S("oc", lo, hi), S("rr", lo, hi)
                    if t == 0:
                        vm, t8, t4 = Wb(c, 256, n), S("t8", lo, hi), S("t4", lo, hi)
                        mm([(vm, A("me", 128 * b, 128 * b + 128), A("vs", v0 + 2 * lo + b * n, v0 + 2 * lo + b * n + n)) for b in range(2)])
                        if r:
                            nearest(t4, vm, 4096)
                        nearest(t8, vm, 16384)
                        tt(oc, vm, t4 if r else t8, OP.subtract)
                        columns(c, lo, hi, bs, bt, [(MH("T1%d" % r), oc)], [], [(MH("S1%d" % r), oc)])
                        stage(6 * r + 2.9, c)
                        dl, qd, w4 = Wb(c, 320, n), Wb(c, 384, n), S("w4", lo, hi)
                        mm([(dl, MH("Pm%d" % r), oc)])
                        mm([(qd, MB("Q%d+" % r), t8)])
                        nearest(w4, dl, 4096)
                        tt(R, dl, w4, OP.subtract)
                        ts(S("tau", lo, hi), qd, bit("lam", hb), bit("nb", hb), OP.mult, OP.is_gt)
                        ts(S("sg", lo, hi), qd, 0.0, 0.5, OP.is_gt, OP.subtract)
                        if r != 1:
                            pu = Wb(c, 448, n)
                            mm([(pu,) + a for a in ([(MH("I"), S(k, lo, hi)) for k in parts] if r else pick(lo, hi))])
                            cp(S("old" if r else "xc", lo, hi), pu)
                        stage(6 * r + 2, c)
                    else:
                        columns(c, lo, hi, bs, bt, [(MH("T"), oc)], [(MH("TL%d" % t), R)], [(MH("I32"), oc), (MH("IL%d" % t), R)])
                    if t == 3:
                        tt(S("rt", lo, hi), R, S("tau", lo, hi), OP.mult)
                    mx, mn = gather_scan(lo, hi)
                    q = Wb(c, 64, n)
                    mm([(q, MH("I"), A("mhalf", 0, n))], last=False)
                    mm([(q, MB("Q%d+" % r), mx)], first=False, last=False)
                    mm([(q, MB("Q%d-" % r), mn)], first=False)
                    stage(6 * r + 3 + t, c)
                    u, k = S("u", lo, hi), A("kk", 256 * t + o + lo, 256 * t + o + hi)
                    tt(u, q, S("sg", lo, hi), OP.mult)
                    ts(k, u, bit("lam", 3 - t), 0.0, OP.mult, OP.is_gt)
                    if t < 3:
                        tt(R, R, k, OP.mult)
                        continue
                    rf = S("rf", lo, hi)
                    tt(rf, S("rt", lo, hi), k, OP.mult)
                    for b in range(2):
                        mm([(X(c, 128 + b * n, n), MH("R%d" % b), rf)])
                    lin(A("nw", 2 * o + 2 * lo, 2 * o + 2 * hi), X(c, 128, 2 * n), 1.0)
            stage(6 * r + 6)
            if r < 2:
                n = CH[0][1]
                pa = X(0, 384, n)
                terms = [(pa, MH("W%d" % r), A("kk", 256 * t + o + lo, 256 * t + o + hi)) for t in range(4) for lo, hi in CH]
                mm(terms[:-1], last=False)
                mm(terms[-1:], first=False)
                bs, bt = A("bias", 2 * r + h, 2 * r + h + 1), A("red", 2 * r + h, 2 * r + h + 1)
                add("V", lambda g, T, bt=bt, pa=pa: g.vector.tensor_reduce(ap(T, bt), ap(T, pa), AX.X, OP.add), [pa], [bt], COST["V"] + n * CY)
                ts(bs, bt, OFF - SUM0, None, OP.add)
            nw = A("nw", 2 * o, 2 * o + 256)
            for c, (lo, hi) in enumerate(CH):
                stage(6 * r + 6, c)
                ni, rc, old = S("ni", lo, hi), A("rl", r0 + lo // 16, r0 + hi // 16), S("old", lo, hi)
                if r < 2:
                    de = S("de%d" % r, lo, hi)
                    add("V", lambda g, T, de=de, rc=rc: g.vector.tensor_copy(ap(T, de), ap(T, nw).indirect(ap(T, rc))),
                        [rc, nw], [de], 0.05 + (hi - lo) * CY * COST["g"])
                    continue
                add("V", lambda g, T, ni=ni, rc=rc, old=old: g.vector.tensor_tensor(ap(T, ni), ap(T, nw).indirect(ap(T, rc)), ap(T, old), OP.add),
                    [rc, nw, old], [ni], 0.05 + (hi - lo) * CY * COST["g"])
                ts(S("na", lo, hi), ni, 4095, None, OP.bitwise_and)
                cp(S("yo", lo, hi), S("na", lo, hi))
        home("y", "yo")

    for step in steps:
        start(*step)
    for h in range(2):
        stream(h, False)
    return ops


def latency(ops, j, i):
    if j in ops[i]["o"] or ops[j]["e"] == ops[i]["e"] == "P":
        return 0.0
    if ops[j]["lat"] is not None:
        return ops[j]["lat"]
    return COST["self"] if ops[j]["e"] == ops[i]["e"] else COST["lat"]


def schedule(ops):
    n = len(ops)
    succ = [[] for _ in ops]
    for i, o in enumerate(ops):
        for j in o["d"] + o["o"]:
            succ[j].append(i)
    pr = [0.0] * n
    sg = [9999 if o["s"] is None else o["s"] for o in ops]
    for i in range(n - 1, -1, -1):
        pr[i] = ops[i]["c"] + max([pr[s] + latency(ops, i, s) for s in succ[i]] + [0.0])
        if ops[i]["s"] is None:
            sg[i] = min([sg[x] for x in succ[i]] + [9999])
    cnt = [len(o["d"] + o["o"]) for o in ops]
    ready, start = [0.0] * n, [0.0] * n
    free, avail = {}, {}
    for i in range(n):
        if cnt[i] == 0:
            avail.setdefault(ops[i]["e"], []).append(i)
    for _ in range(n):
        best = None
        for e, lst in avail.items():
            if not lst:
                continue
            f = free.get(e, 0.0)
            s0 = max(f, min(ready[k] for k in lst))
            if e == "N":
                i = min(lst, key=lambda k: ready[k])
                s = ready[i]
            else:
                i = min((k for k in lst if ready[k] <= s0 + (AHEAD if e == "S" else WIN)),
                        key=lambda k: (sg[k] >= 0 and ops[k]["c"] > COST["long"], sg[k], -pr[k]))
                s = max(f, ready[i])
            if best is None or s < best[0]:
                best = (s, i, e)
        s, i, e = best
        avail[e].remove(i)
        start[i] = s
        end = s + ops[i]["c"]
        if e != "N":
            free[e] = end
        for k in succ[i]:
            ready[k] = max(ready[k], end + latency(ops, i, k))
            cnt[k] -= 1
            if cnt[k] == 0:
                avail.setdefault(ops[k]["e"], []).append(k)
    return start


def justify(ops, start):
    n = len(ops)
    pre = [[(j, latency(ops, j, i)) for j in o["d"] + o["o"]] for i, o in enumerate(ops)]
    suc = [[] for _ in ops]
    for i in range(n):
        for j, d in pre[i]:
            suc[j].append((i, d))

    def place(key, before):
        at, busy = [0.0] * n, {}
        for i in sorted(range(n), key=key):
            c, t = ops[i]["c"], max([at[j] + ops[j]["c"] + d for j, d in before[i]] + [0.0])
            if ops[i]["e"] != "N":
                lst = busy.setdefault(ops[i]["e"], [])
                k = len(lst)
                while k and lst[k - 1][1] > t:
                    k -= 1
                while k < len(lst) and lst[k][0] < t + c - 1e-9:
                    t = max(t, lst[k][1])
                    k += 1
                lst.insert(k, (t, t + c))
            at[i] = t
        return at, max(at[i] + ops[i]["c"] for i in range(n))
    best = (max(start[i] + ops[i]["c"] for i in range(n)), start)
    for _ in range(PASSES):
        back, span = place(lambda i: (-start[i] - ops[i]["c"], -i), suc)
        start, span = place(lambda i: (-back[i] - ops[i]["c"], i), pre)
        best = min(best, (span, start))
    return sorted(range(n), key=lambda i: (best[1][i], i))


def share(topo, cores, src, dst):
    near = [c for c in cores if c != src and topo.chip(c) == topo.chip(src)]
    far = [c for c in cores if topo.chip(c) != topo.chip(src)]
    taken = topo.engines(src, far[0]) if far else []
    pool, who = (taken, far) if dst in far else ([e for e in topo.engines(src, dst) if e not in taken], near)
    k = len(pool) // len(who)
    return pool[k * who.index(dst):k * who.index(dst) + k]


def rank_program(g, core, T, topo):
    rank = T.rank_of(core)
    if rank is None:
        return
    cores = list(T.cores)
    near = [s for s in range(N) if s != rank and topo.chip(cores[s]) == topo.chip(core)]
    ops = build(rank, near)
    queue = {"P": g.tensor, "V": g.vector, "S": g.scalar, "G": g, "Y": g.sync}
    own = {"P": "eP", "V": "eV", "S": "eS", "G": "eG"}
    known = {e: {} for e in queue}
    after = {}
    count, sent = {}, 0
    for i in justify(ops, schedule(ops)):
        o = ops[i]
        e = o["e"]
        if e == "N":
            amt = sum(len(share(topo, cores, cores[s], core)) for s in o["fn"])
            o["at"] = (o["sem"], amt)
            after[i] = {o["sem"]: amt}
            continue
        kn = known[e]
        need = [ops[j]["at"] + (j,) for j in o["d"]
                if (e, ops[j]["e"]) != ("P", "P") and kn.get(ops[j]["at"][0], 0) < ops[j]["at"][1]]
        for (s, v, j) in need:
            if not any(j2 != j and after[j2].get(s, 0) >= v and (s2 != s or v2 > v or j2 > j) for (s2, v2, j2) in need):
                queue[e].wait_ge(T.sem[s], v)
        for (s, v, j) in need:
            for s2, v2 in after[j].items():
                kn[s2] = max(kn.get(s2, 0), v2)
        if o["k"] == "send":
            dst, src, sem = o["fn"]
            trs = []
            for j in sorted(range(N), key=lambda j: j in near):
                if j != rank:
                    rid, pid, ring = topo.addr(cores[j])
                    eng = share(topo, cores, core, cores[j])
                    trs.append(RemoteDMATransfer(dst_ids=[DstId(rid=rid, pnc=pid)], dma_engine_mask=sum(1 << x for x in eng),
                                                 remote_sem=T.sem[sem], src=src(T, j), dst=dst(T, j)))
                    sent += len(eng)
            g.remote_dma_fused(trs, local_sem=T.sem.lsem)
            after[i] = dict(kn)
            o["at"] = ("lsem", 0)
            continue
        s = o["sem"] or own[e]
        o["fn"](g, T).then_inc(T.sem[s], o["amt"])
        count[s] = count.get(s, 0) + o["amt"]
        o["at"] = (s, count[s])
        after[i] = dict(kn)
        after[i][s] = count[s]
    for s, v in sorted(count.items()):
        if known["G"].get(s, 0) < v:
            g.wait_ge(T.sem[s], v)
    g.wait_ge(T.sem.lsem, sent)
